import numpy as np, ml_dtypes
CORES = [2,6,10,14,18,22,26,30]
N = 8
import mx_ref
BF = ml_dtypes.bfloat16
def gcols(t, e):
    v = np.concatenate([t.reshape(8, 16, -1, 4), np.zeros((8, 16, 1, 4), BF)], axis=2)
    return np.ascontiguousarray(np.stack([v[g][:, e[g]] for g in range(8)])).reshape(128, -1)
def tile(rs):
    return np.stack(rs, axis=2).reshape(128, -1).astype(BF)
def pick(q, e):
    c = np.concatenate([q[0].reshape(128, -1, 4), np.zeros((128, 1, 4), np.uint8)], axis=1); s = np.concatenate([q[1], np.ones((16, 1), np.uint8)], axis=1)
    return (np.ascontiguousarray(c[:, e].reshape(128, -1)), np.ascontiguousarray(s[:, e]))
def join(*qs):
    return (np.concatenate([q[0] for q in qs], axis=1), np.concatenate([q[1] for q in qs], axis=1))
def put(q, e, v):
    c, s = q[0].reshape(128, -1, 4).copy(), q[1].copy(); c[:, e] = v[0].reshape(128, -1, 4); s[:, e] = v[1]
    return (c.reshape(128, -1), s)
def pk(c, s):
    return (np.ascontiguousarray(c), mx_ref.live(s))
def emit(q):
    return q[0], q[1]
def packed(v, rng):
    q = [mx_ref.quantize(np.ascontiguousarray(v[r])) for r in range(N)]
    return np.stack([a for a, b in q]), np.stack([mx_ref.plane(b, rng) for a, b in q])
def values_of_codes():
    e, c = np.zeros((128, 128, 4), np.float32), np.zeros((128, 2, 4), np.uint8)
    e[np.arange(128), np.arange(128), 0] = 1
    c[:127, :, 0] = np.arange(256).reshape(2, 128).T[:127]
    return mx_ref.matmul(mx_ref.quantize(e.reshape(128, 512).astype(BF)), (c.reshape(128, 8), np.full((16, 2), 127, np.uint8))).T.reshape(-1).astype(np.float64)
CODE_VALUE, SCALE_VALUE = values_of_codes(), 2.0 ** (np.arange(256) - 127.0)
def decode(q):
    return (CODE_VALUE[q[0]].reshape(16, 8, -1, 4) * SCALE_VALUE[q[1]][:, None, :, None] + 0.0).reshape(128, -1).astype(np.float32)
def f(rng, *shape):
    return mx_ref.flush((rng.standard_normal(shape, dtype=np.float32) * np.exp2(rng.integers(-2, 3, shape[:-1] + (1,)))).astype(BF))
def wide(rng, *shape, cols=0):
    v = rng.standard_normal(shape, dtype=np.float32) * np.exp2(rng.integers(-12, 13, shape)).astype(np.float32)
    if cols: v *= np.repeat(np.exp2(rng.integers(-cols, cols + 1, shape[:-2] + (1, shape[-1] // 4))) * (rng.random(shape[:-2] + (1, shape[-1] // 4)) > 0.0625), 4, axis=-1).astype(np.float32)
    return mx_ref.flush(v.astype(BF))
C, B, F, K, R = 512, 128, 4, 96, 3
def order(p):
    return np.argsort(-(p[::16] + np.float32(0.0)), axis=1, kind="stable")
def layer(w, q):
    return tile([mx_ref.matmul(pick(w, np.arange(128 * b, 128 * b + 128)), q) * np.float32(0.03125) for b in range(4)])
def numbers_of(rng):
    return {"x": np.array(f(rng, N, 128, 4 * C)), "u": np.array(f(rng, N, 128, 512)), "v": np.array(f(rng, N, 128, 512))}
def weights(rng, w):
    c, p = packed(w, rng)
    return {"wc": c, "ws": p}
def still(rng, q=-1):
    w = np.zeros((N, 128, 4, 128, 4), np.float32)
    i = np.arange(128)
    c = np.where(rng.permutation(N) % 2 == 0, 32.0, -32.0)
    for b in range(4): w[:, i, b, i, b] = c[:, None]
    if q >= 0:
        for b in range(4):
            w[:, 16 * q, b, 16 * q, :] = 0
            w[:, 16 * q, b, 16 * q, (b + 1) % 4] = 32
    return weights(rng, w.reshape(N, 128, 2048).astype(BF))
def signs(rng):
    return np.stack([rng.permutation(8) % 2 * 2.0 - 1.0 for r in range(N)])
def planned(rng, kind):
    b = rng.permutation(F)
    n = np.zeros(F, int)
    if kind == 0: n[:] = B // F
    if kind == 1: n[b[0]] = B
    if kind == 2: n[b[:2]] = B // 2
    if kind == 3:
        n[min(b[:2])] = B // 2 - 1
        n[max(b[:2])] = B // 2
        n[b[2]] = 1
    e = rng.permutation(np.concatenate([B * i + rng.permutation(B)[:n[i]] for i in range(F)]))
    return np.concatenate([e, rng.permutation(np.setdiff1d(np.arange(C), e))])
def level(rng):
    a, n, block, may = np.zeros((C, 4)), np.zeros(C, int), np.arange(C) // B, list(range(F))
    for t in range(R):
        least, more = (C - B) // (F + t), (C - B) % (F + t)
        e = [int(j) for j in rng.permutation(may)]
        w = np.concatenate([rng.permutation(np.flatnonzero(block == e[i]))[least + int(i < more):] for i in range(F + t)])
        a[w, n[w]] = R - t
        n[w] += 1
        block[w] = F + 2 * t
        b = min(e[more:])
        s = np.flatnonzero(block == b)
        n[s] += 1
        block[s] = F + 2 * t + 1
        may = [j for j in may if j != b] + [F + 2 * t, F + 2 * t + 1]
    return a
def setup_inputs(rng):
    return {**numbers_of(rng), **weights(rng, f(rng, N, 128, 2048))}
def setup_inputs_ties(rng):
    d = numbers_of(rng)
    e = rng.permutation(N)
    x = d["x"].reshape(N, 8, 16, C, 4)
    for r in range(N):
        k = np.zeros(C, int) if r == e[0] else rng.permutation(C) % 5 // 2
        a = x[r][:, :8, :3].copy()
        a[:, :, 2] = 0
        x[r][:, :8] = a[:, :, k]
        if r == e[1]: x[r][:, :, k == 2] = 0
    u = d["u"].reshape(N, 8, 16, 128, 4)
    u[:, :, 8:, ::16] = 0
    w = np.array(f(rng, N, 128, 2048)).reshape(N, 8, 16, 4, 8, 16, 4)
    w[:, :, 8:, :, :, :8] = 0
    return {"x": x.reshape(N, 128, 4 * C), "u": u.reshape(N, 128, 512), "v": d["v"], **weights(rng, w.reshape(N, 128, 2048))}
def setup_inputs_blocks(rng):
    d = numbers_of(rng)
    x = d["x"].astype(np.float32).reshape(N, 8, 16, C, 4)
    o = rng.permutation(N)
    s = np.zeros((N, 8, C), int)
    for r in range(N):
        k = rng.permutation(8) % 4 if o[r] > 1 else np.full(8, o[r])
        for g in range(8): s[r, g, planned(rng, k[g])] = (C - 1 - np.arange(C)) // 2
    b = ((s[:, :, :, None] >> np.arange(8)) & 1) * np.exp2(np.arange(8) - 23.0)
    x[:, :, 0] = 0
    x[:, :, 0, :, 0] = signs(rng)[:, :, None]
    x[:, :, 8] = b[:, :, :, :4]
    x[:, :, 9] = b[:, :, :, 4:]
    x[:, :, 10:] = rng.integers(4, 8, (N, 8, 6, C, 4)) * rng.choice([-1.0, 1.0], (N, 8, 6, C, 4)) * 2.0 ** -20
    u = d["u"].reshape(N, 128, 128, 4)
    k = np.where(rng.permutation(N) < N // 2, 2.0 ** -30, 1.0).astype(np.float32).astype(BF)
    u[:, :, ::16] = 0
    for h in range(0, 128, 16):
        u[:, h, h, 0] = k
        u[:, h + 8:h + 10, h] = k[:, None, None]
    return {"x": x.reshape(N, 128, 4 * C).astype(BF), "u": u.reshape(N, 128, 512), "v": d["v"], **still(rng)}
def setup_inputs_sizes(rng):
    d = numbers_of(rng)
    x = d["x"].astype(np.float32).reshape(N, 8, 16, C, 4)
    a = rng.integers(-7, 8, (N, 8, C)) * 2.0 ** -30
    r, g = np.nonzero(signs(rng) > 0)
    a[r, g, rng.integers(0, C, len(r))] = 2.0 ** 30 * rng.choice([-1.0, 1.0], len(r))
    x[:, :, :8] = 0
    x[:, :, 0, :, 0] = a
    q = int(rng.integers(8))
    x[:, q, 0] = level(rng) * 2.0 ** -30
    u = d["u"].reshape(N, 128, 128, 4)
    k = signs(rng) * np.where(rng.permutation(N) < N // 2, 2.0 ** -30, 1.0)[:, None]
    k[:, q] = np.abs(k[:, q])
    u[:, :, ::16] = 0
    for h in range(8): u[:, 16 * h, 16 * h, 0] = k[:, h].astype(np.float32).astype(BF)
    return {"x": x.reshape(N, 128, 4 * C).astype(BF), "u": u.reshape(N, 128, 512), "v": d["v"], **still(rng, q)}
def setup_inputs_huge(rng):
    d = numbers_of(rng)
    x = 2.0 ** 30 * (0.6 + 0.4 * rng.random((N, 128, C, 4)))
    c = np.stack([rng.permutation(C) % 2 * 2.0 - 1.0 for r in range(N)])
    c[rng.permutation(N) < N // 2] = 1
    x *= c[:, None, :, None]
    u = d["u"].reshape(N, 128, 128, 4)
    a = 2.0 ** 30 * (1 - 0.25 * rng.random((N, 128, 8, 4))) * signs(rng)[:, None, :, None]
    u[:, :, ::16] = a.astype(np.float32).astype(BF)
    return {"x": x.astype(np.float32).reshape(N, 128, 4 * C).astype(BF), "u": u.reshape(N, 128, 512), "v": d["v"], **still(rng)}
def setup_inputs_spread(rng):
    d = setup_inputs(rng)
    d["x"] = wide(rng, N, 128, 4 * C, cols=6)
    return d
def check_inputs(d):
    b = []
    for k in ("x", "u", "v"):
        a = np.abs(d[k].astype(np.float32))
        if not (np.isfinite(a).all() and ((a == 0) | (a >= 2.0 ** -30) & (a <= 2.0 ** 30)).all()): b.append("a value of " + k)
    return b
def reference(x, u, v, wc, ws):
    qu = [mx_ref.quantize(u[r]) for r in range(N)]
    lay = [pk(wc[r], ws[r]) for r in range(N)]
    now = [x[r] for r in range(N)]
    block = np.tile(np.arange(C) // B, (N, 8, 1))
    gone = np.zeros((N, 8, F + 2 * R), bool)
    for t in range(R):
        first, made, stay, kept, sent = [], [], [], [], []
        for r in range(N):
            q = mx_ref.quantize(now[r])
            o = order(mx_ref.matmul(qu[r], q))
            first.append(o[:, :B])
            made.append(layer(lay[r], mx_ref.quantize(gcols(now[r], o[:, :B]))))
            np.put_along_axis(block[r], o[:, :B], F + 2 * t, axis=1)
            e = np.full((8, K), -1)
            for g in range(8):
                n = np.bincount(block[r, g], minlength=F + 2 * R)
                n[gone[r, g]] = C + 1
                b = np.argmin(n[:F + 2 * t])
                gone[r, g, b] = True
                s = o[g][block[r, g, o[g]] == b]
                e[g, :len(s)] = s
                block[r, g, s] = F + 2 * t + 1
            stay.append(e)
            kept.append(gcols(decode(q).astype(BF), e))
            sent.append(mx_ref.quantize(kept[r]))
        for r in range(N):
            p = (r - 1) % N
            h = layer(lay[r], sent[p])
            e = np.tile(np.arange(C), (8, 1))
            np.put_along_axis(e, first[r], np.tile(C + np.arange(B), (8, 1)), axis=1)
            for g in range(8):
                k = np.flatnonzero(stay[r][g] >= 0)
                e[g, stay[r][g, k]] = C + B + k + np.where(stay[p][g, k] >= 0, 0, K)
            now[r] = gcols(np.concatenate([now[r], made[r], h, kept[r]], axis=1), e)
    y, ob = np.zeros((N, 128, C), np.float32), np.zeros((N, 8, C), np.float32)
    oc, osc = np.zeros((N, 128, 4 * C), np.uint8), np.zeros((N, 16, C), np.uint8)
    for r in range(N):
        q = mx_ref.quantize(now[r])
        y[r] = mx_ref.matmul(mx_ref.quantize(v[r]), q)
        ob[r] = block[r]
        oc[r], osc[r] = emit(q)
    return {"y": y, "ob": ob, "oc": oc, "osc": osc}

@@ -1,0 +1,495 @@
+from concourse.mybir import dt, AluOpType, AxisListType, ActivationFunctionType
+
+A = AluOpType
+AF = ActivationFunctionType
+R = 3
+NPASS = (6, 5, 4)
+APASS = (3, 2, 2)
+VROWS = (15, 14, 12, 11)
+TILES = ((512, 15, 14), (384, 12, 11), (512, 0, 13), (320, 10, 9), (256, 8, 7), (192, 6, 5), (128, 4, 3), (128, 2, 1))
+VPLAN = ("r15", "r14", "q0", "r12", "q3", "r11", "q1", "d", "q2", "q4", "n1", "q5", "n2", "q6", "q7")
+AORDER = (10, 9, 13, 8, 7, 6, 5, 4, 3, 2, 1)
+TBASE = [sum(w for w, _, _ in TILES[:i]) for i in range(len(TILES))]
+CW = sum(w for w, _, _ in TILES)
+BIG = 65536.0
+ROUND16 = 1.5 * 2.0 ** 27
+LAB = 129.0
+F32, BF, I32, U16, X4, U8 = "float32", "bfloat16", "int32", "uint16", "float8_e4m3fn_x4", "uint8"
+
+SCRATCH = {}
+for _d, _names in (
+        (BF, "ut512 vt512 kt512 et2048 idn128 sg1920 sb8192 ds1024 seg512 zer512 junka1152 junkb1152 junkc576 lb512 eqw128 fl384 kc384 "
+             "db2064 tt512 lbo512"),
+        (X4, "uq128 vq128 upq256 wq512 xq512 kq128 eq512 tq128"),
+        (U8, "us128 vs128 ups256 wsc512 xsc512 ks128 es512 ts128"),
+        (F32, "ta512 tb512 tm512 pm512 mk512 rs32 tr512 rn32 rna32 rnb32 rk32 rkt32 vsrc512 o640 cw64 km32 kmt32 sm16 pa8 pp32 pg128 "
+              "pgt128 sl32 slt32 fr128 frt128 tl32 tlt32 sva96 svb96 nv96 ea512 eat512 el32 elt32 cf288 srcb96 kk96 obs512 ys512"),
+        (U16, "rku32 posu8 posv8 slu32 tlu32 elu128 cu64"),
+        (I32, "ci32")):
+    for _s in _names.split():
+        _n = _s.rstrip("0123456789")
+        SCRATCH[_n] = ("sbuf", [128, int(_s[len(_n):])], _d)
+SCRATCH["ct"] = ("sbuf", [128, 4 * CW], BF)
+SCRATCH["cq"] = ("sbuf", [128, CW], X4)
+SCRATCH["cs"] = ("sbuf", [128, CW], U8)
+SCRATCH["x3"] = ("sbuf", [128, 2048], BF)
+for _t in range(R):
+    for _n, _w, _d in (("x", 3584, BF), ("etab", 640, F32), ("sq", 128, X4), ("ss", 128, U8), ("lq", 128, X4), ("ls", 128, U8),
+                       ("cnt", 8, F32), ("lcnt", 8, F32)):
+        SCRATCH["%s%d" % (_n, _t)] = ("sbuf", [128, _w], _d)
+for _b in range(8):
+    SCRATCH["pb%d" % _b] = ("psum", [128, 512], F32)
+
+SEMAPHORES = (["pe", "dve", "act", "pool", "sent"] + ["d%d" % i for i in range(16)]
+              + ["ac%d" % t for t in range(R)] + ["aq%d" % t for t in range(R)])
+QUEUE_SEM = {"T": "pe", "V": "dve", "S": "act", "G": "pool"}
+
+
+def emit(g, T, ops):
+    queue = {"T": g.tensor, "V": g.vector, "S": g.scalar, "G": g, "Y": g.sync}
+    seen = {q: {} for q in queue}
+    writer, readers, seq, marked, done = {}, {}, {}, {}, {}
+    for o in ops:
+        q = o["q"]
+        if q == "G" and not o["sem"]:
+            o["w"].append("pool")
+        need = []
+        for k in o["r"]:
+            need.append(writer[k])
+        for k in o["w"]:
+            if k in writer:
+                need.append(writer[k])
+            need.extend(readers.get(k, []))
+        if o["chain"]:
+            need = [n for n in need if n[0] != QUEUE_SEM[q]]
+        best = {}
+        for s, n in need:
+            best[s] = max(best.get(s, 0), n)
+        waits = []
+        for s, n in sorted(best.items(), key=lambda e: -done[e][1]):
+            if seen[q].get(s, 0) < n:
+                waits.append((s, n))
+                marked.setdefault(s, set()).add(n)
+                for s2, n2 in done[(s, n)][0].items():
+                    seen[q][s2] = max(seen[q].get(s2, 0), n2)
+        o["waits"] = waits
+        s = o["sem"] if o["sem"] else QUEUE_SEM[q]
+        seq[s] = seq.get(s, 0) + 1
+        o["id"] = (s, seq[s])
+        clock = dict(seen[q]) if o["fn"] else {}
+        clock[s] = seq[s]
+        done[o["id"]] = (clock, len(done))
+        for k in o["w"]:
+            writer[k] = o["id"]
+            readers[k] = []
+        for k in o["r"]:
+            readers.setdefault(k, []).append(o["id"])
+    count = {}
+    for o in ops:
+        if o["sem"]:
+            count[o["id"]] = o["inc"]
+    for s in QUEUE_SEM.values():
+        for i, n in enumerate(sorted(marked.get(s, ()))):
+            count[(s, n)] = i + 1
+    for o in ops:
+        for w in o["waits"]:
+            queue[o["q"]].wait_ge(T.sem[w[0]], count[w])
+        if o["fn"]:
+            ins = o["fn"]()
+            if o["sem"] and o["inc"]:
+                ins.then_inc(T.sem[o["sem"]], o["inc"])
+            elif not o["sem"] and o["id"] in count:
+                ins.then_inc(T.sem[o["id"][0]], 1)
+
+
+def rank_program(g, core, T, topo):
+    rank = T.rank_of(core)
+    if rank is None:
+        return
+    n = len(T.cores)
+    nxt, prv = T.cores[(rank + 1) % n], T.cores[(rank - 1) % n]
+    rid, pid = topo.addr(nxt)[0], topo.addr(nxt)[1]
+    out_mask, out_n, in_n = topo.mask(core, nxt), len(topo.engines(core, nxt)), len(topo.engines(prv, core))
+    V, S, PE = g.vector, g.scalar, g.tensor
+    ops = []
+    ndma = [0]
+
+    def op(q, fn, r, w, sem=None, inc=0, chain=False):
+        ops.append({"q": q, "fn": fn, "r": list(r), "w": list(w), "sem": sem, "inc": inc, "chain": chain})
+
+    def dma(q, out, in_, r, w):
+        e = g.sync if q == "Y" else g.scalar
+        op(q, lambda: e.dma_start(out, in_), r, w, "d%d" % ndma[0], 16)
+        ndma[0] += 1
+
+    def ts(out, in0, s1, s2, o0, o1, r, w):
+        if o1 is None:
+            op("V", lambda: V.tensor_scalar(out, in0, s1, None, o0), r, w)
+        else:
+            op("V", lambda: V.tensor_scalar(out, in0, s1, s2, o0, o1), r, w)
+
+    def tt(out, a, b, o, r, w):
+        op("V", lambda: V.tensor_tensor(out, a, b, o), r, w)
+
+    def cp(out, a, r, w):
+        op("V", lambda: V.tensor_copy(out, a), r, w)
+
+    def ms(ap, c, w, r=()):
+        op("V", lambda: V.memset(ap, c), r, w)
+
+    def tp(out, a, r, w):
+        op("V", lambda: V.transpose(out, a), r, w)
+
+    def scan(out, a, b, o0, o1, r, w):
+        op("V", lambda: V.tensor_tensor_scan(out, a, b, 0.0, o0, o1), r, w)
+
+    def quant(q, s, a, r, w):
+        op("V", lambda: V.quantize_mx(q, s, a), r, w)
+
+    def act(out, a, f, r, w, **kw):
+        op("S", lambda: S.activation(out, a, f, **kw), r, w)
+
+    def mm(bank, width, lq, lsc, rq, rsc, r, start=True, stop=True):
+        op("T", lambda: PE.matmul_mx(T["pb%d" % bank][:, 0:width], lq, lsc, rq, rsc, start, stop), r, ["pb%d" % bank], chain=not start)
+
+    def iota(out, pat, base, cm, w, small=True):
+        if small:
+            op("G", lambda: g.iota(out, pat, base, cm, allow_small_or_imprecise_dtypes=True), [], w)
+        else:
+            op("G", lambda: g.iota(out, pat, base, cm), [], w)
+
+    def send(out, in_, sem, r):
+        op("G", lambda: g.remote_dma(out, in_, T.sem[sem], T.sem.sent, pid, rid, out_mask), r, [], "sent", 0)
+
+    def arrival(sem, k, w):
+        op("G", None, [], w, sem, k * in_n)
+
+    def layer(banks, q, s, r):
+        for b, bank in enumerate(banks):
+            mm(bank, 128, T.wq[:, 128 * b:128 * b + 128], T.wsc[:, 128 * b:128 * b + 128], q, s, ["wq", "wsc"] + r)
+
+    def unpack(b, bank):
+        mm(bank, 512, T.eq[:, 128 * b:128 * b + 128], T.es[:, 128 * b:128 * b + 128], T.xq[:], T.xsc[:], ["eq", "xq"])
+
+    ci, cf, cu, sm, pp = T.ci, T.cf, T.cu, T.sm, T.pp
+    ID = AF.Identity
+    dma("Y", T.ut[:], T.u[:], [], ["ut"])
+    dma("S", T.x0[:, 0:1024], T.x[:, 0:1024], [], ["x0a"])
+    dma("Y", T.x0[:, 1024:2048], T.x[:, 1024:2048], [], ["x0b"])
+    dma("Y", T.wq[:].bitcast(dt.uint8), T.wc[:], [], ["wq"])
+    dma("Y", T.wsc[:], T.ws[:], [], ["wsc"])
+    dma("Y", T.vt[:], T.v[:], [], ["vt"])
+
+    PKU, PK4U, UPU, NATU = cu[:, 0:2], cu[:, 2:4], cu[:, 4:20], cu[:, 20:52]
+    RF, SF, HF, R4, RLAB, KB, PLB, OFF, C8, C9, C10, C11 = (cf[:, i:i + 1] for i in range(12))
+    TC, TCL, PAGEL, MASK, CR, ROW = (cf[:, 32 * i:32 * i + 32] for i in range(1, 7))
+    KCOL, NKCOL, K16C, KP1, NAT = cf[:, 224:230], cf[:, 232:238], cf[:, 240:246], cf[:, 248:254], cf[:, 256:288]
+    off = LAB - 0.5 + 1.0 / 1024
+    iota(ci[:, 16:17], [[0, 1]], 0, 1, ["ci_p"], False)
+    iota(ci[:, 0:16], [[16, 2], [32, 4], [0, 2]], 0, 0, ["ci_u"], False)
+    iota(T.mk[:], [[0, 16], [1, 32]], 0, 0, ["mk0"])
+    ms(T.seg[:], 1.0, ["seg0"])
+    op("G", lambda: g.affine_select(T.idn[:], T.seg[:, 0:128], [[-1, 128]], A.is_equal, 0.0, 0, 1), ["seg0"], ["idn"])
+    iota(T.kk[:], [[16, 96]], 0, 0, ["k16"])
+    iota(ROW, [[0, 2], [1, 16]], 0, 0, ["row"])
+    iota(TC, [[0, 8], [1, 4]], 0, 0, ["tc0"])
+    iota(MASK, [[1, 2], [0, 16]], 0, 0, ["mask0"])
+    iota(CR, [[0, 2], [32, 16]], 16 * len(VROWS), 0, ["cr0"])
+    iota(T.vsrc[:], [[1, 32], [640, 4], [32, 4]], 0, 0, ["vsrc0"])
+    ms(T.zer[:], 0.0, ["zer"])
+    for b in range(4):
+        act(T.et[:, 512 * b:512 * b + 512], T.zer[:], AF.Copy, ["zer"], ["etz%d" % b])
+    for b in range(4):
+        act(T.et[:, 512 * b + b:512 * b + 512:4], T.idn[:], AF.Copy, ["idn", "etz%d" % b], ["et%d" % b])
+    ms(T.kt[:], 0.0, ["kt"])
+    cp(UPU, ci[:, 0:16], ["ci_u"], ["upu"])
+    ts(ci[:, 17:18], ci[:, 16:17], 15, None, A.bitwise_and, None, ["ci_p"], ["ci_r"])
+    ts(ci[:, 18:19], ci[:, 16:17], 31, None, A.bitwise_and, None, ["ci_p"], ["ci_s"])
+    ts(ci[:, 19:20], ci[:, 16:17], 16, 4, A.bitwise_and, A.logical_shift_right, ["ci_p"], ["ci_h"])
+    ts(ci[:, 20:21], ci[:, 16:17], 12, 2, A.bitwise_and, A.logical_shift_right, ["ci_p"], ["ci_4"])
+    for a in range(4):
+        ms(T.kt[32 * a:32 * a + 32, 128 * a:128 * a + 64:2], 1.0, ["kt%d" % a], ["kt"])
+        ms(T.kt[32 * a:32 * a + 32, 128 * a + 65:128 * a + 128:2], 1.0, ["kt%d" % (4 + a)], ["kt"])
+    cp(cf[:, 0:4], ci[:, 17:21], ["ci_r", "ci_s", "ci_h", "ci_4"], ["cols"])
+    for i, (w, ra, rb) in enumerate(TILES):
+        lo = 32 * min(ra if ra else 16, rb)
+        ms(T.ct[:, 4 * (TBASE[i] + lo):4 * (TBASE[i] + w)], 0.0, ["c%d_%d" % (i, t) for t in range(4)])
+    ts(T.mk[:], T.mk[:], SF, 0.5, A.is_ge, A.subtract, ["mk0", "cols"], ["mk1"])
+    quant(T.uq[:], T.us[:], T.ut[:], ["ut"], ["uq"])
+    ms(T.rs[:], 0.0, ["rs%d" % i for i in range(32)])
+    cp(T.upq[:].bitcast(dt.uint32), T.uq[:].bitcast(dt.uint32).indirect(UPU), ["uq", "upu"], ["upq"])
+    act(T.ups[:], T.us[:].indirect(UPU), AF.Copy, ["uq", "upu"], ["ups"])
+    act(T.mk[:], T.mk[:], AF.Copy, ["mk1"], ["mk"], scale=2e29)
+    quant(T.kq[:], T.ks[:], T.kt[:], ["kt%d" % a for a in range(8)], ["kq"])
+    ms(T.sb[:, 255:8192:256], 0.0, ["sb%d" % i for i in range(32)])
+
+    def constants_1():
+        ms(T.seg[:, 0:512:32], 0.0, ["seg", "seg0"])
+        ms(OFF, off, ["off"])
+        ts(C8, RF, 32.0, None, A.mult, None, ["cols"], ["c8"])
+        ts(C9, R4, 32.0, None, A.mult, None, ["cols"], ["c9"])
+        ts(C11, RF, 4.0, BIG - 7.5, A.is_ge, A.mult, ["cols"], ["c11a"])
+        ts(MASK, MASK, HF, 4 * BIG, A.not_equal, A.mult, ["mask0", "cols"], ["mask"])
+        ts(PKU, T.kk[:, 0:2], C8, None, A.add, None, ["k16", "c8"], ["pku"])
+        ts(PK4U, T.kk[:, 0:2], C9, None, A.add, None, ["k16", "c9"], ["pk4u"])
+        act(RLAB, RF, ID, ["cols", "off"], ["rlab0"], bias=OFF)
+        act(KCOL, T.kk[:, 0:6], ID, ["k16", "cols"], ["kcol"], bias=RF)
+        act(PLB, C8, ID, ["cols", "c8"], ["plb"], bias=HF)
+        act(T.vsrc[:], T.vsrc[:], AF.Copy, ["vsrc0"], ["vsrc"], scale=1.0 / 512)
+        act(K16C, KCOL, AF.Copy, ["kcol"], ["k16c"], scale=16.0)
+        act(PAGEL, ROW, ID, ["row", "plb"], ["pagel"], bias=PLB, scale=2.0)
+
+    def constants_2():
+        crk = []
+        for b in range(min(VROWS), 16):
+            c = 32.0 * b + 16.0 * len([k for k in VROWS if k > b]) - (16.0 * b if b in VROWS else 0.0)
+            ms(cf[:, 160 + b:192:16], c, ["cr%d" % b], ["cr0"])
+            crk.append("cr%d" % b)
+        ts(RLAB, RLAB, LAB - off, None, A.add, None, ["rlab0"], ["rlab"])
+        ts(C11, C11, 2048.0 - 7.5, None, A.max, None, ["c11a"], ["c11"])
+        ts(CR, CR, SF, None, A.add, None, crk + ["cols"], ["cr"])
+        ts(TCL, TC, 1.0 / 2048, LAB, A.mult, A.add, ["tc0"], ["tcl"])
+        ts(KB, RF, C11, None, A.add, None, ["cols", "c11"], ["kb"])
+        ts(TC, TC, 1.0 / 2048, None, A.mult, None, ["tc0"], ["tc", "tc0"])
+        ts(NKCOL, KCOL, -1.0, -0.5, A.mult, A.add, ["kcol"], ["nkcol"])
+        ts(KP1, KCOL, 1.0, None, A.add, None, ["kcol"], ["kp1"])
+        ms(T.o[:, 512:640], 64.0, ["o_hi"])
+        ms(T.pg[:, 96:128], 1.0, ["pg_hi"])
+        ms(T.db[:, 2048:2064], 0.0, ["db_z"])
+
+    def constants_3():
+        ts(C10, RF, 16.0, None, A.mult, None, ["cols"], ["c10"])
+        for t in range(R - 1):
+            ts(cf[:, 12 + 4 * t:13 + 4 * t], RF, 5.0 + 2 * t, None, A.is_equal, None, ["cols"], ["i5%d" % t])
+            ts(cf[:, 13 + 4 * t:14 + 4 * t], RF, 4.0 + 2 * t, 2048.0, A.is_equal, A.mult, ["cols"], ["i4%d" % t])
+        for i, c in enumerate((4.5, 6.5, BIG, 2 * BIG)):
+            ms(cf[:, 20 + i:21 + i], c, ["half%d" % i])
+
+    where = {}
+    for i, (w, ra, rb) in enumerate(TILES):
+        for h in range(2):
+            where[(h, ra)] = (i, h)
+            where[(h, rb)] = (i, 2 + h)
+
+    def lane(h, b, lo, hi):
+        i, t = where[(h, b)]
+        return T.ct[:, 4 * (TBASE[i] + lo) + t:4 * (TBASE[i] + hi):4]
+
+    def lkey(h, b):
+        return "c%d_%d" % where[(h, b)]
+
+    def labels():
+        cp(T.o[:].indirect(T.posv[:, 0:6]), T.nv[:], ["pos2", "nv"], ["o_w", "o_r", "o_hi"])
+        act(T.vsrc[:], T.o[:].indirect(T.rku[:]), AF.Copy, ["o_w", "o_r", "o_hi", "rku"], ["vsrc"])
+
+    def keys(t, cnt):
+        i5, i4 = cf[:, 12 + 4 * t:13 + 4 * t], cf[:, 13 + 4 * t:14 + 4 * t]
+        act(sm[:, 3:4], i5, ID, ["i5%d" % t, "i4%d" % t, "cnt%d" % t], ["ka"], scale=cnt, bias=i4)
+        act(sm[:, 4:5], T.cw[:, 63:64], ID, ["kb", "cw"], ["kb1"], scale=-1.0, bias=KB)
+        act(sm[:, 5:6], RLAB, AF.Abs, ["rlab", "vlab"], ["kd"], scale=-1.0, bias=sm[:, 1:2])
+        act(sm[:, 6:7], RF, AF.Abs, ["cols", "half%d" % t], ["ke"], scale=-1.0, bias=cf[:, 20 + t:21 + t])
+        act(sm[:, 7:8], sm[:, 3:4], ID, ["ka", "kb1"], ["kf"], bias=sm[:, 4:5])
+        act(sm[:, 8:9], sm[:, 5:6], AF.Relu, ["kd", "half2"], ["kg"], scale=-BIG, bias=cf[:, 22:23])
+        act(sm[:, 9:10], sm[:, 6:7], AF.Relu, ["ke", "half3"], ["kh"], scale=-2 * BIG, bias=cf[:, 23:24])
+        act(sm[:, 10:11], sm[:, 8:9], ID, ["kg", "kf"], ["ki"], bias=sm[:, 7:8])
+        act(KB, sm[:, 9:10], ID, ["kh", "ki"], ["kb"], scale=-1.0, bias=sm[:, 10:11])
+
+    th, tmh = (T.ta, T.tb), (T.tm, T.tb)
+
+    def compare(h, b):
+        ts(lane(h, b, 0, 32 * b), T["pb%d" % h][:, 0:32 * b], th[h][:, 32 * b:32 * b + 1], 0.5, A.is_lt, A.subtract,
+           ["t%d" % h], [lkey(h, b), "pb%d" % h])
+
+    xkeys = ["x0a", "x0b"]
+    for t in range(R):
+        X, XN = T["x%d" % t], T["x%d" % (t + 1)]
+        xk = "x%d" % t
+        et = T["etab%d" % t]
+        quant(T.xq[:], T.xsc[:], X[:, 0:2048], xkeys, ["xq"])
+        for bank, h in ((0, 0), (2, 0), (1, 1), (3, 1)):
+            mm(bank, 512, T.upq[:, 128 * h:128 * h + 128], T.ups[:, 128 * h:128 * h + 128], T.xq[:], T.xsc[:], ["upq", "ups", "xq"])
+        if t:
+            labels()
+        else:
+            constants_1()
+        tp(T.ta[:], T.pb0[:], [], ["t0", "pb0"])
+        for a in range(4):
+            op("G", lambda a=a: g.affine_select(T.tm[32 * a:32 * a + 32, :], T.ta[32 * a:32 * a + 32, :], [[0, 16], [-1, 32]],
+                                                A.is_ge, -1e29, 0, 1), ["t0"], ["tm0_%d" % a])
+        iota(et[:, 0:128], [[1, 4], [4, 32]], 512, 0, ["etab%da" % t])
+        iota(et[:, 128:640], [[0, 512]], 0, 0, ["etab%db" % t])
+        if t == 0:
+            iota(T.srcb[:], [[1, 3], [4, 32]], 640, 0, ["srcb"])
+            iota(NAT, [[1, 16], [256, 2]], 0, 0, ["nat"])
+        compare(0, VROWS[0])
+        tt(T.pm[:], T.pb1[:], T.mk[:], A.min, ["mk"], ["pm", "pb1"])
+        tp(T.tb[:], T.pm[:], ["pm"], ["t1"])
+        if t:
+            for b in range(3):
+                unpack(b, 5 + b)
+
+        arows = [(h, b) for h in range(2) for b in AORDER[:3]] + [(h, b) for b in AORDER[3:] for h in range(2)]
+        for k in range(len(arows) + 1):
+            if k < len(arows):
+                h, b = arows[k]
+                act(T.sg[:, 480 * (k % 4):480 * (k % 4) + 32 * b], T["pb%d" % (2 + h)][:, 0:32 * b], AF.Sign, ["t%d" % h],
+                    ["sg%d" % (k % 4), "pb%d" % (2 + h)], bias=th[h][:, 32 * b:32 * b + 1], scale=-1.0)
+            if k:
+                h, b = arows[k - 1]
+                act(lane(h, b, 0, 32 * b), T.sg[:, 480 * ((k - 1) % 4):480 * ((k - 1) % 4) + 32 * b], AF.Relu, ["sg%d" % ((k - 1) % 4)],
+                    [lkey(h, b), "rs%d" % (16 * h + b)], accum_out=T.rs[:, 16 * h + b:16 * h + b + 1])
+
+        nq = 0
+        for step in VPLAN:
+            if step[0] == "r":
+                b = int(step[1:])
+                for h in range(1 if b == VROWS[0] else 0, 2):
+                    compare(h, b)
+                for h in range(2):
+                    e = 256 * (16 * h + b + 1)
+                    scan(T.sb[:, e - 16 * b:e], lane(h, b, 0, 16 * b), lane(h, b, 16 * b, 32 * b), A.add, A.add, [lkey(h, b)],
+                         ["sb%d" % (16 * h + b)])
+            elif step[0] == "q":
+                i = int(step[1:])
+                lo, hi = TBASE[i], TBASE[i] + TILES[i][0]
+                quant(T.cq[:, lo:hi], T.cs[:, lo:hi], T.ct[:, 4 * lo:4 * hi], ["c%d_%d" % (i, k) for k in range(4)], ["cq%d" % i])
+                mm(4, hi - lo, T.kq[:], T.ks[:], T.cq[:, lo:hi], T.cs[:, lo:hi], ["kq", "cq%d" % i], nq == 0, nq == len(TILES) - 1)
+                nq += 1
+            elif step == "d":
+                for h in (1, 0):
+                    tt(lane(h, 0, 0, 512), T["pb%d" % h][:], tmh[h][:], A.is_lt, ["t1"] if h else ["tm0_%d" % a for a in range(4)],
+                       [lkey(h, 0), "pb%d" % h])
+                for h in (1, 0):
+                    scan(T.ds[:, 512 * h:512 * h + 512], T.seg[:], lane(h, 0, 0, 512), A.mult, A.add, ["seg", lkey(h, 0)], ["ds%d" % h])
+            elif step == "n1":
+                if t == 0:
+                    quant(T.eq[:], T.es[:], T.et[:], ["et%d" % b for b in range(4)], ["eq"])
+                    for b in range(3):
+                        unpack(b, 5 + b)
+                    constants_2()
+                tt(T.rn[:], T.sb[:, 255:8192:256], T.ds[:, 31:1024:32], A.add, ["sb%d" % i for i in range(32)] + ["ds0", "ds1"], ["rn"])
+            elif step == "n2":
+                tt(T.rna[:], CR, T.rn[:], A.subtract, ["cr", "rn"], ["rn2"])
+        tt(T.rnb[:], T.rna[:], T.rs[:], A.subtract, ["rn2"] + ["rs%d" % i for i in range(32)], ["rn3"])
+        unpack(3, 2)
+        for b, bank in enumerate((5, 6, 7, 2)):
+            act(T.db[:, b:2048:4], T["pb%d" % bank][:], AF.Copy, [], ["db%d" % b, "pb%d" % bank])
+        tp(T.tr[:], T.pb4[:], [], ["tr", "pb4"])
+        tt(T.rk[:], T.tr[:].indirect(PKU), T.rnb[:], A.add, ["tr", "pku", "rn3"], ["rk"])
+        tp(T.rkt[:], T.rk[:], ["rk"], ["rkt"])
+        cp(T.rku[:], T.rkt[:], ["rkt"], ["rku"])
+        cp(T.o[:, 0:512].indirect(T.rku[:]), T.vsrc[:], ["rku", "vsrc"], ["o_w", "o_r"])
+        act(T.lb[:, 128:512], T.o[:, 128:512], ID, ["o_r", "off"], ["lb_r"], bias=OFF)
+        ts(T.lb[:, 0:128], T.o[:, 0:128], off, None, A.add, None, ["o_w"], ["lb_w"])
+        ts(T.eqw[:], T.lb[:, 0:128], RLAB, 16.0, A.is_equal, A.mult, ["lb_w", "rlab"], ["eqw"])
+        tt(T.fr[:], T.o[:, 0:128], T.lb[:, 0:128], A.subtract, ["o_w", "lb_w"], ["fr"])
+        scan(T.cw[:], T.eqw[:, 0:64], T.eqw[:, 64:128], A.add, A.add, ["eqw"], ["cw"])
+        tp(T.frt[:], T.fr[:], ["fr"], ["frt"])
+        ts(T.km[:], MASK, KB, T.cw[:, 63:64], A.add, A.subtract, ["mask", "kb", "cw"], ["km"])
+        tt(T.tl[:], T.frt[:].indirect(PK4U), TCL, A.add, ["frt", "pk4u", "tcl"], ["tl"])
+        tp(T.kmt[:], T.km[:], ["km"], ["kmt"])
+        tp(T.tlt[:], T.tl[:], ["tl"], ["tlt"])
+        op("V", lambda: V.tensor_reduce(sm[:, 0:1], T.kmt[:], AxisListType.X, A.min), ["kmt"], ["key"])
+        ts(T.tlu[:], T.tlt[:], 2048.0, None, A.mult, None, ["tlt"], ["tlu"])
+        act(T.tt[:], X[:, 0:2048].indirect(T.tlu[:]), AF.Copy, xkeys + ["tlu"], ["tt"])
+        cnt, lcnt = T["cnt%d" % t][:, 0:1], T["lcnt%d" % t][:, 0:1]
+        ts(cnt, sm[:, 0:1], ROUND16, ROUND16, A.add, A.subtract, ["key"], ["cnt%d" % t])
+        np_, na = NPASS[t], APASS[t]
+        nv = np_ - na
+        if np_ < 6:
+            ms(T.posu[:, np_:6], 512, ["posu_c"])
+        ts(sm[:, 1:2], sm[:, 0:1], cnt, LAB + 7.5, A.subtract, A.add, ["key", "cnt%d" % t], ["vlab"])
+        ts(pp[:, 0:6], K16C, cnt, None, A.is_ge, None, ["k16c", "cnt%d" % t], ["p1"])
+        send(lcnt, cnt, "ac%d" % t, ["cnt%d" % t])
+        arrival("ac%d" % t, 1, ["lcnt%d" % t])
+        ts(T.fl[:], T.lb[:, 128:512], sm[:, 1:2], None, A.is_equal, None, ["lb_r", "vlab"], ["fl"])
+        ts(sm[:, 2:3], sm[:, 1:2], -LAB, None, A.add, None, ["vlab"], ["v"])
+        scan(T.kc[:], T.fl[:], T.zer[:, 0:384], A.add, A.add, ["fl", "zer"], ["kc"])
+        tt(pp[:, 16:22], pp[:, 0:6], KP1, A.mult, ["p1", "kp1"], ["p3"])
+        for m in range(nv, np_):
+            act(T.junka[:, 384 * (m - nv):384 * (m - nv + 1)], T.kc[:], AF.Sign, ["kc", "nkcol"], ["junk%d" % (m - nv), "pa%d" % m],
+                bias=cf[:, 232 + m:233 + m], accum_out=T.pa[:, m:m + 1])
+        for m in range(nv):
+            ts(T.junkb[:, 384 * m:384 * m + 384], T.kc[:], cf[:, 224 + m:225 + m], 0.5, A.is_gt, A.subtract, ["kc", "kcol"], ["j2%d" % m])
+        for m in range(nv):
+            scan(T.junkc[:, 192 * m:192 * m + 192], T.junkb[:, 384 * m:384 * m + 192], T.junkb[:, 384 * m + 192:384 * m + 384], A.add, A.add,
+                 ["j2%d" % m], ["j3%d" % m])
+        quant(T.tq[:], T.ts[:], T.tt[:], ["tt"], ["tq"])
+        layer((0, 1, 3, 4), T.tq[:], T.ts[:], ["tq"])
+        ts(T.posu[:, 0:nv], T.junkc[:, 191:192 * nv:192], -1.0, 320.0, A.mult, A.add, ["j3%d" % m for m in range(nv)], ["posu_a"])
+        ts(T.posu[:, nv:np_], T.pa[:, nv:np_], -0.5, 320.0, A.mult, A.add, ["pa%d" % m for m in range(nv, np_)], ["posu_b"])
+        for b, bank in enumerate((0, 1, 3, 4)):
+            act(X[:, 2048 + b:2560:4], T["pb%d" % bank][:, 0:128], AF.Copy, [], [xk + "y%d" % b, "pb%d" % bank], scale=0.03125)
+        posk = ["posu_a", "posu_b"] + (["posu_c"] if np_ < 6 else [])
+        ts(T.pg[:, 0:96], T.o[:].indirect(T.posu[:, 0:6]), sm[:, 2:3], 1.0, A.subtract, A.min, posk + ["o_w", "o_r", "o_hi", "v"], ["pg"])
+        cp(pp[:, 8:14], T.posu[:, 0:6], posk, ["p2"])
+        tp(T.pgt[:], T.pg[:], ["pg", "pg_hi"], ["pgt"])
+        tt(pp[:, 24:30], pp[:, 16:22], pp[:, 8:14], A.add, ["p3", "p2"], ["p4"])
+        tt(T.sl[:], T.pgt[:].indirect(PK4U), TC, A.add, ["pgt", "pk4u", "tc"], ["sl"])
+        cp(T.posv[:, 0:6], pp[:, 24:30], ["p4"], ["pos2"])
+        tp(T.slt[:], T.sl[:], ["sl"], ["slt"])
+        ts(T.slu[:], T.slt[:], 2048.0, None, A.mult, None, ["slt"], ["slu"])
+        dbk = ["db%d" % b for b in range(4)] + ["db_z", "slu"]
+        act(X[:, 3328:3584], T.db[:].indirect(T.slu[:, 16:32]), AF.Copy, dbk, [xk + "s1"])
+        cp(X[:, 3072:3328], T.db[:].indirect(T.slu[:, 0:16]), dbk, [xk + "s0"])
+        sq, ss, lq, ls = T["sq%d" % t], T["ss%d" % t], T["lq%d" % t], T["ls%d" % t]
+        quant(sq[:], ss[:], X[:, 3072:3584], [xk + "s0", xk + "s1"], ["sq%d" % t])
+        send(lq[:].bitcast(dt.uint8), sq[:].bitcast(dt.uint8), "aq%d" % t, ["sq%d" % t])
+        send(ls[:], ss[:], "aq%d" % t, ["sq%d" % t])
+        arrival("aq%d" % t, 2, ["lq%d" % t])
+        ts(T.sva[:], T.kk[:], lcnt, 128.0, A.is_ge, A.mult, ["k16", "lcnt%d" % t], ["sv1"])
+        ts(T.nv[:], T.pg[:, 0:96], 5.0 + 2 * t, None, A.add, None, ["pg"], ["nv"])
+        tt(T.svb[:], T.sva[:], T.srcb[:], A.add, ["sv1", "srcb"], ["sv2"])
+        ts(T.o[:, 0:128], T.fr[:], LAB + 4.0 + 2 * t, None, A.add, None, ["fr"], ["o_w"])
+        cp(et[:].indirect(T.posv[:, 0:6]), T.svb[:], ["pos2", "sv2"], ["etab%da" % t, "etab%db" % t])
+        etk = ["etab%da" % t, "etab%db" % t, "rku"]
+        act(T.ea[:, 256:512], et[:].indirect(T.rku[:, 16:32]), AF.Copy, etk, ["e1b"])
+        cp(T.ea[:, 0:256], et[:].indirect(T.rku[:, 0:16]), etk, ["e1a"])
+        if t == R - 1:
+            labels()
+            act(T.lbo[:], T.vsrc[:].indirect(NATU), ID, ["vsrc", "natu", "off"], ["lbo"], bias=OFF)
+        tp(T.eat[:], T.ea[:], ["e1a", "e1b"], ["e1t"])
+        tt(T.el[:], T.eat[:].indirect(PKU), PAGEL, A.max, ["e1t", "pku", "pagel"], ["el"])
+        if t == 0:
+            constants_3()
+        if t == 1:
+            ts(NATU, NAT, C10, None, A.add, None, ["nat", "c10"], ["natu"])
+            quant(T.vq[:], T.vs[:], T.vt[:], ["vt"], ["vq"])
+        if t < R - 1:
+            keys(t, cnt)
+        tp(T.elt[:], T.el[:], ["el"], ["elt"])
+        for k in range(4):
+            ts(T.elu[:, 32 * k:32 * k + 32], T.elt[:], 4.0, float(k), A.mult, A.add, ["elt"], ["elu%d" % k])
+        layer((5, 6, 7, 2), lq[:], ls[:], ["lq%d" % t])
+        for b, bank in enumerate((5, 6, 7, 2)):
+            if b % 2:
+                act(X[:, 2560 + b:3072:4], T["pb%d" % bank][:, 0:128], AF.Copy, [], [xk + "h%d" % b, "pb%d" % bank], scale=0.03125)
+            else:
+                ts(X[:, 2560 + b:3072:4], T["pb%d" % bank][:, 0:128], 0.03125, None, A.mult, None, [], [xk + "h%d" % b, "pb%d" % bank])
+        src = xkeys + [xk + "s0", xk + "s1"] + [xk + c + str(b) for c in "yh" for b in range(4)]
+        xkeys = []
+        for k in range(4):
+            for e in range(2):
+                key = "x%d_%d%d" % (t + 1, k, e)
+                xkeys.append(key)
+                win = X[:].indirect(T.elu[:, 32 * k + 16 * e:32 * k + 16 * e + 16])
+                if e:
+                    act(XN[:, 4 * e + k:2048:8], win, AF.Copy, src + ["elu%d" % k], [key])
+                else:
+                    cp(XN[:, 4 * e + k:2048:8], win, src + ["elu%d" % k], [key])
+
+    quant(T.xq[:], T.xsc[:], T.x3[:], xkeys, ["xq"])
+    for k in range(2):
+        mm(k, 256, T.vq[:], T.vs[:], T.xq[:, 256 * k:256 * k + 256], T.xsc[:, 256 * k:256 * k + 256], ["vq", "xq"])
+    dma("Y", T.oc[:], T.xq[:].bitcast(dt.uint8), ["xq"], ["out0"])
+    ms(sm[:, 11:12], -LAB, ["nlab"])
+    act(T.obs[:], T.lbo[:], ID, ["lbo", "nlab"], ["obs"], bias=sm[:, 11:12])
+    cp(T.ys[:, 0:256], T.pb0[:, 0:256], [], ["ys0", "pb0"])
+    act(T.ys[:, 256:512], T.pb1[:, 0:256], AF.Copy, [], ["ys1", "pb1"])
+    dma("S", T.y[:], T.ys[:], ["ys0", "ys1"], ["out1"])
+    for k in range(4):
+        dma("Y", T.osc[4 * k:4 * k + 4, :], T.xsc[32 * k:32 * k + 4, :], ["xq"], ["out%d" % (2 + k)])
+    dma("Y", T.ob[:], T.obs[0:128:16, :], ["obs"], ["out6"])
+    op("G", None, ["out%d" % k for k in range(7)], [], "sent", 0)
+    emit(g, T, ops)
+    g.wait_ge(T.sem.sent, 3 * R * out_n)

@@ -5,37 +5,45 @@ AF = ActivationFunctionType
 R = 3
 NPASS = (6, 5, 4)
 APASS = (3, 2, 2)
-VROWS = (15, 14, 12, 11)
-TILES = ((512, 15, 14), (384, 12, 11), (512, 0, 13), (320, 10, 9), (256, 8, 7), (192, 6, 5), (128, 4, 3), (128, 2, 1))
-VPLAN = ("r15", "r14", "q0", "r12", "q3", "r11", "q1", "d", "q2", "q4", "n1", "q5", "n2", "q6", "q7")
-AORDER = (10, 9, 13, 8, 7, 6, 5, 4, 3, 2, 1)
-TBASE = [sum(w for w, _, _ in TILES[:i]) for i in range(len(TILES))]
-CW = sum(w for w, _, _ in TILES)
-BIG = 65536.0
-ROUND16 = 1.5 * 2.0 ** 27
-LAB = 129.0
+M0 = 22
+MERGE = "SSVS"
+TW = (512, 448, 384, 384, 256, 192, 128, 128)
+TBASE = [sum(TW[:i]) for i in range(8)]
+CW = sum(TW)
+BIG = 1024.0
+HOLD, BP = 2048.0, 624.0
+B4 = 131072.0
+LAB = 138
 F32, BF, I32, U16, X4, U8 = "float32", "bfloat16", "int32", "uint16", "float8_e4m3fn_x4", "uint8"
+
+
+def yoff(t):
+    return 8 * (LAB + 4 + 2 * t) - int(BP)
+
+
+def doff(t):
+    return 8 * (LAB + 5 + 2 * t)
+
 
 SCRATCH = {}
 for _d, _names in (
-        (BF, "ut512 vt512 kt512 et2048 idn128 sg1920 sb8192 ds1024 seg512 zer512 junka1152 junkb1152 junkc576 lb512 eqw128 fl384 kc384 "
-             "db2064 tt512 lbo512"),
-        (X4, "uq128 vq128 upq256 wq512 xq512 kq128 eq512 tq128"),
-        (U8, "us128 vs128 ups256 wsc512 xsc512 ks128 es512 ts128"),
-        (F32, "ta512 tb512 tm512 pm512 mk512 rs32 tr512 rn32 rna32 rnb32 rk32 rkt32 vsrc512 o640 cw64 km32 kmt32 sm16 pa8 pp32 pg128 "
-              "pgt128 sl32 slt32 fr128 frt128 tl32 tlt32 sva96 svb96 nv96 ea512 eat512 el32 elt32 cf288 srcb96 kk96 obs512 ys512"),
-        (U16, "rku32 posu8 posv8 slu32 tlu32 elu128 cu64"),
-        (I32, "ci32")):
+        (BF, "ut512 vt512 kt512 gq512 qs512 one512 et2048 sg2048 sb8192 ds512 zer512 mk512 rst512 junka1536 junkb1536 junkc768 junkd256 "
+             "lb384 fl384 kc384 tt512 st512 hs384"),
+        (X4, "uq128 vq128 upq128 wq512 xq512 kq128 eq512 tq128 sq384"),
+        (U8, "us128 vs128 ups128 wsc512 xsc512 ks128 es512 ts128 ss384"),
+        (F32, "pm512 sc512 cx512 rk512 rs32 rna32 vsrc512 o528 cq128 tsc128 ssc96 pg96 km64 kmt64 mkb64 sm16 pa8 tab4096 cf64 "
+              "qq32 ea32 eb32 ca16 cb8 cr32 jj32 js32 kk24 dump24 kcol16 wa32 wb32 wf32 we32 el32 lab32 lac32 lj32 ha24 hb24 hc24 obs512 ys512"),
+        (U16, "rku32 posu8 tlu32 slu24 hlu24 elu128 vlu32 olu32 upu8 rfu32 tfu8"),
+        (I32, "ci16 ti32 tj32")):
     for _s in _names.split():
         _n = _s.rstrip("0123456789")
         SCRATCH[_n] = ("sbuf", [128, int(_s[len(_n):])], _d)
 SCRATCH["ct"] = ("sbuf", [128, 4 * CW], BF)
-SCRATCH["cq"] = ("sbuf", [128, CW], X4)
+SCRATCH["cc"] = ("sbuf", [128, CW], X4)
 SCRATCH["cs"] = ("sbuf", [128, CW], U8)
-SCRATCH["x3"] = ("sbuf", [128, 2048], BF)
+SCRATCH["x3"] = ("sbuf", [128, 2432], BF)
 for _t in range(R):
-    for _n, _w, _d in (("x", 3584, BF), ("etab", 640, F32), ("sq", 128, X4), ("ss", 128, U8), ("lq", 128, X4), ("ls", 128, U8),
-                       ("cnt", 8, F32), ("lcnt", 8, F32)):
+    for _n, _w, _d in (("x", 4 * (doff(_t) + 516), BF), ("lq", 224, X4), ("ls", 224, U8), ("cnt", 8, F32), ("lcnt", 8, F32)):
         SCRATCH["%s%d" % (_n, _t)] = ("sbuf", [128, _w], _d)
 for _b in range(8):
     SCRATCH["pb%d" % _b] = ("psum", [128, 512], F32)
@@ -51,8 +59,6 @@ def emit(g, T, ops):
     writer, readers, seq, marked, done = {}, {}, {}, {}, {}
     for o in ops:
         q = o["q"]
-        if q == "G" and not o["sem"]:
-            o["w"].append("pool")
         need = []
         for k in o["r"]:
             need.append(writer[k])
@@ -137,17 +143,20 @@ def rank_program(g, core, T, topo):
     def ms(ap, c, w, r=()):
         op("V", lambda: V.memset(ap, c), r, w)
 
-    def tp(out, a, r, w):
-        op("V", lambda: V.transpose(out, a), r, w)
-
-    def scan(out, a, b, o0, o1, r, w):
-        op("V", lambda: V.tensor_tensor_scan(out, a, b, 0.0, o0, o1), r, w)
+    def scan(out, a, b, init, o0, o1, r, w):
+        op("V", lambda: V.tensor_tensor_scan(out, a, b, init, o0, o1), r, w)
 
     def quant(q, s, a, r, w):
         op("V", lambda: V.quantize_mx(q, s, a), r, w)
 
     def act(out, a, f, r, w, **kw):
         op("S", lambda: S.activation(out, a, f, **kw), r, w)
+
+    def move(q, out, a, r, w):
+        if q == "V":
+            cp(out, a, r, w)
+        else:
+            act(out, a, AF.Copy, r, w)
 
     def mm(bank, width, lq, lsc, rq, rsc, r, start=True, stop=True):
         op("T", lambda: PE.matmul_mx(T["pb%d" % bank][:, 0:width], lq, lsc, rq, rsc, start, stop), r, ["pb%d" % bank], chain=not start)
@@ -168,328 +177,304 @@ def rank_program(g, core, T, topo):
         for b, bank in enumerate(banks):
             mm(bank, 128, T.wq[:, 128 * b:128 * b + 128], T.wsc[:, 128 * b:128 * b + 128], q, s, ["wq", "wsc"] + r)
 
-    def unpack(b, bank):
-        mm(bank, 512, T.eq[:, 128 * b:128 * b + 128], T.es[:, 128 * b:128 * b + 128], T.xq[:], T.xsc[:], ["eq", "xq"])
+    def unpack():
+        for b in range(4):
+            mm(4 + b, 512, T.eq[:, 128 * b:128 * b + 128], T.es[:, 128 * b:128 * b + 128], T.xq[:], T.xsc[:], ["eq", "xq"])
 
-    ci, cf, cu, sm, pp = T.ci, T.cf, T.cu, T.sm, T.pp
+    ci, cf, sm = T.ci, T.cf, T.sm
     ID = AF.Identity
     dma("Y", T.ut[:], T.u[:], [], ["ut"])
     dma("S", T.x0[:, 0:1024], T.x[:, 0:1024], [], ["x0a"])
     dma("Y", T.x0[:, 1024:2048], T.x[:, 1024:2048], [], ["x0b"])
-    dma("Y", T.wq[:].bitcast(dt.uint8), T.wc[:], [], ["wq"])
+    dma("Y", T.wq[:].bitcast(dt.uint8), T.wc[:], ["x0b"], ["wq"])
     dma("Y", T.wsc[:], T.ws[:], [], ["wsc"])
     dma("Y", T.vt[:], T.v[:], [], ["vt"])
 
-    PKU, PK4U, UPU, NATU = cu[:, 0:2], cu[:, 2:4], cu[:, 4:20], cu[:, 20:52]
-    RF, SF, HF, R4, RLAB, KB, PLB, OFF, C8, C9, C10, C11 = (cf[:, i:i + 1] for i in range(12))
-    TC, TCL, PAGEL, MASK, CR, ROW = (cf[:, 32 * i:32 * i + 32] for i in range(1, 7))
-    KCOL, NKCOL, K16C, KP1, NAT = cf[:, 224:230], cf[:, 232:238], cf[:, 240:246], cf[:, 248:254], cf[:, 256:288]
-    off = LAB - 0.5 + 1.0 / 1024
-    iota(ci[:, 16:17], [[0, 1]], 0, 1, ["ci_p"], False)
-    iota(ci[:, 0:16], [[16, 2], [32, 4], [0, 2]], 0, 0, ["ci_u"], False)
-    iota(T.mk[:], [[0, 16], [1, 32]], 0, 0, ["mk0"])
-    ms(T.seg[:], 1.0, ["seg0"])
-    op("G", lambda: g.affine_select(T.idn[:], T.seg[:, 0:128], [[-1, 128]], A.is_equal, 0.0, 0, 1), ["seg0"], ["idn"])
-    iota(T.kk[:], [[16, 96]], 0, 0, ["k16"])
-    iota(ROW, [[0, 2], [1, 16]], 0, 0, ["row"])
-    iota(TC, [[0, 8], [1, 4]], 0, 0, ["tc0"])
-    iota(MASK, [[1, 2], [0, 16]], 0, 0, ["mask0"])
-    iota(CR, [[0, 2], [32, 16]], 16 * len(VROWS), 0, ["cr0"])
-    iota(T.vsrc[:], [[1, 32], [640, 4], [32, 4]], 0, 0, ["vsrc0"])
-    ms(T.zer[:], 0.0, ["zer"])
+    RF, GF, R4, T4, HF, NA, NB, RW, TB4, KB0, KB1, CC0, CC1, K2R = (cf[:, i:i + 1] for i in range(14))
+    KEY, W, WL, MN, CA, CB, K2, K3 = (sm[:, i:i + 1] for i in range(8))
+    iota(ci[:, 8:9], [[0, 1]], 0, 1, ["ci_p"], False)
+    iota(T.qq[:], [[1, 32]], 0, 0, ["qq"])
+    iota(ci[:, 0:8], [[16, 8]], 0, 0, ["ci_u"], False)
+    iota(T.qs[:], [[0, 32], [1, 16]], 0, 0, ["qs"])
+    iota(T.gq[:], [[1, 8], [0, 64]], 0, 0, ["gq"])
+    iota(T.cr[:, 0:M0], [[16, M0]], 8 * (32 - M0), 0, ["cr_a"])
+    iota(T.cr[:, M0:32], [[0, 32 - M0]], 248, 0, ["cr_b"])
+    ms(T.one[:], 1.0, ["one"])
     for b in range(4):
-        act(T.et[:, 512 * b:512 * b + 512], T.zer[:], AF.Copy, ["zer"], ["etz%d" % b])
-    for b in range(4):
-        act(T.et[:, 512 * b + b:512 * b + 512:4], T.idn[:], AF.Copy, ["idn", "etz%d" % b], ["et%d" % b])
-    ms(T.kt[:], 0.0, ["kt"])
-    cp(UPU, ci[:, 0:16], ["ci_u"], ["upu"])
-    ts(ci[:, 17:18], ci[:, 16:17], 15, None, A.bitwise_and, None, ["ci_p"], ["ci_r"])
-    ts(ci[:, 18:19], ci[:, 16:17], 31, None, A.bitwise_and, None, ["ci_p"], ["ci_s"])
-    ts(ci[:, 19:20], ci[:, 16:17], 16, 4, A.bitwise_and, A.logical_shift_right, ["ci_p"], ["ci_h"])
-    ts(ci[:, 20:21], ci[:, 16:17], 12, 2, A.bitwise_and, A.logical_shift_right, ["ci_p"], ["ci_4"])
-    for a in range(4):
-        ms(T.kt[32 * a:32 * a + 32, 128 * a:128 * a + 64:2], 1.0, ["kt%d" % a], ["kt"])
-        ms(T.kt[32 * a:32 * a + 32, 128 * a + 65:128 * a + 128:2], 1.0, ["kt%d" % (4 + a)], ["kt"])
-    cp(cf[:, 0:4], ci[:, 17:21], ["ci_r", "ci_s", "ci_h", "ci_4"], ["cols"])
-    for i, (w, ra, rb) in enumerate(TILES):
-        lo = 32 * min(ra if ra else 16, rb)
-        ms(T.ct[:, 4 * (TBASE[i] + lo):4 * (TBASE[i] + w)], 0.0, ["c%d_%d" % (i, t) for t in range(4)])
-    ts(T.mk[:], T.mk[:], SF, 0.5, A.is_ge, A.subtract, ["mk0", "cols"], ["mk1"])
+        op("G", lambda b=b: g.affine_select(T.et[:, 512 * b:512 * b + 512], T.one[:], [[-1, 512]], A.is_equal, 0.0, b, 4), ["one"], ["et%d" % b])
+    iota(T.vsrc[:], [[640, 4], [1, 128]], 512 * LAB, 0, ["vs0", "vs1"])
+    iota(T.mkb[:], [[0, 2], [1, 2], [0, 16]], 0, 0, ["mkb0"])
+    iota(T.jj[:], [[16, 32]], 0, 0, ["jj0"])
+    iota(T.kk[:], [[8, 24]], 256, 0, ["kk0"])
+    iota(T.lab[:], [[8, 4], [0, 8]], 8 * LAB, 0, ["lab"])
+    iota(T.o[:, 512:528], [[0, 16]], 1000000, 0, ["o_hi"])
+    for t in range(R):
+        iota(T["x%d" % t][:, 4 * doff(t) + 2048:4 * doff(t) + 2064], [[0, 16]], 0, 0, ["dz%d" % t])
+    iota(T.st[:, 384:512], [[0, 128]], 0, 0, ["st_hi"])
+
+    ts(ci[:, 9:10], ci[:, 8:9], 15, None, A.bitwise_and, None, ["ci_p"], ["ci_r"])
+    ts(ci[:, 10:11], ci[:, 8:9], 4, None, A.logical_shift_right, None, ["ci_p"], ["ci_g"])
+    ts(ci[:, 11:12], ci[:, 8:9], 12, 2, A.bitwise_and, A.logical_shift_right, ["ci_p"], ["ci_4"])
+    ts(ci[:, 12:13], ci[:, 8:9], 3, None, A.bitwise_and, None, ["ci_p"], ["ci_t"])
+    ts(ci[:, 13:14], ci[:, 8:9], 16, 4, A.bitwise_and, A.logical_shift_right, ["ci_p"], ["ci_h"])
+    cp(T.upu[:], ci[:, 0:8], ["ci_u"], ["upu"])
+    cp(cf[:, 0:5], ci[:, 9:14], ["ci_r", "ci_g", "ci_4", "ci_t", "ci_h"], ["cols"])
+    for i in range(8):
+        lo = 16 * (29 - 4 * i)
+        ms(T.ct[:, 4 * (TBASE[i] + lo):4 * (TBASE[i] + TW[i])], 0.0, ["c%d" % m for m in range(29 - 4 * i, 33 - 4 * i)])
+        if i == 0:
+            ts(T.ea[:], T.qq[:], RF, None, A.is_equal, None, ["qq", "cols"], ["ea"])
+            ts(T.rfu[:], T.qq[:], 0.0, RF, A.mult, A.add, ["qq", "cols"], ["rfu"])
+            act(T.mk[:], T.ea[:].indirect(T.rfu[:]), AF.Copy, ["ea", "rfu"], ["mk"], scale=2e29, bias=-1e29)
+            act(T.rst[:], T.qs[:], AF.Copy, ["qs"], ["rst"], scale=2e29, bias=-1e29)
     quant(T.uq[:], T.us[:], T.ut[:], ["ut"], ["uq"])
-    ms(T.rs[:], 0.0, ["rs%d" % i for i in range(32)])
-    cp(T.upq[:].bitcast(dt.uint32), T.uq[:].bitcast(dt.uint32).indirect(UPU), ["uq", "upu"], ["upq"])
-    act(T.ups[:], T.us[:].indirect(UPU), AF.Copy, ["uq", "upu"], ["ups"])
-    act(T.mk[:], T.mk[:], AF.Copy, ["mk1"], ["mk"], scale=2e29)
-    quant(T.kq[:], T.ks[:], T.kt[:], ["kt%d" % a for a in range(8)], ["kq"])
-    ms(T.sb[:, 255:8192:256], 0.0, ["sb%d" % i for i in range(32)])
+    ts(T.kt[:], T.gq[:], GF, None, A.is_equal, None, ["gq", "cols"], ["kt"])
+    cp(T.upq[:].bitcast(dt.uint32), T.uq[:].bitcast(dt.uint32).indirect(T.upu[:]), ["uq", "upu"], ["upq"])
+    act(T.ups[:], T.us[:].indirect(T.upu[:]), AF.Copy, ["uq", "upu"], ["ups"])
+    ms(T.rs[:, 0:1], 0.0, ["rs0"])
+    quant(T.kq[:], T.ks[:], T.kt[:], ["kt"], ["kq"])
 
     def constants_1():
-        ms(T.seg[:, 0:512:32], 0.0, ["seg", "seg0"])
-        ms(OFF, off, ["off"])
-        ts(C8, RF, 32.0, None, A.mult, None, ["cols"], ["c8"])
-        ts(C9, R4, 32.0, None, A.mult, None, ["cols"], ["c9"])
-        ts(C11, RF, 4.0, BIG - 7.5, A.is_ge, A.mult, ["cols"], ["c11a"])
-        ts(MASK, MASK, HF, 4 * BIG, A.not_equal, A.mult, ["mask0", "cols"], ["mask"])
-        ts(PKU, T.kk[:, 0:2], C8, None, A.add, None, ["k16", "c8"], ["pku"])
-        ts(PK4U, T.kk[:, 0:2], C9, None, A.add, None, ["k16", "c9"], ["pk4u"])
-        act(RLAB, RF, ID, ["cols", "off"], ["rlab0"], bias=OFF)
-        act(KCOL, T.kk[:, 0:6], ID, ["k16", "cols"], ["kcol"], bias=RF)
-        act(PLB, C8, ID, ["cols", "c8"], ["plb"], bias=HF)
-        act(T.vsrc[:], T.vsrc[:], AF.Copy, ["vsrc0"], ["vsrc"], scale=1.0 / 512)
-        act(K16C, KCOL, AF.Copy, ["kcol"], ["k16c"], scale=16.0)
-        act(PAGEL, ROW, ID, ["row", "plb"], ["pagel"], bias=PLB, scale=2.0)
+        ts(T.ca[:], T.ea[:, 1:17], -2.0, None, A.mult, None, ["ea"], ["ca0"])
+        act(CC0, RF, AF.Copy, ["cols"], ["cc0"], scale=-1.0, bias=15.0 - HOLD - BP)
+        tt(T.ca[:], T.ca[:], T.ea[:, 0:16], A.add, ["ea", "ca0"], ["ca"])
+        act(CC1, T.ea[:, 15:16], ID, ["ea", "cc0"], ["cc1"], scale=HOLD, bias=CC0)
+        act(T.cx[:], T.ca[:].indirect(T.rfu[:]), AF.Copy, ["ca", "rfu"], ["cxu", "cxm", "cxl"], scale=HOLD)
+        act(T.cr[:], T.cr[:], ID, ["cr_a", "cr_b", "cc1"], ["cr"], bias=CC1)
 
     def constants_2():
-        crk = []
-        for b in range(min(VROWS), 16):
-            c = 32.0 * b + 16.0 * len([k for k in VROWS if k > b]) - (16.0 * b if b in VROWS else 0.0)
-            ms(cf[:, 160 + b:192:16], c, ["cr%d" % b], ["cr0"])
-            crk.append("cr%d" % b)
-        ts(RLAB, RLAB, LAB - off, None, A.add, None, ["rlab0"], ["rlab"])
-        ts(C11, C11, 2048.0 - 7.5, None, A.max, None, ["c11a"], ["c11"])
-        ts(CR, CR, SF, None, A.add, None, crk + ["cols"], ["cr"])
-        ts(TCL, TC, 1.0 / 2048, LAB, A.mult, A.add, ["tc0"], ["tcl"])
-        ts(KB, RF, C11, None, A.add, None, ["cols", "c11"], ["kb"])
-        ts(TC, TC, 1.0 / 2048, None, A.mult, None, ["tc0"], ["tc", "tc0"])
-        ts(NKCOL, KCOL, -1.0, -0.5, A.mult, A.add, ["kcol"], ["nkcol"])
-        ts(KP1, KCOL, 1.0, None, A.add, None, ["kcol"], ["kp1"])
-        ms(T.o[:, 512:640], 64.0, ["o_hi"])
-        ms(T.pg[:, 96:128], 1.0, ["pg_hi"])
-        ms(T.db[:, 2048:2064], 0.0, ["db_z"])
+        ms(T.zer[:], 0.0, ["zer"])
+        ts(T.eb[:, 0:8], T.qq[:, 0:8], R4, None, A.is_equal, None, ["qq", "cols"], ["eb"])
+        ts(T.tfu[:], T.qq[:, 0:8], 0.0, T4, A.mult, A.add, ["qq", "cols"], ["tfu"])
+        ts(KB0, RF, 4.0, BIG - 256.0, A.is_ge, A.mult, ["cols"], ["kb0"])
+        ts(T.cb[:, 0:4], T.eb[:, 1:5], -2.0, None, A.mult, None, ["eb"], ["cb0"])
+        ts(KB1, RF, 1.0 / 256, 512.0 + LAB / 256.0, A.mult, A.add, ["cols"], ["kb1"])
+        ts(T.mkb[:], T.mkb[:], HF, 4 * BIG, A.not_equal, A.mult, ["mkb0", "cols"], ["mkb1"])
+        tt(T.cb[:, 0:4], T.cb[:, 0:4], T.eb[:, 0:4], A.add, ["eb", "cb0"], ["cb1"])
+        ts(NA, RF, -512.0, 0.5 - 512.0 * LAB, A.mult, A.add, ["cols"], ["na"])
+        ts(T.mkb[:, 0:32], T.mkb[:, 0:32], KB0, KB1, A.add, A.add, ["mkb1", "kb0", "kb1"], ["mkb"])
+        ts(T.mkb[:, 32:64], T.mkb[:, 32:64], KB0, 512.0, A.add, A.add, ["mkb1", "kb0"], ["mkc"])
+        ts(T.cb[:, 3:4], T.cb[:, 3:4], -2.0, None, A.add, None, ["cb1"], ["cb"])
+        ts(NB, RF, -512.0, 0.5 - 512.0 * (LAB + 1), A.mult, A.add, ["cols"], ["nb"])
+        for t in range(R):
+            k = 16 * NPASS[t]
+            quant(T["lq%d" % t][:, k:k + 128], T["ls%d" % t][:, k:k + 128], T.zer[:], ["zer"], ["lz%d" % t])
 
     def constants_3():
-        ts(C10, RF, 16.0, None, A.mult, None, ["cols"], ["c10"])
+        act(T.cq[:], T.cb[:].indirect(T.tfu[:]), AF.Copy, ["cb", "tfu", "cb_hi"], ["cq"], scale=B4)
+        act(T.jj[:], T.jj[:], ID, ["jj0", "cols"], ["jj"], bias=RF)
+        act(K2R, R4, AF.Copy, ["cols"], ["k2r"], scale=2.0)
+        act(TB4, T4, AF.Copy, ["cols"], ["tb4"], scale=0.25, bias=B4)
+        act(T.kcol[:, 8:14], T.jj[:, 0:6], AF.Copy, ["jj"], ["nk"], scale=-1.0, bias=-0.5)
+
+    def constants_4():
+        act(T.kk[:], T.kk[:], ID, ["kk0", "k2r"], ["kk"], bias=K2R)
+        act(T.js[:], T.jj[:], AF.Copy, ["jj"], ["js"], scale=1.0 / 64, bias=-8.0 * LAB)
+        act(RW, RF, AF.Copy, ["cols"], ["rw"], scale=512.0, bias=512.0 * LAB)
+        act(T.dump[:], T.kk[:], AF.Copy, ["kk"], ["dump"], scale=0.5, bias=384.0 - B4)
         for t in range(R - 1):
-            ts(cf[:, 12 + 4 * t:13 + 4 * t], RF, 5.0 + 2 * t, None, A.is_equal, None, ["cols"], ["i5%d" % t])
-            ts(cf[:, 13 + 4 * t:14 + 4 * t], RF, 4.0 + 2 * t, 2048.0, A.is_equal, A.mult, ["cols"], ["i4%d" % t])
-        for i, c in enumerate((4.5, 6.5, BIG, 2 * BIG)):
-            ms(cf[:, 20 + i:21 + i], c, ["half%d" % i])
+            act(cf[:, 16 + t:17 + t], T.ea[:, 4 + 2 * t:5 + 2 * t], AF.Copy, ["ea"], ["c4%d" % t], scale=256.0 - BIG)
+        for t in range(R - 1):
+            act(cf[:, 18 + t:19 + t], T.ea[:, 5 + 2 * t:6 + 2 * t], ID, ["ea", "c4%d" % t], ["c5%d" % t], scale=-256.0 - BIG,
+                bias=cf[:, 16 + t:17 + t])
 
-    where = {}
-    for i, (w, ra, rb) in enumerate(TILES):
-        for h in range(2):
-            where[(h, ra)] = (i, h)
-            where[(h, rb)] = (i, 2 + h)
+    iota(T.cb[:, 4:8], [[0, 4]], 0, 0, ["cb_hi"])
+    iota(T.tab[:], [[1, 4096]], 512 * LAB, 0, ["tab"])
 
-    def lane(h, b, lo, hi):
-        i, t = where[(h, b)]
-        return T.ct[:, 4 * (TBASE[i] + lo) + t:4 * (TBASE[i] + hi):4]
+    def lane(m, lo, hi):
+        i, k = (32 - m) // 4, (32 - m) % 4
+        return T.ct[:, 4 * (TBASE[i] + lo) + k:4 * (TBASE[i] + hi):4]
 
-    def lkey(h, b):
-        return "c%d_%d" % where[(h, b)]
+    def pivot(m):
+        return T.sc[:, 16 * m + 15:16 * m + 16]
 
-    def labels():
-        cp(T.o[:].indirect(T.posv[:, 0:6]), T.nv[:], ["pos2", "nv"], ["o_w", "o_r", "o_hi"])
-        act(T.vsrc[:], T.o[:].indirect(T.rku[:]), AF.Copy, ["o_w", "o_r", "o_hi", "rku"], ["vsrc"])
+    def tile(i):
+        lo, w = TBASE[i], TW[i]
+        quant(T.cc[:, lo:lo + w], T.cs[:, lo:lo + w], T.ct[:, 4 * lo:4 * (lo + w)], ["c%d" % m for m in range(29 - 4 * i, 33 - 4 * i)], ["cc%d" % i])
+        if w > 256:
+            mm(2, w - 256, T.kq[:], T.ks[:], T.cc[:, lo + 256:lo + w], T.cs[:, lo + 256:lo + w], ["kq", "cc%d" % i], i == 0, i == 3)
+        w = min(w, 256)
+        mm(3, w, T.kq[:], T.ks[:], T.cc[:, lo:lo + w], T.cs[:, lo:lo + w], ["kq", "cc%d" % i], i == 0, i == 7)
 
-    def keys(t, cnt):
-        i5, i4 = cf[:, 12 + 4 * t:13 + 4 * t], cf[:, 13 + 4 * t:14 + 4 * t]
-        act(sm[:, 3:4], i5, ID, ["i5%d" % t, "i4%d" % t, "cnt%d" % t], ["ka"], scale=cnt, bias=i4)
-        act(sm[:, 4:5], T.cw[:, 63:64], ID, ["kb", "cw"], ["kb1"], scale=-1.0, bias=KB)
-        act(sm[:, 5:6], RLAB, AF.Abs, ["rlab", "vlab"], ["kd"], scale=-1.0, bias=sm[:, 1:2])
-        act(sm[:, 6:7], RF, AF.Abs, ["cols", "half%d" % t], ["ke"], scale=-1.0, bias=cf[:, 20 + t:21 + t])
-        act(sm[:, 7:8], sm[:, 3:4], ID, ["ka", "kb1"], ["kf"], bias=sm[:, 4:5])
-        act(sm[:, 8:9], sm[:, 5:6], AF.Relu, ["kd", "half2"], ["kg"], scale=-BIG, bias=cf[:, 22:23])
-        act(sm[:, 9:10], sm[:, 6:7], AF.Relu, ["ke", "half3"], ["kh"], scale=-2 * BIG, bias=cf[:, 23:24])
-        act(sm[:, 10:11], sm[:, 8:9], ID, ["kg", "kf"], ["ki"], bias=sm[:, 7:8])
-        act(KB, sm[:, 9:10], ID, ["kh", "ki"], ["kb"], scale=-1.0, bias=sm[:, 10:11])
+    def places(h):
+        lo = 256 * h
+        bank = "pb%d" % (3 - h)
+        scan(T.rk[:, lo:lo + 256], T[bank][:, 0:256], T.cx[:, lo:lo + 256], -2 * HOLD, A.max, A.add,
+             ["cxu", "cxm"] if h else ["cxl"], ["rk%d" % h, bank])
+        ts(T.rku[:, 16 * h:16 * h + 16], T.rk[:, lo + 15:lo + 256:16], BP, None, A.add, None, ["rk%d" % h], ["rku%d" % h])
 
-    th, tmh = (T.ta, T.tb), (T.tm, T.tb)
-
-    def compare(h, b):
-        ts(lane(h, b, 0, 32 * b), T["pb%d" % h][:, 0:32 * b], th[h][:, 32 * b:32 * b + 1], 0.5, A.is_lt, A.subtract,
-           ["t%d" % h], [lkey(h, b), "pb%d" % h])
+    def sort(h):
+        cp(T.o[:, 0:512].indirect(T.rku[:, 16 * h:16 * h + 16]), T.vsrc[:, 256 * h:256 * h + 256], ["rku%d" % h, "vs%d" % h], ["o"])
 
     xkeys = ["x0a", "x0b"]
     for t in range(R):
         X, XN = T["x%d" % t], T["x%d" % (t + 1)]
         xk = "x%d" % t
-        et = T["etab%d" % t]
+        yo, do = 4 * yoff(t), 4 * doff(t)
+        np_, na = NPASS[t], APASS[t]
+        nv, ns = np_ - na, 16 * np_
+        cnt, lcnt, lq, ls = T["cnt%d" % t][:, 0:1], T["lcnt%d" % t][:, 0:1], T["lq%d" % t], T["ls%d" % t]
         quant(T.xq[:], T.xsc[:], X[:, 0:2048], xkeys, ["xq"])
-        for bank, h in ((0, 0), (2, 0), (1, 1), (3, 1)):
-            mm(bank, 512, T.upq[:, 128 * h:128 * h + 128], T.ups[:, 128 * h:128 * h + 128], T.xq[:], T.xsc[:], ["upq", "ups", "xq"])
+        for bank in range(2):
+            mm(bank, 512, T.upq[:], T.ups[:], T.xq[:], T.xsc[:], ["upq", "ups", "xq"])
         if t:
-            labels()
+            unpack()
         else:
             constants_1()
-        tp(T.ta[:], T.pb0[:], [], ["t0", "pb0"])
-        for a in range(4):
-            op("G", lambda a=a: g.affine_select(T.tm[32 * a:32 * a + 32, :], T.ta[32 * a:32 * a + 32, :], [[0, 16], [-1, 32]],
-                                                A.is_ge, -1e29, 0, 1), ["t0"], ["tm0_%d" % a])
-        iota(et[:, 0:128], [[1, 4], [4, 32]], 512, 0, ["etab%da" % t])
-        iota(et[:, 128:640], [[0, 512]], 0, 0, ["etab%db" % t])
-        if t == 0:
-            iota(T.srcb[:], [[1, 3], [4, 32]], 640, 0, ["srcb"])
-            iota(NAT, [[1, 16], [256, 2]], 0, 0, ["nat"])
-        compare(0, VROWS[0])
-        tt(T.pm[:], T.pb1[:], T.mk[:], A.min, ["mk"], ["pm", "pb1"])
-        tp(T.tb[:], T.pm[:], ["pm"], ["t1"])
-        if t:
-            for b in range(3):
-                unpack(b, 5 + b)
+        for h in (1, 0):
+            lo = 256 * h
+            tt(T.pm[:, lo:lo + 256], T.pb0[:, lo:lo + 256], T.mk[:, lo:lo + 256], A.min, ["mk"], ["pm%d" % h, "pb0"])
+            if h == 0:
+                ts(lane(31, 0, 496), T.pb0[:, 0:496], pivot(31), 0.5, A.is_lt, A.subtract, ["sc1"], ["c31", "pb0"])
+            scan(T.sc[:, lo:lo + 256], T.rst[:, lo:lo + 256], T.pm[:, lo:lo + 256], 0.0, A.min, A.max, ["rst", "pm%d" % h], ["sc%d" % h])
 
-        arows = [(h, b) for h in range(2) for b in AORDER[:3]] + [(h, b) for b in AORDER[3:] for h in range(2)]
+        arows = list(range(M0 - 1, 0, -1))
         for k in range(len(arows) + 1):
             if k < len(arows):
-                h, b = arows[k]
-                act(T.sg[:, 480 * (k % 4):480 * (k % 4) + 32 * b], T["pb%d" % (2 + h)][:, 0:32 * b], AF.Sign, ["t%d" % h],
-                    ["sg%d" % (k % 4), "pb%d" % (2 + h)], bias=th[h][:, 32 * b:32 * b + 1], scale=-1.0)
+                m = arows[k]
+                act(T.sg[:, 512 * (k % 4):512 * (k % 4) + 16 * m], T.pb1[:, 0:16 * m], AF.Sign, ["sc%d" % (m // 16)],
+                    ["sg%d" % (k % 4), "pb1"], bias=pivot(m), scale=-1.0)
             if k:
-                h, b = arows[k - 1]
-                act(lane(h, b, 0, 32 * b), T.sg[:, 480 * ((k - 1) % 4):480 * ((k - 1) % 4) + 32 * b], AF.Relu, ["sg%d" % ((k - 1) % 4)],
-                    [lkey(h, b), "rs%d" % (16 * h + b)], accum_out=T.rs[:, 16 * h + b:16 * h + b + 1])
-
-        nq = 0
-        for step in VPLAN:
-            if step[0] == "r":
-                b = int(step[1:])
-                for h in range(1 if b == VROWS[0] else 0, 2):
-                    compare(h, b)
-                for h in range(2):
-                    e = 256 * (16 * h + b + 1)
-                    scan(T.sb[:, e - 16 * b:e], lane(h, b, 0, 16 * b), lane(h, b, 16 * b, 32 * b), A.add, A.add, [lkey(h, b)],
-                         ["sb%d" % (16 * h + b)])
-            elif step[0] == "q":
-                i = int(step[1:])
-                lo, hi = TBASE[i], TBASE[i] + TILES[i][0]
-                quant(T.cq[:, lo:hi], T.cs[:, lo:hi], T.ct[:, 4 * lo:4 * hi], ["c%d_%d" % (i, k) for k in range(4)], ["cq%d" % i])
-                mm(4, hi - lo, T.kq[:], T.ks[:], T.cq[:, lo:hi], T.cs[:, lo:hi], ["kq", "cq%d" % i], nq == 0, nq == len(TILES) - 1)
-                nq += 1
-            elif step == "d":
-                for h in (1, 0):
-                    tt(lane(h, 0, 0, 512), T["pb%d" % h][:], tmh[h][:], A.is_lt, ["t1"] if h else ["tm0_%d" % a for a in range(4)],
-                       [lkey(h, 0), "pb%d" % h])
-                for h in (1, 0):
-                    scan(T.ds[:, 512 * h:512 * h + 512], T.seg[:], lane(h, 0, 0, 512), A.mult, A.add, ["seg", lkey(h, 0)], ["ds%d" % h])
-            elif step == "n1":
-                if t == 0:
-                    quant(T.eq[:], T.es[:], T.et[:], ["et%d" % b for b in range(4)], ["eq"])
-                    for b in range(3):
-                        unpack(b, 5 + b)
-                    constants_2()
-                tt(T.rn[:], T.sb[:, 255:8192:256], T.ds[:, 31:1024:32], A.add, ["sb%d" % i for i in range(32)] + ["ds0", "ds1"], ["rn"])
-            elif step == "n2":
-                tt(T.rna[:], CR, T.rn[:], A.subtract, ["cr", "rn"], ["rn2"])
-        tt(T.rnb[:], T.rna[:], T.rs[:], A.subtract, ["rn2"] + ["rs%d" % i for i in range(32)], ["rn3"])
-        unpack(3, 2)
-        for b, bank in enumerate((5, 6, 7, 2)):
-            act(T.db[:, b:2048:4], T["pb%d" % bank][:], AF.Copy, [], ["db%d" % b, "pb%d" % bank])
-        tp(T.tr[:], T.pb4[:], [], ["tr", "pb4"])
-        tt(T.rk[:], T.tr[:].indirect(PKU), T.rnb[:], A.add, ["tr", "pku", "rn3"], ["rk"])
-        tp(T.rkt[:], T.rk[:], ["rk"], ["rkt"])
-        cp(T.rku[:], T.rkt[:], ["rkt"], ["rku"])
-        cp(T.o[:, 0:512].indirect(T.rku[:]), T.vsrc[:], ["rku", "vsrc"], ["o_w", "o_r"])
-        act(T.lb[:, 128:512], T.o[:, 128:512], ID, ["o_r", "off"], ["lb_r"], bias=OFF)
-        ts(T.lb[:, 0:128], T.o[:, 0:128], off, None, A.add, None, ["o_w"], ["lb_w"])
-        ts(T.eqw[:], T.lb[:, 0:128], RLAB, 16.0, A.is_equal, A.mult, ["lb_w", "rlab"], ["eqw"])
-        tt(T.fr[:], T.o[:, 0:128], T.lb[:, 0:128], A.subtract, ["o_w", "lb_w"], ["fr"])
-        scan(T.cw[:], T.eqw[:, 0:64], T.eqw[:, 64:128], A.add, A.add, ["eqw"], ["cw"])
-        tp(T.frt[:], T.fr[:], ["fr"], ["frt"])
-        ts(T.km[:], MASK, KB, T.cw[:, 63:64], A.add, A.subtract, ["mask", "kb", "cw"], ["km"])
-        tt(T.tl[:], T.frt[:].indirect(PK4U), TCL, A.add, ["frt", "pk4u", "tcl"], ["tl"])
-        tp(T.kmt[:], T.km[:], ["km"], ["kmt"])
-        tp(T.tlt[:], T.tl[:], ["tl"], ["tlt"])
-        op("V", lambda: V.tensor_reduce(sm[:, 0:1], T.kmt[:], AxisListType.X, A.min), ["kmt"], ["key"])
-        ts(T.tlu[:], T.tlt[:], 2048.0, None, A.mult, None, ["tlt"], ["tlu"])
+                m = arows[k - 1]
+                act(lane(m, 0, 16 * m), T.sg[:, 512 * ((k - 1) % 4):512 * ((k - 1) % 4) + 16 * m], AF.Relu, ["sg%d" % ((k - 1) % 4)],
+                    ["c%d" % m, "rs%d" % m], accum_out=T.rs[:, m:m + 1])
+        tt(lane(32, 0, 512), T.pb0[:], T.sc[:], A.is_le, ["sc0", "sc1"], ["c32", "pb0"])
+        for m in range(31, M0 - 1, -1):
+            if m > M0:
+                ts(lane(m - 1, 0, 16 * m - 16), T.pb0[:, 0:16 * m - 16], pivot(m - 1), 0.5, A.is_lt, A.subtract, ["sc1"], ["c%d" % (m - 1), "pb0"])
+            if m == 31:
+                scan(T.ds[:], T.qs[:], lane(32, 0, 512), 0.0, A.min, A.add, ["qs", "c32"], ["ds"])
+            e = 256 * (m + 1)
+            scan(T.sb[:, e - 8 * m:e], lane(m, 0, 8 * m), lane(m, 8 * m, 16 * m), 0.0, A.add, A.add, ["c%d" % m], ["sb%d" % m])
+            if m == 30:
+                tt(T.rna[:], T.cr[:], T.ds[:, 15:512:16], A.subtract, ["cr", "ds"], ["rna"])
+            if m % 4 == 1:
+                tile((29 - m) // 4)
+        tt(T.cx[:, 16 * M0 + 15:512:16], T.rna[:, M0:32], T.sb[:, 256 * M0 + 255:8192:256], A.subtract,
+           ["rna"] + ["sb%d" % m for m in range(M0, 32)], ["cxu"])
+        if t == 0:
+            quant(T.eq[:], T.es[:], T.et[:], ["et%d" % b for b in range(4)], ["eq"])
+        for i in range((32 - M0 + 1) // 4, 4):
+            tile(i)
+        if t == 0:
+            unpack()
+            constants_2()
+            constants_3()
+        tt(T.cx[:, 271:16 * M0:16], T.rna[:, 16:M0], T.rs[:, 16:M0], A.subtract, ["rna"] + ["rs%d" % m for m in range(16, M0)], ["cxm"])
+        tile(4)
+        places(1)
+        tile(5)
+        sort(1)
+        tile(6)
+        tt(T.cx[:, 15:256:16], T.rna[:, 0:16], T.rs[:, 0:16], A.subtract, ["rna"] + ["rs%d" % m for m in range(16)], ["cxl"])
+        tile(7)
+        for b in range(4):
+            act(X[:, do + b:do + 2048:4], T["pb%d" % (4 + b)][:], AF.Copy, [], ["db%d" % b, "pb%d" % (4 + b)])
+        places(0)
+        sort(0)
+        act(T.junkd[:, 0:128], T.o[:, 0:128], AF.Sign, ["o", "na"], ["jd0", "ca_"], bias=NA, accum_out=CA)
+        act(T.junkd[:, 128:256], T.o[:, 0:128], AF.Sign, ["o", "nb"], ["jd1", "cb_"], bias=NB, accum_out=CB)
+        act(T.lb[:], T.o[:, 128:512], AF.Copy, ["o"], ["lb"], scale=1.0 / 131072, bias=(1.0 / 1024 - 0.5) / 256)
+        scan(T.tsc[:], T.o[:, 0:128], T.cq[:], -B4, A.max, A.add, ["o", "cq"], ["tsc"])
+        rkk = ["rku0", "rku1"]
+        ts(T.wa[:], T.rku[:], 128.0, 8.0 * (LAB + 4 + 2 * t), A.is_lt, A.mult, rkk, ["wa"])
+        ts(T.ti[:], T.tsc[:, 3:128:4], B4, None, A.add, None, ["tsc"], ["ti"])
+        ts(T.km[:], T.mkb[:], CA, CB, A.subtract, A.add, ["mkb", "mkc", "ca_", "cb_"], ["km"])
+        ts(T.tj[:], T.ti[:], 511, None, A.bitwise_and, None, ["ti"], ["tj"])
+        op("V", lambda: V.transpose(T.kmt[:], T.km[:]), ["km"], ["kmt"])
+        ts(T.tlu[:], T.tj[:], 4.0, T4, A.mult, A.add, ["tj", "cols"], ["tlu"])
         act(T.tt[:], X[:, 0:2048].indirect(T.tlu[:]), AF.Copy, xkeys + ["tlu"], ["tt"])
-        cnt, lcnt = T["cnt%d" % t][:, 0:1], T["lcnt%d" % t][:, 0:1]
-        ts(cnt, sm[:, 0:1], ROUND16, ROUND16, A.add, A.subtract, ["key"], ["cnt%d" % t])
-        np_, na = NPASS[t], APASS[t]
-        nv = np_ - na
-        if np_ < 6:
-            ms(T.posu[:, np_:6], 512, ["posu_c"])
-        ts(sm[:, 1:2], sm[:, 0:1], cnt, LAB + 7.5, A.subtract, A.add, ["key", "cnt%d" % t], ["vlab"])
-        ts(pp[:, 0:6], K16C, cnt, None, A.is_ge, None, ["k16c", "cnt%d" % t], ["p1"])
+        op("V", lambda: V.tensor_reduce(KEY, T.kmt[:, 0:32], AxisListType.X, A.min), ["kmt"], ["key"])
+        op("V", lambda cnt=cnt: V.tensor_reduce(cnt, T.kmt[:, 32:64], AxisListType.X, A.min), ["kmt"], ["cnt%d" % t])
         send(lcnt, cnt, "ac%d" % t, ["cnt%d" % t])
         arrival("ac%d" % t, 1, ["lcnt%d" % t])
-        ts(T.fl[:], T.lb[:, 128:512], sm[:, 1:2], None, A.is_equal, None, ["lb_r", "vlab"], ["fl"])
-        ts(sm[:, 2:3], sm[:, 1:2], -LAB, None, A.add, None, ["vlab"], ["v"])
-        scan(T.kc[:], T.fl[:], T.zer[:, 0:384], A.add, A.add, ["fl", "zer"], ["kc"])
-        tt(pp[:, 16:22], pp[:, 0:6], KP1, A.mult, ["p1", "kp1"], ["p3"])
+        vk = ["key", "cnt%d" % t]
+        tt(T.lac[:], T.lab[:], T.wa[:], A.max, ["lab", "wa"], ["lac"])
+        ts(T.fl[:], T.lb[:], cnt, KEY, A.add, A.is_equal, ["lb"] + vk, ["fl"])
+        ts(WL, KEY, cnt, 2048.0, A.subtract, A.mult, vk, ["wl"])
+        scan(T.kc[:], T.fl[:], T.zer[:, 0:384], 0.0, A.add, A.add, ["fl", "zer"], ["kc"])
+        ts(W, KEY, cnt, 131072.0, A.subtract, A.mult, vk, ["w"])
         for m in range(nv, np_):
-            act(T.junka[:, 384 * (m - nv):384 * (m - nv + 1)], T.kc[:], AF.Sign, ["kc", "nkcol"], ["junk%d" % (m - nv), "pa%d" % m],
-                bias=cf[:, 232 + m:233 + m], accum_out=T.pa[:, m:m + 1])
+            act(T.junka[:, 384 * (m - nv):384 * (m - nv + 1)], T.kc[:], AF.Sign, ["kc", "nk"], ["junk%d" % (m - nv), "pa%d" % m],
+                bias=T.kcol[:, 8 + m:9 + m], accum_out=T.pa[:, m:m + 1])
         for m in range(nv):
-            ts(T.junkb[:, 384 * m:384 * m + 384], T.kc[:], cf[:, 224 + m:225 + m], 0.5, A.is_gt, A.subtract, ["kc", "kcol"], ["j2%d" % m])
+            ts(T.junkb[:, 384 * m:384 * m + 384], T.kc[:], T.jj[:, m:m + 1], 0.5, A.is_gt, A.subtract, ["kc", "jj"], ["j2%d" % m])
         for m in range(nv):
-            scan(T.junkc[:, 192 * m:192 * m + 192], T.junkb[:, 384 * m:384 * m + 192], T.junkb[:, 384 * m + 192:384 * m + 384], A.add, A.add,
+            scan(T.junkc[:, 192 * m:192 * m + 192], T.junkb[:, 384 * m:384 * m + 192], T.junkb[:, 384 * m + 192:384 * m + 384], 0.0, A.add, A.add,
                  ["j2%d" % m], ["j3%d" % m])
         quant(T.tq[:], T.ts[:], T.tt[:], ["tt"], ["tq"])
-        layer((0, 1, 3, 4), T.tq[:], T.ts[:], ["tq"])
+        layer((0, 1, 2, 3), T.tq[:], T.ts[:], ["tq"])
         ts(T.posu[:, 0:nv], T.junkc[:, 191:192 * nv:192], -1.0, 320.0, A.mult, A.add, ["j3%d" % m for m in range(nv)], ["posu_a"])
+        ts(T.wf[:], T.lac[:], WL, float(doff(t)), A.is_equal, A.mult, ["lac", "wl"], ["wf"])
         ts(T.posu[:, nv:np_], T.pa[:, nv:np_], -0.5, 320.0, A.mult, A.add, ["pa%d" % m for m in range(nv, np_)], ["posu_b"])
-        for b, bank in enumerate((0, 1, 3, 4)):
-            act(X[:, 2048 + b:2560:4], T["pb%d" % bank][:, 0:128], AF.Copy, [], [xk + "y%d" % b, "pb%d" % bank], scale=0.03125)
-        posk = ["posu_a", "posu_b"] + (["posu_c"] if np_ < 6 else [])
-        ts(T.pg[:, 0:96], T.o[:].indirect(T.posu[:, 0:6]), sm[:, 2:3], 1.0, A.subtract, A.min, posk + ["o_w", "o_r", "o_hi", "v"], ["pg"])
-        cp(pp[:, 8:14], T.posu[:, 0:6], posk, ["p2"])
-        tp(T.pgt[:], T.pg[:], ["pg", "pg_hi"], ["pgt"])
-        tt(pp[:, 24:30], pp[:, 16:22], pp[:, 8:14], A.add, ["p3", "p2"], ["p4"])
-        tt(T.sl[:], T.pgt[:].indirect(PK4U), TC, A.add, ["pgt", "pk4u", "tc"], ["sl"])
-        cp(T.posv[:, 0:6], pp[:, 24:30], ["p4"], ["pos2"])
-        tp(T.slt[:], T.sl[:], ["sl"], ["slt"])
-        ts(T.slu[:], T.slt[:], 2048.0, None, A.mult, None, ["slt"], ["slu"])
-        dbk = ["db%d" % b for b in range(4)] + ["db_z", "slu"]
-        act(X[:, 3328:3584], T.db[:].indirect(T.slu[:, 16:32]), AF.Copy, dbk, [xk + "s1"])
-        cp(X[:, 3072:3328], T.db[:].indirect(T.slu[:, 0:16]), dbk, [xk + "s0"])
-        sq, ss, lq, ls = T["sq%d" % t], T["ss%d" % t], T["lq%d" % t], T["ls%d" % t]
-        quant(sq[:], ss[:], X[:, 3072:3584], [xk + "s0", xk + "s1"], ["sq%d" % t])
-        send(lq[:].bitcast(dt.uint8), sq[:].bitcast(dt.uint8), "aq%d" % t, ["sq%d" % t])
-        send(ls[:], ss[:], "aq%d" % t, ["sq%d" % t])
-        arrival("aq%d" % t, 2, ["lq%d" % t])
-        ts(T.sva[:], T.kk[:], lcnt, 128.0, A.is_ge, A.mult, ["k16", "lcnt%d" % t], ["sv1"])
-        ts(T.nv[:], T.pg[:, 0:96], 5.0 + 2 * t, None, A.add, None, ["pg"], ["nv"])
-        tt(T.svb[:], T.sva[:], T.srcb[:], A.add, ["sv1", "srcb"], ["sv2"])
-        ts(T.o[:, 0:128], T.fr[:], LAB + 4.0 + 2 * t, None, A.add, None, ["fr"], ["o_w"])
-        cp(et[:].indirect(T.posv[:, 0:6]), T.svb[:], ["pos2", "sv2"], ["etab%da" % t, "etab%db" % t])
-        etk = ["etab%da" % t, "etab%db" % t, "rku"]
-        act(T.ea[:, 256:512], et[:].indirect(T.rku[:, 16:32]), AF.Copy, etk, ["e1b"])
-        cp(T.ea[:, 0:256], et[:].indirect(T.rku[:, 0:16]), etk, ["e1a"])
-        if t == R - 1:
-            labels()
-            act(T.lbo[:], T.vsrc[:].indirect(NATU), ID, ["vsrc", "natu", "off"], ["lbo"], bias=OFF)
-        tp(T.eat[:], T.ea[:], ["e1a", "e1b"], ["e1t"])
-        tt(T.el[:], T.eat[:].indirect(PKU), PAGEL, A.max, ["e1t", "pku", "pagel"], ["el"])
+        for b in range(4):
+            act(X[:, yo + b:yo + 512:4], T["pb%d" % b][:, 0:128], AF.Copy, [], [xk + "y%d" % b, "pb%d" % b], scale=0.03125)
+        tt(T.wb[:], T.wa[:], T.rk[:, 15:512:16], A.add, ["wa", "rk0", "rk1"], ["wb"])
+        ts(T.pg[:, 0:ns], T.o[:].indirect(T.posu[:, 0:np_]), W, 512.0, A.subtract, A.min, ["posu_a", "posu_b", "o", "o_hi", "w"], ["pg"])
+        tt(T.we[:], T.wf[:], T.jj[:], A.add, ["wf", "jj"], ["we"])
+        scan(T.ssc[:, 0:ns], T.pg[:, 0:ns], T.cq[:, 0:ns], -B4, A.max, A.add, ["pg", "cq"], ["ssc"])
+        tt(T.el[:], T.we[:], T.wb[:], A.max, ["we", "wb"], ["el"])
+        ts(T.slu[:, 0:ns // 4], T.ssc[:, 3:ns:4], TB4, 4.0, A.add, A.mult, ["ssc", "tb4"], ["slu"])
         if t == 0:
-            constants_3()
+            constants_4()
+        dbk = ["db%d" % b for b in range(4)] + ["dz%d" % t]
+        dwin = X[:, do:do + 2064]
+        act(T.st[:, 2 * ns:4 * ns], dwin.indirect(T.slu[:, ns // 8:ns // 4]), AF.Copy, dbk + ["slu"], ["st1"])
+        ts(T.elu[:, 0:32], T.el[:], 4.0, 0.0, A.mult, A.add, ["el"], ["elu0"])
+        cp(T.st[:, 0:2 * ns], dwin.indirect(T.slu[:, 0:ns // 8]), dbk + ["slu"], ["st0"])
+        ts(T.elu[:, 32:64], T.el[:], 4.0, 1.0, A.mult, A.add, ["el"], ["elu1"])
+        sq, ss = T.sq[:, 128 * t:128 * t + 128], T.ss[:, 128 * t:128 * t + 128]
+        quant(sq, ss, T.st[:], ["st0", "st1", "st_hi"], ["sq%d" % t])
+        send(lq[:, 0:ns].bitcast(dt.uint8), T.sq[:, 128 * t:128 * t + ns].bitcast(dt.uint8), "aq%d" % t, ["sq%d" % t])
+        send(ls[:, 0:ns], T.ss[:, 128 * t:128 * t + ns], "aq%d" % t, ["sq%d" % t])
+        arrival("aq%d" % t, 2, ["lq%d" % t])
+        for k in range(2, 4):
+            ts(T.elu[:, 32 * k:32 * k + 32], T.el[:], 4.0, float(k), A.mult, A.add, ["el"], ["elu%d" % k])
+        src = xkeys + dbk + [xk + "y%d" % b for b in range(4)]
+        xkeys = ["x%d_%d" % (t + 1, k) for k in range(4)]
+        ts(MN, cnt, lcnt, None, A.min, None, ["cnt%d" % t, "lcnt%d" % t], ["mn"])
+        tt(T.lab[:], T.lac[:], T.wf[:], A.max, ["lac", "wf"], ["lab"])
+        ts(T.ha[:, 0:ns // 4], T.kk[:, 0:ns // 4], MN, -4096.0, A.is_lt, A.mult, ["kk", "mn"], ["ha"])
+        for k in range(4):
+            move(MERGE[k], XN[:, k:2048:4], X[:].indirect(T.elu[:, 32 * k:32 * k + 32]), src + ["elu%d" % k], [xkeys[k]])
+        tt(T.hb[:, 0:ns // 4], T.ha[:, 0:ns // 4], T.dump[:, 0:ns // 4], A.add, ["ha", "dump"], ["hb"])
+        if t < R - 1:
+            tt(T.lj[:], T.lab[:], T.js[:], A.add, ["lab", "js"], ["lj"])
+        else:
+            ts(T.olu[:], T.lab[:], -8.0 * LAB, 0.125, A.add, A.mult, ["lab"], ["olu"])
+        tt(T.hc[:, 0:ns // 4], T.hb[:, 0:ns // 4], T.ssc[:, 3:ns:4], A.max, ["hb", "ssc"], ["hc"])
+        if t < R - 1:
+            ts(T.vlu[:], T.lj[:], 64.0, None, A.mult, None, ["lj"], ["vlu"])
+        ts(T.hlu[:, 0:ns // 4], T.hc[:, 0:ns // 4], TB4, 4.0, A.add, A.mult, ["hc", "tb4"], ["hlu"])
+        if t < R - 1:
+            ts(K2, RW, W, BIG, A.is_equal, A.mult, ["rw", "w"], ["k2"])
+            ts(K3, T.ea[:, 5 + 2 * t:6 + 2 * t], cnt, cf[:, 18 + t:19 + t], A.mult, A.add, ["ea", "cnt%d" % t, "c5%d" % t], ["k3"])
         if t == 1:
-            ts(NATU, NAT, C10, None, A.add, None, ["nat", "c10"], ["natu"])
             quant(T.vq[:], T.vs[:], T.vt[:], ["vt"], ["vq"])
         if t < R - 1:
-            keys(t, cnt)
-        tp(T.elt[:], T.el[:], ["el"], ["elt"])
-        for k in range(4):
-            ts(T.elu[:, 32 * k:32 * k + 32], T.elt[:], 4.0, float(k), A.mult, A.add, ["elt"], ["elu%d" % k])
-        layer((5, 6, 7, 2), lq[:], ls[:], ["lq%d" % t])
-        for b, bank in enumerate((5, 6, 7, 2)):
-            if b % 2:
-                act(X[:, 2560 + b:3072:4], T["pb%d" % bank][:, 0:128], AF.Copy, [], [xk + "h%d" % b, "pb%d" % bank], scale=0.03125)
+            ts(T.mkb[:], T.km[:], K2, K3, A.add, A.add, ["km", "k2", "k3"], ["mkb", "mkc"])
+        layer((4, 5, 6, 7), lq[:, 0:128], ls[:, 0:128], ["lq%d" % t, "lz%d" % t])
+        for b in range(4):
+            if b == 3:
+                act(T.hs[:, b:4 * ns:4], T["pb%d" % (4 + b)][:, 0:ns], AF.Copy, [], ["h%d" % b, "pb%d" % (4 + b)], scale=0.03125)
             else:
-                ts(X[:, 2560 + b:3072:4], T["pb%d" % bank][:, 0:128], 0.03125, None, A.mult, None, [], [xk + "h%d" % b, "pb%d" % bank])
-        src = xkeys + [xk + "s0", xk + "s1"] + [xk + c + str(b) for c in "yh" for b in range(4)]
-        xkeys = []
-        for k in range(4):
-            for e in range(2):
-                key = "x%d_%d%d" % (t + 1, k, e)
-                xkeys.append(key)
-                win = X[:].indirect(T.elu[:, 32 * k + 16 * e:32 * k + 16 * e + 16])
-                if e:
-                    act(XN[:, 4 * e + k:2048:8], win, AF.Copy, src + ["elu%d" % k], [key])
-                else:
-                    cp(XN[:, 4 * e + k:2048:8], win, src + ["elu%d" % k], [key])
+                ts(T.hs[:, b:4 * ns:4], T["pb%d" % (4 + b)][:, 0:ns], 0.03125, None, A.mult, None, [], ["h%d" % b, "pb%d" % (4 + b)])
+        cp(XN[:, 0:2432].indirect(T.hlu[:, 0:ns // 4]), T.hs[:, 0:4 * ns], ["hlu"] + ["h%d" % b for b in range(4)], xkeys)
+        if t < R - 1:
+            act(T.vsrc[:], T.tab[:].indirect(T.vlu[:]), AF.Copy, ["tab", "vlu"], ["vs0", "vs1"])
+        else:
+            act(T.obs[:], T.qq[:].indirect(T.olu[:]), AF.Copy, ["qq", "olu"], ["obs"])
+            dma("Y", T.ob[:], T.obs[0:128:16, :], ["obs"], ["out6"])
 
-    quant(T.xq[:], T.xsc[:], T.x3[:], xkeys, ["xq"])
+    quant(T.xq[:], T.xsc[:], T.x3[:, 0:2048], xkeys, ["xq"])
     for k in range(2):
         mm(k, 256, T.vq[:], T.vs[:], T.xq[:, 256 * k:256 * k + 256], T.xsc[:, 256 * k:256 * k + 256], ["vq", "xq"])
     dma("Y", T.oc[:], T.xq[:].bitcast(dt.uint8), ["xq"], ["out0"])
-    ms(sm[:, 11:12], -LAB, ["nlab"])
-    act(T.obs[:], T.lbo[:], ID, ["lbo", "nlab"], ["obs"], bias=sm[:, 11:12])
     cp(T.ys[:, 0:256], T.pb0[:, 0:256], [], ["ys0", "pb0"])
     act(T.ys[:, 256:512], T.pb1[:, 0:256], AF.Copy, [], ["ys1", "pb1"])
     dma("S", T.y[:], T.ys[:], ["ys0", "ys1"], ["out1"])
     for k in range(4):
         dma("Y", T.osc[4 * k:4 * k + 4, :], T.xsc[32 * k:32 * k + 4, :], ["xq"], ["out%d" % (2 + k)])
-    dma("Y", T.ob[:], T.obs[0:128:16, :], ["obs"], ["out6"])
     op("G", None, ["out%d" % k for k in range(7)], [], "sent", 0)
     emit(g, T, ops)
     g.wait_ge(T.sem.sent, 3 * R * out_n)

@@ -6,7 +6,9 @@ R = 3
 NPASS = (6, 5, 4)
 APASS = (3, 2, 2)
 M0 = 22
-MERGE = "SSVS"
+SPLIT = True
+LAG = 2
+MERGE = "SSSV"
 TW = (512, 448, 384, 384, 256, 192, 128, 128)
 TBASE = [sum(TW[:i]) for i in range(8)]
 CW = sum(TW)
@@ -15,6 +17,17 @@ HOLD, BP = 2048.0, 624.0
 B4 = 131072.0
 LAB = 138
 F32, BF, I32, U16, X4, U8 = "float32", "bfloat16", "int32", "uint16", "float8_e4m3fn_x4", "uint8"
+COLS = (([[0, 2], [1, 16]], 0),
+        ([[0, 2], [-1, 16]], int(15 - HOLD - BP)),
+        ([[0, 2], [1, 4], [0, 4]], 0),
+        ([[0, 8], [1, 4]], 0),
+        ([[1, 2], [0, 16]], 0),
+        ([[0, 2], [-1024, 16]], 1 - 1024 * LAB),
+        ([[0, 2], [-1024, 16]], 1 - 1024 * (LAB + 1)),
+        ([[0, 2], [512, 16]], 512 * LAB),
+        ([[0, 8], [1, 4]], int(4 * B4)),
+        ([[0, 2], [int(BIG) - 256, 4], [0, 4]], 512),
+        ([[0, 2], [2, 4], [0, 4]], 0))
 
 
 def yoff(t):
@@ -27,14 +40,14 @@ def doff(t):
 
 SCRATCH = {}
 for _d, _names in (
-        (BF, "ut512 vt512 kt512 gq512 qs512 one512 et2048 sg2048 sb8192 ds512 zer512 mk512 rst512 junka1536 junkb1536 junkc768 junkd256 "
+        (BF, "ut512 vt512 kt512 gq512 qs512 one528 et528 sg2048 sb8192 ds512 mk512 rst512 junka1536 junkb1536 junkc768 junkd256 "
              "lb384 fl384 kc384 tt512 st512 hs384"),
-        (X4, "uq128 vq128 upq128 wq512 xq512 kq128 eq512 tq128 sq384"),
-        (U8, "us128 vs128 ups128 wsc512 xsc512 ks128 es512 ts128 ss384"),
-        (F32, "pm512 sc512 cx512 rk512 rs32 rna32 vsrc512 o528 cq128 tsc128 ssc96 pg96 km64 kmt64 mkb64 sm16 pa8 tab4096 cf64 "
+        (X4, "uq128 vq128 upq128 wq512 xq512 kq128 eq512 tq128 sq384 lq368"),
+        (U8, "us128 vs128 ups128 wsc512 xsc512 ks128 es512 ts128 ss384 ls368"),
+        (F32, "pm512 sc512 cx512 rk512 rs32 rna32 vsrc512 o528 cq128 tsc128 ssc96 pg96 km64 kmt64 mkb64 mkc64 sm16 pa8 tab4096 cn352 cf352 cg16 "
               "qq32 ea32 eb32 ca16 cb8 cr32 jj32 js32 kk24 dump24 kcol16 wa32 wb32 wf32 we32 el32 lab32 lac32 lj32 ha24 hb24 hc24 obs512 ys512"),
         (U16, "rku32 posu8 tlu32 slu24 hlu24 elu128 vlu32 olu32 upu8 rfu32 tfu8"),
-        (I32, "ci16 ti32 tj32")):
+        (I32, "ti32 tj32")):
     for _s in _names.split():
         _n = _s.rstrip("0123456789")
         SCRATCH[_n] = ("sbuf", [128, int(_s[len(_n):])], _d)
@@ -43,7 +56,7 @@ SCRATCH["cc"] = ("sbuf", [128, CW], X4)
 SCRATCH["cs"] = ("sbuf", [128, CW], U8)
 SCRATCH["x3"] = ("sbuf", [128, 2432], BF)
 for _t in range(R):
-    for _n, _w, _d in (("x", 4 * (doff(_t) + 516), BF), ("lq", 224, X4), ("ls", 224, U8), ("cnt", 8, F32), ("lcnt", 8, F32)):
+    for _n, _w, _d in (("x", 4 * (doff(_t) + 516), BF), ("cnt", 8, F32), ("lcnt", 8, F32)):
         SCRATCH["%s%d" % (_n, _t)] = ("sbuf", [128, _w], _d)
 for _b in range(8):
     SCRATCH["pb%d" % _b] = ("psum", [128, 512], F32)
@@ -62,6 +75,8 @@ def emit(g, T, ops):
         need = []
         for k in o["r"]:
             need.append(writer[k])
+            if k[:2] == "pb":
+                need.extend(n for n in readers[k] if n[0] != QUEUE_SEM[q])
         for k in o["w"]:
             if k in writer:
                 need.append(writer[k])
@@ -121,7 +136,8 @@ def rank_program(g, core, T, topo):
     ndma = [0]
 
     def op(q, fn, r, w, sem=None, inc=0, chain=False):
-        ops.append({"q": q, "fn": fn, "r": list(r), "w": list(w), "sem": sem, "inc": inc, "chain": chain})
+        banks = [k for k in w if k[:2] == "pb" and q != "T"]
+        ops.append({"q": q, "fn": fn, "r": list(r) + banks, "w": [k for k in w if k not in banks], "sem": sem, "inc": inc, "chain": chain})
 
     def dma(q, out, in_, r, w):
         e = g.sync if q == "Y" else g.scalar
@@ -143,6 +159,9 @@ def rank_program(g, core, T, topo):
     def ms(ap, c, w, r=()):
         op("V", lambda: V.memset(ap, c), r, w)
 
+    def tp(out, a, r, w):
+        op("V", lambda: V.transpose(out, a), r, w)
+
     def scan(out, a, b, init, o0, o1, r, w):
         op("V", lambda: V.tensor_tensor_scan(out, a, b, init, o0, o1), r, w)
 
@@ -161,11 +180,11 @@ def rank_program(g, core, T, topo):
     def mm(bank, width, lq, lsc, rq, rsc, r, start=True, stop=True):
         op("T", lambda: PE.matmul_mx(T["pb%d" % bank][:, 0:width], lq, lsc, rq, rsc, start, stop), r, ["pb%d" % bank], chain=not start)
 
-    def iota(out, pat, base, cm, w, small=True):
-        if small:
-            op("G", lambda: g.iota(out, pat, base, cm, allow_small_or_imprecise_dtypes=True), [], w)
-        else:
-            op("G", lambda: g.iota(out, pat, base, cm), [], w)
+    def iota(out, pat, base, w):
+        op("G", lambda: g.iota(out, pat, base, 0, allow_small_or_imprecise_dtypes=True), [], w)
+
+    def select(out, in_, pat, cmp, base, cm, r, w):
+        op("G", lambda: g.affine_select(out, in_, pat, cmp, 0.0, base, cm), r, w)
 
     def send(out, in_, sem, r):
         op("G", lambda: g.remote_dma(out, in_, T.sem[sem], T.sem.sent, pid, rid, out_mask), r, [], "sent", 0)
@@ -179,107 +198,96 @@ def rank_program(g, core, T, topo):
 
     def unpack():
         for b in range(4):
-            mm(4 + b, 512, T.eq[:, 128 * b:128 * b + 128], T.es[:, 128 * b:128 * b + 128], T.xq[:], T.xsc[:], ["eq", "xq"])
+            mm(4 + b, 512, T.eq[:, 128 * b:128 * b + 128], T.es[:, 128 * b:128 * b + 128], T.xq[:], T.xsc[:], ["eq%d" % b, "xq0", "xq1"])
 
-    ci, cf, sm = T.ci, T.cf, T.sm
+    cf, cg, sm = T.cf, T.cg, T.sm
     ID = AF.Identity
     dma("Y", T.ut[:], T.u[:], [], ["ut"])
-    dma("S", T.x0[:, 0:1024], T.x[:, 0:1024], [], ["x0a"])
-    dma("Y", T.x0[:, 1024:2048], T.x[:, 1024:2048], [], ["x0b"])
-    dma("Y", T.wq[:].bitcast(dt.uint8), T.wc[:], ["x0b"], ["wq"])
+    dma("S", T.x0[:, 1024:2048], T.x[:, 1024:2048], [], ["x0b"])
+    dma("Y", T.x0[:, 0:1024], T.x[:, 0:1024], [], ["x0a"])
+    dma("Y", T.wq[:].bitcast(dt.uint8), T.wc[:], ["x0a"], ["wq"])
     dma("Y", T.wsc[:], T.ws[:], [], ["wsc"])
     dma("Y", T.vt[:], T.v[:], [], ["vt"])
 
-    RF, GF, R4, T4, HF, NA, NB, RW, TB4, KB0, KB1, CC0, CC1, K2R = (cf[:, i:i + 1] for i in range(14))
-    KEY, W, WL, MN, CA, CB, K2, K3 = (sm[:, i:i + 1] for i in range(8))
-    iota(ci[:, 8:9], [[0, 1]], 0, 1, ["ci_p"], False)
-    iota(T.qq[:], [[1, 32]], 0, 0, ["qq"])
-    iota(ci[:, 0:8], [[16, 8]], 0, 0, ["ci_u"], False)
-    iota(T.qs[:], [[0, 32], [1, 16]], 0, 0, ["qs"])
-    iota(T.gq[:], [[1, 8], [0, 64]], 0, 0, ["gq"])
-    iota(T.cr[:, 0:M0], [[16, M0]], 8 * (32 - M0), 0, ["cr_a"])
-    iota(T.cr[:, M0:32], [[0, 32 - M0]], 248, 0, ["cr_b"])
+    RF, CC0, R4, T4, HF, NA, NB, RW, TB4, KB0, K2R = (cf[:, 32 * i:32 * i + 1] for i in range(11))
+    CC1, KB1 = cg[:, 0:1], cg[:, 1:2]
+    KEY, W, WL, MN, CA, CB, K2, K3, K4, K5 = (sm[:, i:i + 1] for i in range(10))
+    for i in range(2):
+        iota(T.cn[:, 32 * i:32 * i + 32], COLS[i][0], COLS[i][1], ["cn%d" % i])
+    iota(T.qq[:], [[1, 32]], 0, ["qq"])
+    iota(T.qs[:], [[0, 32], [1, 16]], 0, ["qs"])
+    iota(T.cr[:, 0:M0], [[16, M0]], 8 * (32 - M0), ["cr_a"])
+    iota(T.cr[:, M0:32], [[0, 32 - M0]], 248, ["cr_b"])
     ms(T.one[:], 1.0, ["one"])
-    for b in range(4):
-        op("G", lambda b=b: g.affine_select(T.et[:, 512 * b:512 * b + 512], T.one[:], [[-1, 512]], A.is_equal, 0.0, b, 4), ["one"], ["et%d" % b])
-    iota(T.vsrc[:], [[640, 4], [1, 128]], 512 * LAB, 0, ["vs0", "vs1"])
-    iota(T.mkb[:], [[0, 2], [1, 2], [0, 16]], 0, 0, ["mkb0"])
-    iota(T.jj[:], [[16, 32]], 0, 0, ["jj0"])
-    iota(T.kk[:], [[8, 24]], 256, 0, ["kk0"])
-    iota(T.lab[:], [[8, 4], [0, 8]], 8 * LAB, 0, ["lab"])
-    iota(T.o[:, 512:528], [[0, 16]], 1000000, 0, ["o_hi"])
+    select(T.gq[:], T.one[:, 0:512], [[-16, 8], [0, 64]], A.is_ge, 0, 1, ["one"], ["gq"])
+    select(T.kt[:], T.gq[:], [[16, 8], [0, 64]], A.is_ge, 15, -1, ["gq"], ["kt"])
+    select(T.et[:], T.one[:], [[-1, 528]], A.is_equal, 3, 4, ["one"], ["et"])
+    for i in range(2, len(COLS)):
+        iota(T.cn[:, 32 * i:32 * i + 32], COLS[i][0], COLS[i][1], ["cn%d" % i])
+    iota(T.vsrc[:], [[640, 4], [1, 128]], 512 * LAB, ["vs0", "vs1"])
+    iota(T.mkc[:], [[0, 2], [1, 2], [0, 16]], 0, ["mk0"])
+    iota(T.jj[:], [[16, 32]], 0, ["jj0"])
+    iota(T.cb[:, 4:8], [[0, 4]], 0, ["cb_hi"])
+    iota(T.rs[:, 0:1], [[0, 1]], 0, ["rs0"])
+    iota(T.kk[:], [[8, 24]], 256, ["kk0"])
+    iota(T.lab[:], [[8, 4], [0, 8]], 8 * LAB, ["lab"])
+    iota(T.o[:, 512:528], [[0, 16]], 1000000, ["o_hi"])
     for t in range(R):
-        iota(T["x%d" % t][:, 4 * doff(t) + 2048:4 * doff(t) + 2064], [[0, 16]], 0, 0, ["dz%d" % t])
-    iota(T.st[:, 384:512], [[0, 128]], 0, 0, ["st_hi"])
+        iota(T["x%d" % t][:, 4 * doff(t) + 2048:4 * doff(t) + 2064], [[0, 16]], 0, ["dz%d" % t])
+    iota(T.st[:, 384:512], [[0, 128]], 0, ["st_hi"])
+    iota(T.tab[:, 0:3072], [[1, 3072]], 512 * LAB, ["tab0"])
 
-    ts(ci[:, 9:10], ci[:, 8:9], 15, None, A.bitwise_and, None, ["ci_p"], ["ci_r"])
-    ts(ci[:, 10:11], ci[:, 8:9], 4, None, A.logical_shift_right, None, ["ci_p"], ["ci_g"])
-    ts(ci[:, 11:12], ci[:, 8:9], 12, 2, A.bitwise_and, A.logical_shift_right, ["ci_p"], ["ci_4"])
-    ts(ci[:, 12:13], ci[:, 8:9], 3, None, A.bitwise_and, None, ["ci_p"], ["ci_t"])
-    ts(ci[:, 13:14], ci[:, 8:9], 16, 4, A.bitwise_and, A.logical_shift_right, ["ci_p"], ["ci_h"])
-    cp(T.upu[:], ci[:, 0:8], ["ci_u"], ["upu"])
-    cp(cf[:, 0:5], ci[:, 9:14], ["ci_r", "ci_g", "ci_4", "ci_t", "ci_h"], ["cols"])
-    for i in range(8):
+    def pad(i):
         lo = 16 * (29 - 4 * i)
         ms(T.ct[:, 4 * (TBASE[i] + lo):4 * (TBASE[i] + TW[i])], 0.0, ["c%d" % m for m in range(29 - 4 * i, 33 - 4 * i)])
-        if i == 0:
-            ts(T.ea[:], T.qq[:], RF, None, A.is_equal, None, ["qq", "cols"], ["ea"])
-            ts(T.rfu[:], T.qq[:], 0.0, RF, A.mult, A.add, ["qq", "cols"], ["rfu"])
-            act(T.mk[:], T.ea[:].indirect(T.rfu[:]), AF.Copy, ["ea", "rfu"], ["mk"], scale=2e29, bias=-1e29)
-            act(T.rst[:], T.qs[:], AF.Copy, ["qs"], ["rst"], scale=2e29, bias=-1e29)
-    quant(T.uq[:], T.us[:], T.ut[:], ["ut"], ["uq"])
-    ts(T.kt[:], T.gq[:], GF, None, A.is_equal, None, ["gq", "cols"], ["kt"])
-    cp(T.upq[:].bitcast(dt.uint32), T.uq[:].bitcast(dt.uint32).indirect(T.upu[:]), ["uq", "upu"], ["upq"])
-    act(T.ups[:], T.us[:].indirect(T.upu[:]), AF.Copy, ["uq", "upu"], ["ups"])
-    ms(T.rs[:, 0:1], 0.0, ["rs0"])
-    quant(T.kq[:], T.ks[:], T.kt[:], ["kt"], ["kq"])
 
-    def constants_1():
-        ts(T.ca[:], T.ea[:, 1:17], -2.0, None, A.mult, None, ["ea"], ["ca0"])
-        act(CC0, RF, AF.Copy, ["cols"], ["cc0"], scale=-1.0, bias=15.0 - HOLD - BP)
-        tt(T.ca[:], T.ca[:], T.ea[:, 0:16], A.add, ["ea", "ca0"], ["ca"])
-        act(CC1, T.ea[:, 15:16], ID, ["ea", "cc0"], ["cc1"], scale=HOLD, bias=CC0)
-        act(T.cx[:], T.ca[:].indirect(T.rfu[:]), AF.Copy, ["ca", "rfu"], ["cxu", "cxm", "cxl"], scale=HOLD)
-        act(T.cr[:], T.cr[:], ID, ["cr_a", "cr_b", "cc1"], ["cr"], bias=CC1)
+    tp(cf[:, 0:64], T.cn[:, 0:64], ["cn0", "cn1"], ["cols"])
+    pad(0)
+    ts(T.ea[:], T.qq[:], RF, None, A.is_equal, None, ["qq", "cols"], ["ea"])
+    cp(T.rfu[:], cf[:, 0:32], ["cols"], ["rfu"])
+    ts(T.ca[:], T.ea[:, 1:17], -2.0, None, A.mult, None, ["ea"], ["ca0"])
+    ts(T.upu[:], T.qq[:, 0:8], 16.0, None, A.mult, None, ["qq"], ["upu"])
+    tt(T.ca[:], T.ca[:], T.ea[:, 0:16], A.add, ["ea", "ca0"], ["ca"])
+    act(T.mk[:], T.ea[:].indirect(T.rfu[:]), AF.Copy, ["ea", "rfu"], ["mk"], scale=2e29, bias=-1e29)
+    act(T.rst[:], T.qs[:], AF.Copy, ["qs"], ["rst"], scale=2e29, bias=-1e29)
+    for i in (2, 3, 1, 4, 5, 6, 7):
+        pad(i)
+    quant(T.uq[:], T.us[:], T.ut[:], ["ut"], ["uq"])
+    act(T.ups[:], T.us[:].indirect(T.upu[:]), AF.Copy, ["uq", "upu"], ["ups"])
+    cp(T.upq[:].bitcast(dt.uint32), T.uq[:].bitcast(dt.uint32).indirect(T.upu[:]), ["uq", "upu"], ["upq"])
+    act(CC1, T.ea[:, 15:16], ID, ["ea", "cols"], ["cc1"], scale=HOLD, bias=CC0)
+    act(T.cx[:], T.ca[:].indirect(T.rfu[:]), AF.Copy, ["ca", "rfu"], ["cxu", "cxm", "cxl"], scale=HOLD)
+    act(T.cr[:], T.cr[:], ID, ["cr_a", "cr_b", "cc1"], ["cr"], bias=CC1)
 
     def constants_2():
-        ms(T.zer[:], 0.0, ["zer"])
-        ts(T.eb[:, 0:8], T.qq[:, 0:8], R4, None, A.is_equal, None, ["qq", "cols"], ["eb"])
-        ts(T.tfu[:], T.qq[:, 0:8], 0.0, T4, A.mult, A.add, ["qq", "cols"], ["tfu"])
-        ts(KB0, RF, 4.0, BIG - 256.0, A.is_ge, A.mult, ["cols"], ["kb0"])
+        tp(cf[:, 64:352], T.cn[:, 64:352], ["cn%d" % i for i in range(2, len(COLS))], ["col2"])
+        quant(T.lq[:, 240:368], T.ls[:, 240:368], T.x0[:, 0:512], ["x0a"], ["lz"])
+        ts(T.eb[:, 0:8], T.qq[:, 0:8], R4, None, A.is_equal, None, ["qq", "col2"], ["eb"])
+        cp(T.tfu[:], cf[:, 96:104], ["col2"], ["tfu"])
         ts(T.cb[:, 0:4], T.eb[:, 1:5], -2.0, None, A.mult, None, ["eb"], ["cb0"])
-        ts(KB1, RF, 1.0 / 256, 512.0 + LAB / 256.0, A.mult, A.add, ["cols"], ["kb1"])
-        ts(T.mkb[:], T.mkb[:], HF, 4 * BIG, A.not_equal, A.mult, ["mkb0", "cols"], ["mkb1"])
+        ts(T.mkc[:], T.mkc[:], HF, 4 * BIG, A.not_equal, A.mult, ["mk0", "col2"], ["mk1"])
         tt(T.cb[:, 0:4], T.cb[:, 0:4], T.eb[:, 0:4], A.add, ["eb", "cb0"], ["cb1"])
-        ts(NA, RF, -512.0, 0.5 - 512.0 * LAB, A.mult, A.add, ["cols"], ["na"])
-        ts(T.mkb[:, 0:32], T.mkb[:, 0:32], KB0, KB1, A.add, A.add, ["mkb1", "kb0", "kb1"], ["mkb"])
-        ts(T.mkb[:, 32:64], T.mkb[:, 32:64], KB0, 512.0, A.add, A.add, ["mkb1", "kb0"], ["mkc"])
-        ts(T.cb[:, 3:4], T.cb[:, 3:4], -2.0, None, A.add, None, ["cb1"], ["cb"])
-        ts(NB, RF, -512.0, 0.5 - 512.0 * (LAB + 1), A.mult, A.add, ["cols"], ["nb"])
-        for t in range(R):
-            k = 16 * NPASS[t]
-            quant(T["lq%d" % t][:, k:k + 128], T["ls%d" % t][:, k:k + 128], T.zer[:], ["zer"], ["lz%d" % t])
 
     def constants_3():
-        act(T.cq[:], T.cb[:].indirect(T.tfu[:]), AF.Copy, ["cb", "tfu", "cb_hi"], ["cq"], scale=B4)
+        act(T.cb[:, 3:4], T.cb[:, 3:4], AF.Copy, ["cb1"], ["cb"], bias=-2.0)
+        act(KB1, RW, ID, ["col2"], ["kb1"], scale=1.0 / 131072, bias=KB0)
         act(T.jj[:], T.jj[:], ID, ["jj0", "cols"], ["jj"], bias=RF)
-        act(K2R, R4, AF.Copy, ["cols"], ["k2r"], scale=2.0)
-        act(TB4, T4, AF.Copy, ["cols"], ["tb4"], scale=0.25, bias=B4)
+        act(T.cq[:], T.cb[:].indirect(T.tfu[:]), AF.Copy, ["cb", "tfu", "cb_hi"], ["cq"], scale=B4)
+        act(T.mkb[:, 0:32], T.mkc[:, 0:32], ID, ["mk1", "kb1"], ["mkb"], bias=KB1)
+        act(T.mkb[:, 32:64], T.mkc[:, 32:64], ID, ["mk1", "col2"], ["mkc"], bias=KB0)
         act(T.kcol[:, 8:14], T.jj[:, 0:6], AF.Copy, ["jj"], ["nk"], scale=-1.0, bias=-0.5)
 
     def constants_4():
-        act(T.kk[:], T.kk[:], ID, ["kk0", "k2r"], ["kk"], bias=K2R)
+        act(T.kk[:], T.kk[:], ID, ["kk0", "col2"], ["kk"], bias=K2R)
         act(T.js[:], T.jj[:], AF.Copy, ["jj"], ["js"], scale=1.0 / 64, bias=-8.0 * LAB)
-        act(RW, RF, AF.Copy, ["cols"], ["rw"], scale=512.0, bias=512.0 * LAB)
         act(T.dump[:], T.kk[:], AF.Copy, ["kk"], ["dump"], scale=0.5, bias=384.0 - B4)
-        for t in range(R - 1):
-            act(cf[:, 16 + t:17 + t], T.ea[:, 4 + 2 * t:5 + 2 * t], AF.Copy, ["ea"], ["c4%d" % t], scale=256.0 - BIG)
-        for t in range(R - 1):
-            act(cf[:, 18 + t:19 + t], T.ea[:, 5 + 2 * t:6 + 2 * t], ID, ["ea", "c4%d" % t], ["c5%d" % t], scale=-256.0 - BIG,
-                bias=cf[:, 16 + t:17 + t])
 
-    iota(T.cb[:, 4:8], [[0, 4]], 0, 0, ["cb_hi"])
-    iota(T.tab[:], [[1, 4096]], 512 * LAB, 0, ["tab"])
+    def constants_5():
+        for t in range(R - 1):
+            act(cg[:, 2 + t:3 + t], T.ea[:, 4 + 2 * t:5 + 2 * t], AF.Copy, ["ea"], ["c4%d" % t], scale=256.0 - BIG)
+        for t in range(R - 1):
+            act(cg[:, 4 + t:5 + t], T.ea[:, 5 + 2 * t:6 + 2 * t], ID, ["ea", "c4%d" % t], ["c5%d" % t], scale=-256.0 - BIG,
+                bias=cg[:, 2 + t:3 + t])
 
     def lane(m, lo, hi):
         i, k = (32 - m) // 4, (32 - m) % 4
@@ -313,49 +321,56 @@ def rank_program(g, core, T, topo):
         yo, do = 4 * yoff(t), 4 * doff(t)
         np_, na = NPASS[t], APASS[t]
         nv, ns = np_ - na, 16 * np_
-        cnt, lcnt, lq, ls = T["cnt%d" % t][:, 0:1], T["lcnt%d" % t][:, 0:1], T["lq%d" % t], T["ls%d" % t]
-        quant(T.xq[:], T.xsc[:], X[:, 0:2048], xkeys, ["xq"])
-        for bank in range(2):
-            mm(bank, 512, T.upq[:], T.ups[:], T.xq[:], T.xsc[:], ["upq", "ups", "xq"])
+        la = 16 * sum(NPASS[t + 1:])
+        cnt, lcnt, lq, ls = T["cnt%d" % t][:, 0:1], T["lcnt%d" % t][:, 0:1], T.lq, T.ls
+        quant(T.xq[:, 256:512], T.xsc[:, 256:512], X[:, 1024:2048], xkeys[-1:] if t == 0 else xkeys, ["xq1"])
+        mm(2, 256, T.upq[:], T.ups[:], T.xq[:, 256:512], T.xsc[:, 256:512], ["upq", "ups", "xq1"])
+        quant(T.xq[:, 0:256], T.xsc[:, 0:256], X[:, 0:1024], xkeys, ["xq0"])
+        ws = 16 * (M0 - 1)
+        mm(1, ws, T.upq[:], T.ups[:], T.xq[:, 0:ws], T.xsc[:, 0:ws], ["upq", "ups", "xq0", "xq1"])
+        mm(0, 512, T.upq[:], T.ups[:], T.xq[:], T.xsc[:], ["upq", "ups", "xq0", "xq1"])
         if t:
             unpack()
-        else:
-            constants_1()
-        for h in (1, 0):
-            lo = 256 * h
-            tt(T.pm[:, lo:lo + 256], T.pb0[:, lo:lo + 256], T.mk[:, lo:lo + 256], A.min, ["mk"], ["pm%d" % h, "pb0"])
-            if h == 0:
-                ts(lane(31, 0, 496), T.pb0[:, 0:496], pivot(31), 0.5, A.is_lt, A.subtract, ["sc1"], ["c31", "pb0"])
-            scan(T.sc[:, lo:lo + 256], T.rst[:, lo:lo + 256], T.pm[:, lo:lo + 256], 0.0, A.min, A.max, ["rst", "pm%d" % h], ["sc%d" % h])
+        tt(T.pm[:, 256:512], T.pb2[:, 0:256], T.mk[:, 256:512], A.min, ["mk"], ["pm1", "pb2"])
+        scan(T.sc[:, 256:512], T.rst[:, 256:512], T.pm[:, 256:512], 0.0, A.min, A.max, ["rst", "pm1"], ["sc1"])
+        if t == 0:
+            quant(T.kq[:], T.ks[:], T.kt[:], ["kt"], ["kq"])
+        tt(T.pm[:, 0:256], T.pb0[:, 0:256], T.mk[:, 0:256], A.min, ["mk"], ["pm0", "pb0"])
+        ts(lane(31, 0, 496), T.pb0[:, 0:496], pivot(31), 0.5, A.is_lt, A.subtract, ["sc1"], ["c31", "pb0"])
+        scan(T.sc[:, 0:256], T.rst[:, 0:256], T.pm[:, 0:256], 0.0, A.min, A.max, ["rst", "pm0"], ["sc0"])
 
         arows = list(range(M0 - 1, 0, -1))
-        for k in range(len(arows) + 1):
+        for k in range(len(arows) + LAG):
             if k < len(arows):
                 m = arows[k]
                 act(T.sg[:, 512 * (k % 4):512 * (k % 4) + 16 * m], T.pb1[:, 0:16 * m], AF.Sign, ["sc%d" % (m // 16)],
                     ["sg%d" % (k % 4), "pb1"], bias=pivot(m), scale=-1.0)
-            if k:
-                m = arows[k - 1]
-                act(lane(m, 0, 16 * m), T.sg[:, 512 * ((k - 1) % 4):512 * ((k - 1) % 4) + 16 * m], AF.Relu, ["sg%d" % ((k - 1) % 4)],
+            j = k - LAG
+            if j >= 0:
+                m = arows[j]
+                act(lane(m, 0, 16 * m), T.sg[:, 512 * (j % 4):512 * (j % 4) + 16 * m], AF.Relu, ["sg%d" % (j % 4)],
                     ["c%d" % m, "rs%d" % m], accum_out=T.rs[:, m:m + 1])
+        ts(lane(30, 0, 480), T.pb0[:, 0:480], pivot(30), 0.5, A.is_lt, A.subtract, ["sc1"], ["c30", "pb0"])
         tt(lane(32, 0, 512), T.pb0[:], T.sc[:], A.is_le, ["sc0", "sc1"], ["c32", "pb0"])
         for m in range(31, M0 - 1, -1):
-            if m > M0:
-                ts(lane(m - 1, 0, 16 * m - 16), T.pb0[:, 0:16 * m - 16], pivot(m - 1), 0.5, A.is_lt, A.subtract, ["sc1"], ["c%d" % (m - 1), "pb0"])
+            if m - 2 >= M0:
+                ts(lane(m - 2, 0, 16 * m - 32), T.pb0[:, 0:16 * m - 32], pivot(m - 2), 0.5, A.is_lt, A.subtract, ["sc1"], ["c%d" % (m - 2), "pb0"])
             if m == 31:
                 scan(T.ds[:], T.qs[:], lane(32, 0, 512), 0.0, A.min, A.add, ["qs", "c32"], ["ds"])
             e = 256 * (m + 1)
             scan(T.sb[:, e - 8 * m:e], lane(m, 0, 8 * m), lane(m, 8 * m, 16 * m), 0.0, A.add, A.add, ["c%d" % m], ["sb%d" % m])
             if m == 30:
                 tt(T.rna[:], T.cr[:], T.ds[:, 15:512:16], A.subtract, ["cr", "ds"], ["rna"])
-            if m % 4 == 1:
-                tile((29 - m) // 4)
-        tt(T.cx[:, 16 * M0 + 15:512:16], T.rna[:, M0:32], T.sb[:, 256 * M0 + 255:8192:256], A.subtract,
-           ["rna"] + ["sb%d" % m for m in range(M0, 32)], ["cxu"])
-        if t == 0:
-            quant(T.eq[:], T.es[:], T.et[:], ["et%d" % b for b in range(4)], ["eq"])
-        for i in range((32 - M0 + 1) // 4, 4):
+            if m % 4 == 2 and m - 1 >= M0:
+                tile((30 - m) // 4)
+        for i in range((33 - M0) // 4, 4):
+            if i == 3 and t == 0:
+                for b in range(4):
+                    quant(T.eq[:, 128 * b:128 * b + 128], T.es[:, 128 * b:128 * b + 128], T.et[:, 3 - b:515 - b], ["et"], ["eq%d" % b])
             tile(i)
+            if i == 2:
+                tt(T.cx[:, 16 * M0 + 15:512:16], T.rna[:, M0:32], T.sb[:, 256 * M0 + 255:8192:256], A.subtract,
+                   ["rna"] + ["sb%d" % m for m in range(M0, 32)], ["cxu"])
         if t == 0:
             unpack()
             constants_2()
@@ -372,71 +387,80 @@ def rank_program(g, core, T, topo):
             act(X[:, do + b:do + 2048:4], T["pb%d" % (4 + b)][:], AF.Copy, [], ["db%d" % b, "pb%d" % (4 + b)])
         places(0)
         sort(0)
-        act(T.junkd[:, 0:128], T.o[:, 0:128], AF.Sign, ["o", "na"], ["jd0", "ca_"], bias=NA, accum_out=CA)
-        act(T.junkd[:, 128:256], T.o[:, 0:128], AF.Sign, ["o", "nb"], ["jd1", "cb_"], bias=NB, accum_out=CB)
+        act(T.junkd[:, 0:128], T.o[:, 0:128], AF.Sign, ["o", "col2"], ["jd0", "ca_"], scale=2.0, bias=NA, accum_out=CA)
+        act(T.junkd[:, 128:256], T.o[:, 0:128], AF.Sign, ["o", "col2"], ["jd1", "cb_"], scale=2.0, bias=NB, accum_out=CB)
         act(T.lb[:], T.o[:, 128:512], AF.Copy, ["o"], ["lb"], scale=1.0 / 131072, bias=(1.0 / 1024 - 0.5) / 256)
+        ts(T.wa[:], T.rku[:], 128.0, 8.0 * (LAB + 4 + 2 * t), A.is_lt, A.mult, ["rku0", "rku1"], ["wa"])
         scan(T.tsc[:], T.o[:, 0:128], T.cq[:], -B4, A.max, A.add, ["o", "cq"], ["tsc"])
-        rkk = ["rku0", "rku1"]
-        ts(T.wa[:], T.rku[:], 128.0, 8.0 * (LAB + 4 + 2 * t), A.is_lt, A.mult, rkk, ["wa"])
+        tt(T.lac[:], T.lab[:], T.wa[:], A.max, ["lab", "wa"], ["lac"])
         ts(T.ti[:], T.tsc[:, 3:128:4], B4, None, A.add, None, ["tsc"], ["ti"])
         ts(T.km[:], T.mkb[:], CA, CB, A.subtract, A.add, ["mkb", "mkc", "ca_", "cb_"], ["km"])
         ts(T.tj[:], T.ti[:], 511, None, A.bitwise_and, None, ["ti"], ["tj"])
-        op("V", lambda: V.transpose(T.kmt[:], T.km[:]), ["km"], ["kmt"])
-        ts(T.tlu[:], T.tj[:], 4.0, T4, A.mult, A.add, ["tj", "cols"], ["tlu"])
+        tp(T.kmt[:], T.km[:], ["km"], ["kmt"])
+        ts(T.tlu[:], T.tj[:], 4.0, T4, A.mult, A.add, ["tj", "col2"], ["tlu"])
         act(T.tt[:], X[:, 0:2048].indirect(T.tlu[:]), AF.Copy, xkeys + ["tlu"], ["tt"])
         op("V", lambda: V.tensor_reduce(KEY, T.kmt[:, 0:32], AxisListType.X, A.min), ["kmt"], ["key"])
         op("V", lambda cnt=cnt: V.tensor_reduce(cnt, T.kmt[:, 32:64], AxisListType.X, A.min), ["kmt"], ["cnt%d" % t])
         send(lcnt, cnt, "ac%d" % t, ["cnt%d" % t])
         arrival("ac%d" % t, 1, ["lcnt%d" % t])
         vk = ["key", "cnt%d" % t]
-        tt(T.lac[:], T.lab[:], T.wa[:], A.max, ["lab", "wa"], ["lac"])
+        tt(T.wb[:], T.wa[:], T.rk[:, 15:512:16], A.add, ["wa", "rk0", "rk1"], ["wb"])
         ts(T.fl[:], T.lb[:], cnt, KEY, A.add, A.is_equal, ["lb"] + vk, ["fl"])
         ts(WL, KEY, cnt, 2048.0, A.subtract, A.mult, vk, ["wl"])
-        scan(T.kc[:], T.fl[:], T.zer[:, 0:384], 0.0, A.add, A.add, ["fl", "zer"], ["kc"])
+        scan(T.kc[:], T.fl[:], T.fl[:], 0.0, A.add, A.max, ["fl"], ["kc"])
         ts(W, KEY, cnt, 131072.0, A.subtract, A.mult, vk, ["w"])
         for m in range(nv, np_):
             act(T.junka[:, 384 * (m - nv):384 * (m - nv + 1)], T.kc[:], AF.Sign, ["kc", "nk"], ["junk%d" % (m - nv), "pa%d" % m],
                 bias=T.kcol[:, 8 + m:9 + m], accum_out=T.pa[:, m:m + 1])
         for m in range(nv):
             ts(T.junkb[:, 384 * m:384 * m + 384], T.kc[:], T.jj[:, m:m + 1], 0.5, A.is_gt, A.subtract, ["kc", "jj"], ["j2%d" % m])
+            if m == 0:
+                quant(T.tq[:], T.ts[:], T.tt[:], ["tt"], ["tq"])
+                layer((0, 1, 2, 3), T.tq[:], T.ts[:], ["tq"])
         for m in range(nv):
             scan(T.junkc[:, 192 * m:192 * m + 192], T.junkb[:, 384 * m:384 * m + 192], T.junkb[:, 384 * m + 192:384 * m + 384], 0.0, A.add, A.add,
                  ["j2%d" % m], ["j3%d" % m])
-        quant(T.tq[:], T.ts[:], T.tt[:], ["tt"], ["tq"])
-        layer((0, 1, 2, 3), T.tq[:], T.ts[:], ["tq"])
-        ts(T.posu[:, 0:nv], T.junkc[:, 191:192 * nv:192], -1.0, 320.0, A.mult, A.add, ["j3%d" % m for m in range(nv)], ["posu_a"])
         ts(T.wf[:], T.lac[:], WL, float(doff(t)), A.is_equal, A.mult, ["lac", "wl"], ["wf"])
+        ts(T.posu[:, 0:nv], T.junkc[:, 191:192 * nv:192], -1.0, 320.0, A.mult, A.add, ["j3%d" % m for m in range(nv)], ["posu_a"])
         ts(T.posu[:, nv:np_], T.pa[:, nv:np_], -0.5, 320.0, A.mult, A.add, ["pa%d" % m for m in range(nv, np_)], ["posu_b"])
         for b in range(4):
             act(X[:, yo + b:yo + 512:4], T["pb%d" % b][:, 0:128], AF.Copy, [], [xk + "y%d" % b, "pb%d" % b], scale=0.03125)
-        tt(T.wb[:], T.wa[:], T.rk[:, 15:512:16], A.add, ["wa", "rk0", "rk1"], ["wb"])
-        ts(T.pg[:, 0:ns], T.o[:].indirect(T.posu[:, 0:np_]), W, 512.0, A.subtract, A.min, ["posu_a", "posu_b", "o", "o_hi", "w"], ["pg"])
         tt(T.we[:], T.wf[:], T.jj[:], A.add, ["wf", "jj"], ["we"])
-        scan(T.ssc[:, 0:ns], T.pg[:, 0:ns], T.cq[:, 0:ns], -B4, A.max, A.add, ["pg", "cq"], ["ssc"])
+        ts(T.pg[:, 0:ns], T.o[:].indirect(T.posu[:, 0:np_]), W, 512.0, A.subtract, A.min, ["posu_a", "posu_b", "o", "o_hi", "w"], ["pg"])
         tt(T.el[:], T.we[:], T.wb[:], A.max, ["we", "wb"], ["el"])
-        ts(T.slu[:, 0:ns // 4], T.ssc[:, 3:ns:4], TB4, 4.0, A.add, A.mult, ["ssc", "tb4"], ["slu"])
+        scan(T.ssc[:, 0:ns], T.pg[:, 0:ns], T.cq[:, 0:ns], -B4, A.max, A.add, ["pg", "cq"], ["ssc"])
+        ts(T.elu[:, 0:32], T.el[:], 4.0, 0.0, A.mult, A.add, ["el"], ["elu0"])
+        ts(T.slu[:, 0:ns // 4], T.ssc[:, 3:ns:4], 4.0, TB4, A.mult, A.add, ["ssc", "col2"], ["slu"])
         if t == 0:
             constants_4()
         dbk = ["db%d" % b for b in range(4)] + ["dz%d" % t]
         dwin = X[:, do:do + 2064]
-        act(T.st[:, 2 * ns:4 * ns], dwin.indirect(T.slu[:, ns // 8:ns // 4]), AF.Copy, dbk + ["slu"], ["st1"])
-        ts(T.elu[:, 0:32], T.el[:], 4.0, 0.0, A.mult, A.add, ["el"], ["elu0"])
-        cp(T.st[:, 0:2 * ns], dwin.indirect(T.slu[:, 0:ns // 8]), dbk + ["slu"], ["st0"])
-        ts(T.elu[:, 32:64], T.el[:], 4.0, 1.0, A.mult, A.add, ["el"], ["elu1"])
-        sq, ss = T.sq[:, 128 * t:128 * t + 128], T.ss[:, 128 * t:128 * t + 128]
-        quant(sq, ss, T.st[:], ["st0", "st1", "st_hi"], ["sq%d" % t])
-        send(lq[:, 0:ns].bitcast(dt.uint8), T.sq[:, 128 * t:128 * t + ns].bitcast(dt.uint8), "aq%d" % t, ["sq%d" % t])
-        send(ls[:, 0:ns], T.ss[:, 128 * t:128 * t + ns], "aq%d" % t, ["sq%d" % t])
-        arrival("aq%d" % t, 2, ["lq%d" % t])
-        for k in range(2, 4):
-            ts(T.elu[:, 32 * k:32 * k + 32], T.el[:], 4.0, float(k), A.mult, A.add, ["el"], ["elu%d" % k])
         src = xkeys + dbk + [xk + "y%d" % b for b in range(4)]
         xkeys = ["x%d_%d" % (t + 1, k) for k in range(4)]
+
+        def merge(k):
+            move(MERGE[k], XN[:, k:2048:4], X[:].indirect(T.elu[:, 32 * k:32 * k + 32]), src + ["elu%d" % k], [xkeys[k]])
+
+        cut = ns // 8 if SPLIT else ns // 4
+        if SPLIT:
+            act(T.st[:, 2 * ns:4 * ns], dwin.indirect(T.slu[:, cut:ns // 4]), AF.Copy, dbk + ["slu"], ["st1"])
+        merge(0)
+        ts(T.elu[:, 32:64], T.el[:], 4.0, 1.0, A.mult, A.add, ["el"], ["elu1"])
+        cp(T.st[:, 0:16 * cut], dwin.indirect(T.slu[:, 0:cut]), dbk + ["slu"], ["st0"])
+        ts(T.elu[:, 64:96], T.el[:], 4.0, 2.0, A.mult, A.add, ["el"], ["elu2"])
+        sq, ss = T.sq[:, 128 * t:128 * t + 128], T.ss[:, 128 * t:128 * t + 128]
+        quant(sq, ss, T.st[:], ["st0", "st_hi"] + (["st1"] if SPLIT else []), ["sq%d" % t])
+        send(lq[:, la:la + ns].bitcast(dt.uint8), T.sq[:, 128 * t:128 * t + ns].bitcast(dt.uint8), "aq%d" % t, ["sq%d" % t])
+        send(ls[:, la:la + ns], T.ss[:, 128 * t:128 * t + ns], "aq%d" % t, ["sq%d" % t])
+        arrival("aq%d" % t, 2, ["lq%d" % t])
+        if t == 0:
+            iota(T.tab[:, 3072:4096], [[1, 1024]], 512 * (LAB + 6), ["tab1"])
+        ts(T.elu[:, 96:128], T.el[:], 4.0, 3.0, A.mult, A.add, ["el"], ["elu3"])
         ts(MN, cnt, lcnt, None, A.min, None, ["cnt%d" % t, "lcnt%d" % t], ["mn"])
         tt(T.lab[:], T.lac[:], T.wf[:], A.max, ["lac", "wf"], ["lab"])
         ts(T.ha[:, 0:ns // 4], T.kk[:, 0:ns // 4], MN, -4096.0, A.is_lt, A.mult, ["kk", "mn"], ["ha"])
-        for k in range(4):
-            move(MERGE[k], XN[:, k:2048:4], X[:].indirect(T.elu[:, 32 * k:32 * k + 32]), src + ["elu%d" % k], [xkeys[k]])
+        for k in range(1, 4):
+            merge(k)
         tt(T.hb[:, 0:ns // 4], T.ha[:, 0:ns // 4], T.dump[:, 0:ns // 4], A.add, ["ha", "dump"], ["hb"])
         if t < R - 1:
             tt(T.lj[:], T.lab[:], T.js[:], A.add, ["lab", "js"], ["lj"])
@@ -445,36 +469,40 @@ def rank_program(g, core, T, topo):
         tt(T.hc[:, 0:ns // 4], T.hb[:, 0:ns // 4], T.ssc[:, 3:ns:4], A.max, ["hb", "ssc"], ["hc"])
         if t < R - 1:
             ts(T.vlu[:], T.lj[:], 64.0, None, A.mult, None, ["lj"], ["vlu"])
-        ts(T.hlu[:, 0:ns // 4], T.hc[:, 0:ns // 4], TB4, 4.0, A.add, A.mult, ["hc", "tb4"], ["hlu"])
-        if t < R - 1:
-            ts(K2, RW, W, BIG, A.is_equal, A.mult, ["rw", "w"], ["k2"])
-            ts(K3, T.ea[:, 5 + 2 * t:6 + 2 * t], cnt, cf[:, 18 + t:19 + t], A.mult, A.add, ["ea", "cnt%d" % t, "c5%d" % t], ["k3"])
+        ts(T.hlu[:, 0:ns // 4], T.hc[:, 0:ns // 4], 4.0, TB4, A.mult, A.add, ["hc", "col2"], ["hlu"])
         if t == 1:
             quant(T.vq[:], T.vs[:], T.vt[:], ["vt"], ["vq"])
-        if t < R - 1:
-            ts(T.mkb[:], T.km[:], K2, K3, A.add, A.add, ["km", "k2", "k3"], ["mkb", "mkc"])
-        layer((4, 5, 6, 7), lq[:, 0:128], ls[:, 0:128], ["lq%d" % t, "lz%d" % t])
+        layer((4, 5, 6, 7), lq[:, la:la + 128], ls[:, la:la + 128], ["lq%d" % t, "lz"])
         for b in range(4):
             if b == 3:
                 act(T.hs[:, b:4 * ns:4], T["pb%d" % (4 + b)][:, 0:ns], AF.Copy, [], ["h%d" % b, "pb%d" % (4 + b)], scale=0.03125)
             else:
                 ts(T.hs[:, b:4 * ns:4], T["pb%d" % (4 + b)][:, 0:ns], 0.03125, None, A.mult, None, [], ["h%d" % b, "pb%d" % (4 + b)])
         cp(XN[:, 0:2432].indirect(T.hlu[:, 0:ns // 4]), T.hs[:, 0:4 * ns], ["hlu"] + ["h%d" % b for b in range(4)], xkeys)
+        if t == 0:
+            constants_5()
         if t < R - 1:
-            act(T.vsrc[:], T.tab[:].indirect(T.vlu[:]), AF.Copy, ["tab", "vlu"], ["vs0", "vs1"])
+            act(T.vsrc[:], T.tab[:, 0:3072 + 1024 * t].indirect(T.vlu[:]), AF.Copy, ["tab0", "vlu"] + ["tab1"] * t, ["vs0", "vs1"])
+            act(K2, RW, AF.Abs, ["col2", "w"], ["k2"], scale=-1.0, bias=W)
+            act(K3, cnt, ID, ["ea", "cnt%d" % t, "c5%d" % t], ["k3"], scale=T.ea[:, 5 + 2 * t:6 + 2 * t], bias=cg[:, 4 + t:5 + t])
+            act(K4, K2, AF.Relu, ["k2"], ["k4"], scale=-BIG, bias=BIG)
+            act(K5, K4, ID, ["k4", "k3"], ["k5"], bias=K3)
+            act(T.mkb[:], T.km[:], ID, ["km", "k5"], ["mkb", "mkc"], bias=K5)
         else:
             act(T.obs[:], T.qq[:].indirect(T.olu[:]), AF.Copy, ["qq", "olu"], ["obs"])
             dma("Y", T.ob[:], T.obs[0:128:16, :], ["obs"], ["out6"])
 
-    quant(T.xq[:], T.xsc[:], T.x3[:, 0:2048], xkeys, ["xq"])
     for k in range(2):
-        mm(k, 256, T.vq[:], T.vs[:], T.xq[:, 256 * k:256 * k + 256], T.xsc[:, 256 * k:256 * k + 256], ["vq", "xq"])
-    dma("Y", T.oc[:], T.xq[:].bitcast(dt.uint8), ["xq"], ["out0"])
-    cp(T.ys[:, 0:256], T.pb0[:, 0:256], [], ["ys0", "pb0"])
-    act(T.ys[:, 256:512], T.pb1[:, 0:256], AF.Copy, [], ["ys1", "pb1"])
-    dma("S", T.y[:], T.ys[:], ["ys0", "ys1"], ["out1"])
+        lo = 256 * k
+        quant(T.xq[:, lo:lo + 256], T.xsc[:, lo:lo + 256], T.x3[:, 4 * lo:4 * lo + 1024], xkeys, ["xq%d" % k])
+        mm(k, 256, T.vq[:], T.vs[:], T.xq[:, lo:lo + 256], T.xsc[:, lo:lo + 256], ["vq", "xq%d" % k])
+    act(T.ys[:, 0:256], T.pb0[:, 0:256], AF.Copy, [], ["ys0", "pb0"])
+    dma("S", T.y[:, 0:256], T.ys[:, 0:256], ["ys0"], ["out1"])
+    cp(T.ys[:, 256:512], T.pb1[:, 0:256], [], ["ys1", "pb1"])
+    dma("Y", T.oc[:], T.xq[:].bitcast(dt.uint8), ["xq0", "xq1"], ["out0"])
     for k in range(4):
-        dma("Y", T.osc[4 * k:4 * k + 4, :], T.xsc[32 * k:32 * k + 4, :], ["xq"], ["out%d" % (2 + k)])
-    op("G", None, ["out%d" % k for k in range(7)], [], "sent", 0)
+        dma("Y", T.osc[4 * k:4 * k + 4, :], T.xsc[32 * k:32 * k + 4, :], ["xq0", "xq1"], ["out%d" % (2 + k)])
+    dma("S", T.y[:, 256:512], T.ys[:, 256:512], ["ys1"], ["out7"])
+    op("G", None, ["out%d" % k for k in range(8)], [], "sent", 0)
     emit(g, T, ops)
     g.wait_ge(T.sem.sent, 3 * R * out_n)

@@ -5,10 +5,11 @@ AF = ActivationFunctionType
 R = 3
 NPASS = (6, 5, 4)
 APASS = (3, 2, 2)
-M0 = 22
+M0 = 21
 SPLIT = True
 LAG = 2
 MERGE = "SSSV"
+TAIL = "q4 q5 p1 q6 o1 c0 q7 s47 p0 s78 o0 s04"
 TW = (512, 448, 384, 384, 256, 192, 128, 128)
 TBASE = [sum(TW[:i]) for i in range(8)]
 CW = sum(TW)
@@ -26,8 +27,7 @@ COLS = (([[0, 2], [1, 16]], 0),
         ([[0, 2], [-1024, 16]], 1 - 1024 * (LAB + 1)),
         ([[0, 2], [512, 16]], 512 * LAB),
         ([[0, 8], [1, 4]], int(4 * B4)),
-        ([[0, 2], [int(BIG) - 256, 4], [0, 4]], 512),
-        ([[0, 2], [2, 4], [0, 4]], 0))
+        ([[0, 2], [int(BIG) - 256, 4], [0, 4]], 512))
 
 
 def yoff(t):
@@ -44,8 +44,9 @@ for _d, _names in (
              "lb384 fl384 kc384 tt512 st512 hs384"),
         (X4, "uq128 vq128 upq128 wq512 xq512 kq128 eq512 tq128 sq384 lq368"),
         (U8, "us128 vs128 ups128 wsc512 xsc512 ks128 es512 ts128 ss384 ls368"),
-        (F32, "pm512 sc512 cx512 rk512 rs32 rna32 vsrc512 o528 cq128 tsc128 ssc96 pg96 km64 kmt64 mkb64 mkc64 sm16 pa8 tab4096 cn352 cf352 cg16 "
-              "qq32 ea32 eb32 ca16 cb8 cr32 jj32 js32 kk24 dump24 kcol16 wa32 wb32 wf32 we32 el32 lab32 lac32 lj32 ha24 hb24 hc24 obs512 ys512"),
+        (F32, "pm512 sc512 cx512 rk512 rs32 rna32 vsrc512 o528 cq128 tsc128 ssc96 pg96 km64 kmt64 mkb64 mkc64 sm16 pa8 tab4096 cn320 cf320 cg16 "
+              "qq32 ea32 eb32 ca16 cb8 cr32 jj32 js32 kk8 dump8 kcol16 wa32 wb32 wf32 we32 el32 lab32 lac32 lj32 ha8 hb8 hc8 obs512 ys512 "
+              "ch96 hsc96"),
         (U16, "rku32 posu8 tlu32 slu24 hlu24 elu128 vlu32 olu32 upu8 rfu32 tfu8"),
         (I32, "ti32 tj32")):
     for _s in _names.split():
@@ -209,19 +210,19 @@ def rank_program(g, core, T, topo):
     dma("Y", T.wsc[:], T.ws[:], [], ["wsc"])
     dma("Y", T.vt[:], T.v[:], [], ["vt"])
 
-    RF, CC0, R4, T4, HF, NA, NB, RW, TB4, KB0, K2R = (cf[:, 32 * i:32 * i + 1] for i in range(11))
+    RF, CC0, R4, T4, HF, NA, NB, RW, TB4, KB0 = (cf[:, 32 * i:32 * i + 1] for i in range(10))
     CC1, KB1 = cg[:, 0:1], cg[:, 1:2]
     KEY, W, WL, MN, CA, CB, K2, K3, K4, K5 = (sm[:, i:i + 1] for i in range(10))
     for i in range(2):
         iota(T.cn[:, 32 * i:32 * i + 32], COLS[i][0], COLS[i][1], ["cn%d" % i])
     iota(T.qq[:], [[1, 32]], 0, ["qq"])
+    ms(T.one[:], 1.0, ["one"])
+    select(T.et[:], T.one[:], [[-1, 528]], A.is_equal, 3, 4, ["one"], ["et"])
     iota(T.qs[:], [[0, 32], [1, 16]], 0, ["qs"])
+    select(T.gq[:], T.one[:, 0:512], [[-16, 8], [0, 64]], A.is_ge, 0, 1, ["one"], ["gq"])
     iota(T.cr[:, 0:M0], [[16, M0]], 8 * (32 - M0), ["cr_a"])
     iota(T.cr[:, M0:32], [[0, 32 - M0]], 248, ["cr_b"])
-    ms(T.one[:], 1.0, ["one"])
-    select(T.gq[:], T.one[:, 0:512], [[-16, 8], [0, 64]], A.is_ge, 0, 1, ["one"], ["gq"])
     select(T.kt[:], T.gq[:], [[16, 8], [0, 64]], A.is_ge, 15, -1, ["gq"], ["kt"])
-    select(T.et[:], T.one[:], [[-1, 528]], A.is_equal, 3, 4, ["one"], ["et"])
     for i in range(2, len(COLS)):
         iota(T.cn[:, 32 * i:32 * i + 32], COLS[i][0], COLS[i][1], ["cn%d" % i])
     iota(T.vsrc[:], [[640, 4], [1, 128]], 512 * LAB, ["vs0", "vs1"])
@@ -229,7 +230,6 @@ def rank_program(g, core, T, topo):
     iota(T.jj[:], [[16, 32]], 0, ["jj0"])
     iota(T.cb[:, 4:8], [[0, 4]], 0, ["cb_hi"])
     iota(T.rs[:, 0:1], [[0, 1]], 0, ["rs0"])
-    iota(T.kk[:], [[8, 24]], 256, ["kk0"])
     iota(T.lab[:], [[8, 4], [0, 8]], 8 * LAB, ["lab"])
     iota(T.o[:, 512:528], [[0, 16]], 1000000, ["o_hi"])
     for t in range(R):
@@ -249,38 +249,43 @@ def rank_program(g, core, T, topo):
     ts(T.upu[:], T.qq[:, 0:8], 16.0, None, A.mult, None, ["qq"], ["upu"])
     tt(T.ca[:], T.ca[:], T.ea[:, 0:16], A.add, ["ea", "ca0"], ["ca"])
     act(T.mk[:], T.ea[:].indirect(T.rfu[:]), AF.Copy, ["ea", "rfu"], ["mk"], scale=2e29, bias=-1e29)
-    act(T.rst[:], T.qs[:], AF.Copy, ["qs"], ["rst"], scale=2e29, bias=-1e29)
-    for i in (2, 3, 1, 4, 5, 6, 7):
+    for i in (2, 3, 1, 4):
         pad(i)
     quant(T.uq[:], T.us[:], T.ut[:], ["ut"], ["uq"])
+    for i in (5, 6, 7):
+        pad(i)
     act(T.ups[:], T.us[:].indirect(T.upu[:]), AF.Copy, ["uq", "upu"], ["ups"])
+    act(T.rst[:], T.qs[:], AF.Copy, ["qs"], ["rst"], scale=2e29, bias=-1e29)
     cp(T.upq[:].bitcast(dt.uint32), T.uq[:].bitcast(dt.uint32).indirect(T.upu[:]), ["uq", "upu"], ["upq"])
     act(CC1, T.ea[:, 15:16], ID, ["ea", "cols"], ["cc1"], scale=HOLD, bias=CC0)
     act(T.cx[:], T.ca[:].indirect(T.rfu[:]), AF.Copy, ["ca", "rfu"], ["cxu", "cxm", "cxl"], scale=HOLD)
     act(T.cr[:], T.cr[:], ID, ["cr_a", "cr_b", "cc1"], ["cr"], bias=CC1)
 
-    def constants_2():
-        tp(cf[:, 64:352], T.cn[:, 64:352], ["cn%d" % i for i in range(2, len(COLS))], ["col2"])
-        quant(T.lq[:, 240:368], T.ls[:, 240:368], T.x0[:, 0:512], ["x0a"], ["lz"])
-        ts(T.eb[:, 0:8], T.qq[:, 0:8], R4, None, A.is_equal, None, ["qq", "col2"], ["eb"])
-        cp(T.tfu[:], cf[:, 96:104], ["col2"], ["tfu"])
-        ts(T.cb[:, 0:4], T.eb[:, 1:5], -2.0, None, A.mult, None, ["eb"], ["cb0"])
-        ts(T.mkc[:], T.mkc[:], HF, 4 * BIG, A.not_equal, A.mult, ["mk0", "col2"], ["mk1"])
-        tt(T.cb[:, 0:4], T.cb[:, 0:4], T.eb[:, 0:4], A.add, ["eb", "cb0"], ["cb1"])
+    def unit(b):
+        quant(T.eq[:, 128 * b:128 * b + 128], T.es[:, 128 * b:128 * b + 128], T.et[:, 3 - b:515 - b], ["et"], ["eq%d" % b])
+
+    between = [
+        lambda: quant(T.lq[:, 240:368], T.ls[:, 240:368], T.x0[:, 0:512], ["x0a"], ["lz"]),
+        lambda: tp(cf[:, 64:320], T.cn[:, 64:320], ["cn%d" % i for i in range(2, len(COLS))], ["col2"]),
+        lambda: ts(T.eb[:, 0:8], T.qq[:, 0:8], R4, None, A.is_equal, None, ["qq", "col2"], ["eb"]),
+        lambda: ts(T.cb[:, 0:4], T.eb[:, 1:5], -2.0, None, A.mult, None, ["eb"], ["cb0"]),
+        lambda: tt(T.cb[:, 0:4], T.cb[:, 0:4], T.eb[:, 0:4], A.add, ["eb", "cb0"], ["cb1"]),
+        lambda: cp(T.tfu[:], cf[:, 96:104], ["col2"], ["tfu"]),
+        lambda: ts(T.mkc[:], T.mkc[:], HF, 4 * BIG, A.not_equal, A.mult, ["mk0", "col2"], ["mk1"])]
 
     def constants_3():
         act(T.cb[:, 3:4], T.cb[:, 3:4], AF.Copy, ["cb1"], ["cb"], bias=-2.0)
+        act(T.ca[:, 15:16], T.ca[:, 15:16], AF.Copy, ["ca"], ["ca", "ca1"], bias=-2.0)
         act(KB1, RW, ID, ["col2"], ["kb1"], scale=1.0 / 131072, bias=KB0)
         act(T.jj[:], T.jj[:], ID, ["jj0", "cols"], ["jj"], bias=RF)
         act(T.cq[:], T.cb[:].indirect(T.tfu[:]), AF.Copy, ["cb", "tfu", "cb_hi"], ["cq"], scale=B4)
         act(T.mkb[:, 0:32], T.mkc[:, 0:32], ID, ["mk1", "kb1"], ["mkb"], bias=KB1)
         act(T.mkb[:, 32:64], T.mkc[:, 32:64], ID, ["mk1", "col2"], ["mkc"], bias=KB0)
         act(T.kcol[:, 8:14], T.jj[:, 0:6], AF.Copy, ["jj"], ["nk"], scale=-1.0, bias=-0.5)
-
-    def constants_4():
-        act(T.kk[:], T.kk[:], ID, ["kk0", "col2"], ["kk"], bias=K2R)
+        act(T.ch[:], T.ca[:].indirect(T.rfu[:, 0:6]), AF.Copy, ["ca1", "rfu"], ["ch"], scale=B4)
+        act(T.kk[:], T.jj[:, 0:8], AF.Copy, ["jj"], ["kk"], scale=2.0, bias=256.0)
         act(T.js[:], T.jj[:], AF.Copy, ["jj"], ["js"], scale=1.0 / 64, bias=-8.0 * LAB)
-        act(T.dump[:], T.kk[:], AF.Copy, ["kk"], ["dump"], scale=0.5, bias=384.0 - B4)
+        act(T.dump[:], T.jj[:, 0:8], AF.Copy, ["jj"], ["dump"], bias=512.0 - B4)
 
     def constants_5():
         for t in range(R - 1):
@@ -309,10 +314,12 @@ def rank_program(g, core, T, topo):
         bank = "pb%d" % (3 - h)
         scan(T.rk[:, lo:lo + 256], T[bank][:, 0:256], T.cx[:, lo:lo + 256], -2 * HOLD, A.max, A.add,
              ["cxu", "cxm"] if h else ["cxl"], ["rk%d" % h, bank])
-        ts(T.rku[:, 16 * h:16 * h + 16], T.rk[:, lo + 15:lo + 256:16], BP, None, A.add, None, ["rk%d" % h], ["rku%d" % h])
 
-    def sort(h):
-        cp(T.o[:, 0:512].indirect(T.rku[:, 16 * h:16 * h + 16]), T.vsrc[:, 256 * h:256 * h + 256], ["rku%d" % h, "vs%d" % h], ["o"])
+    def offsets(h):
+        ts(T.rku[:, 16 * h:16 * h + 16], T.rk[:, 256 * h + 15:256 * h + 256:16], BP, None, A.add, None, ["rk%d" % h], ["rku%d" % h])
+
+    def sort(a, b):
+        cp(T.o[:, 0:512].indirect(T.rku[:, 4 * a:4 * b]), T.vsrc[:, 64 * a:64 * b], ["rku%d" % (a // 4), "vs%d" % (a // 4)], ["o"])
 
     xkeys = ["x0a", "x0b"]
     for t in range(R):
@@ -327,14 +334,18 @@ def rank_program(g, core, T, topo):
         mm(2, 256, T.upq[:], T.ups[:], T.xq[:, 256:512], T.xsc[:, 256:512], ["upq", "ups", "xq1"])
         quant(T.xq[:, 0:256], T.xsc[:, 0:256], X[:, 0:1024], xkeys, ["xq0"])
         ws = 16 * (M0 - 1)
-        mm(1, ws, T.upq[:], T.ups[:], T.xq[:, 0:ws], T.xsc[:, 0:ws], ["upq", "ups", "xq0", "xq1"])
         mm(0, 512, T.upq[:], T.ups[:], T.xq[:], T.xsc[:], ["upq", "ups", "xq0", "xq1"])
-        if t:
-            unpack()
-        tt(T.pm[:, 256:512], T.pb2[:, 0:256], T.mk[:, 256:512], A.min, ["mk"], ["pm1", "pb2"])
-        scan(T.sc[:, 256:512], T.rst[:, 256:512], T.pm[:, 256:512], 0.0, A.min, A.max, ["rst", "pm1"], ["sc1"])
+        mm(1, ws, T.upq[:], T.ups[:], T.xq[:, 0:ws], T.xsc[:, 0:ws], ["upq", "ups", "xq0", "xq1"])
         if t == 0:
-            quant(T.kq[:], T.ks[:], T.kt[:], ["kt"], ["kq"])
+            for b in range(3):
+                unit(b)
+        if t == 2:
+            quant(T.vq[:], T.vs[:], T.vt[:], ["vt"], ["vq"])
+        tt(T.pm[:, 256:512], T.pb2[:, 0:256], T.mk[:, 256:512], A.min, ["mk"], ["pm1", "pb2"])
+        if t == 0:
+            unit(3)
+        unpack()
+        scan(T.sc[:, 256:512], T.rst[:, 256:512], T.pm[:, 256:512], 0.0, A.min, A.max, ["rst", "pm1"], ["sc1"])
         tt(T.pm[:, 0:256], T.pb0[:, 0:256], T.mk[:, 0:256], A.min, ["mk"], ["pm0", "pb0"])
         ts(lane(31, 0, 496), T.pb0[:, 0:496], pivot(31), 0.5, A.is_lt, A.subtract, ["sc1"], ["c31", "pb0"])
         scan(T.sc[:, 0:256], T.rst[:, 0:256], T.pm[:, 0:256], 0.0, A.min, A.max, ["rst", "pm0"], ["sc0"])
@@ -361,32 +372,35 @@ def rank_program(g, core, T, topo):
             scan(T.sb[:, e - 8 * m:e], lane(m, 0, 8 * m), lane(m, 8 * m, 16 * m), 0.0, A.add, A.add, ["c%d" % m], ["sb%d" % m])
             if m == 30:
                 tt(T.rna[:], T.cr[:], T.ds[:, 15:512:16], A.subtract, ["cr", "ds"], ["rna"])
+            if m == 31 and t == 0:
+                quant(T.kq[:], T.ks[:], T.kt[:], ["kt"], ["kq"])
             if m % 4 == 2 and m - 1 >= M0:
                 tile((30 - m) // 4)
+            if m < 30 and between:
+                between.pop(0)()
         for i in range((33 - M0) // 4, 4):
-            if i == 3 and t == 0:
-                for b in range(4):
-                    quant(T.eq[:, 128 * b:128 * b + 128], T.es[:, 128 * b:128 * b + 128], T.et[:, 3 - b:515 - b], ["et"], ["eq%d" % b])
             tile(i)
-            if i == 2:
-                tt(T.cx[:, 16 * M0 + 15:512:16], T.rna[:, M0:32], T.sb[:, 256 * M0 + 255:8192:256], A.subtract,
-                   ["rna"] + ["sb%d" % m for m in range(M0, 32)], ["cxu"])
+        tt(T.cx[:, 16 * M0 + 15:512:16], T.rna[:, M0:32], T.sb[:, 256 * M0 + 255:8192:256], A.subtract,
+           ["rna"] + ["sb%d" % m for m in range(M0, 32)], ["cxu"])
+        while between:
+            between.pop(0)()
         if t == 0:
-            unpack()
-            constants_2()
             constants_3()
         tt(T.cx[:, 271:16 * M0:16], T.rna[:, 16:M0], T.rs[:, 16:M0], A.subtract, ["rna"] + ["rs%d" % m for m in range(16, M0)], ["cxm"])
-        tile(4)
-        places(1)
-        tile(5)
-        sort(1)
-        tile(6)
-        tt(T.cx[:, 15:256:16], T.rna[:, 0:16], T.rs[:, 0:16], A.subtract, ["rna"] + ["rs%d" % m for m in range(16)], ["cxl"])
-        tile(7)
         for b in range(4):
             act(X[:, do + b:do + 2048:4], T["pb%d" % (4 + b)][:], AF.Copy, [], ["db%d" % b, "pb%d" % (4 + b)])
-        places(0)
-        sort(0)
+        for step in TAIL.split():
+            k = int(step[1:], 16)
+            if step[0] == "q":
+                tile(k)
+            elif step[0] == "p":
+                places(k)
+            elif step[0] == "o":
+                offsets(k)
+            elif step[0] == "s":
+                sort(k // 16, k % 16)
+            else:
+                tt(T.cx[:, 15:256:16], T.rna[:, 0:16], T.rs[:, 0:16], A.subtract, ["rna"] + ["rs%d" % m for m in range(16)], ["cxl"])
         act(T.junkd[:, 0:128], T.o[:, 0:128], AF.Sign, ["o", "col2"], ["jd0", "ca_"], scale=2.0, bias=NA, accum_out=CA)
         act(T.junkd[:, 128:256], T.o[:, 0:128], AF.Sign, ["o", "col2"], ["jd1", "cb_"], scale=2.0, bias=NB, accum_out=CB)
         act(T.lb[:], T.o[:, 128:512], AF.Copy, ["o"], ["lb"], scale=1.0 / 131072, bias=(1.0 / 1024 - 0.5) / 256)
@@ -414,10 +428,10 @@ def rank_program(g, core, T, topo):
                 bias=T.kcol[:, 8 + m:9 + m], accum_out=T.pa[:, m:m + 1])
         for m in range(nv):
             ts(T.junkb[:, 384 * m:384 * m + 384], T.kc[:], T.jj[:, m:m + 1], 0.5, A.is_gt, A.subtract, ["kc", "jj"], ["j2%d" % m])
-            if m == 0:
+        for m in range(nv):
+            if m == nv - 1:
                 quant(T.tq[:], T.ts[:], T.tt[:], ["tt"], ["tq"])
                 layer((0, 1, 2, 3), T.tq[:], T.ts[:], ["tq"])
-        for m in range(nv):
             scan(T.junkc[:, 192 * m:192 * m + 192], T.junkb[:, 384 * m:384 * m + 192], T.junkb[:, 384 * m + 192:384 * m + 384], 0.0, A.add, A.add,
                  ["j2%d" % m], ["j3%d" % m])
         ts(T.wf[:], T.lac[:], WL, float(doff(t)), A.is_equal, A.mult, ["lac", "wl"], ["wf"])
@@ -431,8 +445,6 @@ def rank_program(g, core, T, topo):
         scan(T.ssc[:, 0:ns], T.pg[:, 0:ns], T.cq[:, 0:ns], -B4, A.max, A.add, ["pg", "cq"], ["ssc"])
         ts(T.elu[:, 0:32], T.el[:], 4.0, 0.0, A.mult, A.add, ["el"], ["elu0"])
         ts(T.slu[:, 0:ns // 4], T.ssc[:, 3:ns:4], 4.0, TB4, A.mult, A.add, ["ssc", "col2"], ["slu"])
-        if t == 0:
-            constants_4()
         dbk = ["db%d" % b for b in range(4)] + ["dz%d" % t]
         dwin = X[:, do:do + 2064]
         src = xkeys + dbk + [xk + "y%d" % b for b in range(4)]
@@ -458,27 +470,28 @@ def rank_program(g, core, T, topo):
         ts(T.elu[:, 96:128], T.el[:], 4.0, 3.0, A.mult, A.add, ["el"], ["elu3"])
         ts(MN, cnt, lcnt, None, A.min, None, ["cnt%d" % t, "lcnt%d" % t], ["mn"])
         tt(T.lab[:], T.lac[:], T.wf[:], A.max, ["lac", "wf"], ["lab"])
-        ts(T.ha[:, 0:ns // 4], T.kk[:, 0:ns // 4], MN, -4096.0, A.is_lt, A.mult, ["kk", "mn"], ["ha"])
-        for k in range(1, 4):
-            merge(k)
-        tt(T.hb[:, 0:ns // 4], T.ha[:, 0:ns // 4], T.dump[:, 0:ns // 4], A.add, ["ha", "dump"], ["hb"])
+        scan(T.hsc[:, 0:ns], T.pg[:, 0:ns], T.ch[:, 0:ns], -B4, A.max, A.add, ["pg", "ch"], ["hsc"])
+        ts(T.ha[:, 0:np_], T.kk[:, 0:np_], MN, -4096.0, A.is_lt, A.mult, ["kk", "mn"], ["ha"])
         if t < R - 1:
             tt(T.lj[:], T.lab[:], T.js[:], A.add, ["lab", "js"], ["lj"])
         else:
             ts(T.olu[:], T.lab[:], -8.0 * LAB, 0.125, A.add, A.mult, ["lab"], ["olu"])
-        tt(T.hc[:, 0:ns // 4], T.hb[:, 0:ns // 4], T.ssc[:, 3:ns:4], A.max, ["hb", "ssc"], ["hc"])
+        for k in range(1, 4):
+            merge(k)
+        tt(T.hb[:, 0:np_], T.ha[:, 0:np_], T.dump[:, 0:np_], A.add, ["ha", "dump"], ["hb"])
         if t < R - 1:
             ts(T.vlu[:], T.lj[:], 64.0, None, A.mult, None, ["lj"], ["vlu"])
-        ts(T.hlu[:, 0:ns // 4], T.hc[:, 0:ns // 4], 4.0, TB4, A.mult, A.add, ["hc", "col2"], ["hlu"])
-        if t == 1:
-            quant(T.vq[:], T.vs[:], T.vt[:], ["vt"], ["vq"])
+        tt(T.hc[:, 0:np_], T.hb[:, 0:np_], T.hsc[:, 15:ns:16], A.max, ["hb", "hsc"], ["hc"])
+        for b in range(4):
+            ts(T.hlu[:, np_ * b:np_ * (b + 1)], T.hc[:, 0:np_], 4.0, 4 * B4 + b, A.mult, A.add, ["hc"], ["hlu%d" % b])
         layer((4, 5, 6, 7), lq[:, la:la + 128], ls[:, la:la + 128], ["lq%d" % t, "lz"])
         for b in range(4):
-            if b == 3:
-                act(T.hs[:, b:4 * ns:4], T["pb%d" % (4 + b)][:, 0:ns], AF.Copy, [], ["h%d" % b, "pb%d" % (4 + b)], scale=0.03125)
+            h = T.hs[:, ns * b:ns * (b + 1)]
+            if b == 2:
+                act(h, T["pb%d" % (4 + b)][:, 0:ns], AF.Copy, [], ["h%d" % b, "pb%d" % (4 + b)], scale=0.03125)
             else:
-                ts(T.hs[:, b:4 * ns:4], T["pb%d" % (4 + b)][:, 0:ns], 0.03125, None, A.mult, None, [], ["h%d" % b, "pb%d" % (4 + b)])
-        cp(XN[:, 0:2432].indirect(T.hlu[:, 0:ns // 4]), T.hs[:, 0:4 * ns], ["hlu"] + ["h%d" % b for b in range(4)], xkeys)
+                ts(h, T["pb%d" % (4 + b)][:, 0:ns], 0.03125, None, A.mult, None, [], ["h%d" % b, "pb%d" % (4 + b)])
+        cp(XN[:, 0:2432].indirect(T.hlu[:, 0:4 * np_]), T.hs[:, 0:4 * ns], [c + str(b) for c in ("hlu", "h") for b in range(4)], xkeys)
         if t == 0:
             constants_5()
         if t < R - 1:
@@ -499,10 +512,11 @@ def rank_program(g, core, T, topo):
     act(T.ys[:, 0:256], T.pb0[:, 0:256], AF.Copy, [], ["ys0", "pb0"])
     dma("S", T.y[:, 0:256], T.ys[:, 0:256], ["ys0"], ["out1"])
     cp(T.ys[:, 256:512], T.pb1[:, 0:256], [], ["ys1", "pb1"])
-    dma("Y", T.oc[:], T.xq[:].bitcast(dt.uint8), ["xq0", "xq1"], ["out0"])
+    dma("Y", T.oc[:, 0:1024], T.xq[:, 0:256].bitcast(dt.uint8), ["xq0"], ["out0"])
+    dma("Y", T.oc[:, 1024:2048], T.xq[:, 256:512].bitcast(dt.uint8), ["xq1"], ["out8"])
     for k in range(4):
         dma("Y", T.osc[4 * k:4 * k + 4, :], T.xsc[32 * k:32 * k + 4, :], ["xq0", "xq1"], ["out%d" % (2 + k)])
     dma("S", T.y[:, 256:512], T.ys[:, 256:512], ["ys1"], ["out7"])
-    op("G", None, ["out%d" % k for k in range(8)], [], "sent", 0)
+    op("G", None, ["out%d" % k for k in range(9)], [], "sent", 0)
     emit(g, T, ops)
     g.wait_ge(T.sem.sent, 3 * R * out_n)

@@ -4,11 +4,10 @@ A = AluOpType
 AF = ActivationFunctionType
 R = 3
 NPASS = (6, 5, 4)
-APASS = (3, 2, 2)
-M0 = 21
-SPLIT = True
+APASS = (2, 2, 2)
+M0 = 22
+PIECES = ((256, 384), (384, 512), (0, 256))
 LAG = 2
-MERGE = "SSSV"
 TAIL = "q4 q5 p1 q6 o1 c0 q7 s47 p0 s78 o0 s04"
 TW = (512, 448, 384, 384, 256, 192, 128, 128)
 TBASE = [sum(TW[:i]) for i in range(8)]
@@ -20,7 +19,7 @@ LAB = 138
 F32, BF, I32, U16, X4, U8 = "float32", "bfloat16", "int32", "uint16", "float8_e4m3fn_x4", "uint8"
 COLS = (([[0, 2], [1, 16]], 0),
         ([[0, 2], [-1, 16]], int(15 - HOLD - BP)),
-        ([[0, 2], [1, 4], [0, 4]], 0),
+        ([[0, 2], [1, 4], [0, 4]], 1),
         ([[0, 8], [1, 4]], 0),
         ([[1, 2], [0, 16]], 0),
         ([[0, 2], [-1024, 16]], 1 - 1024 * LAB),
@@ -40,13 +39,12 @@ def doff(t):
 
 SCRATCH = {}
 for _d, _names in (
-        (BF, "ut512 vt512 kt512 gq512 qs512 one528 et528 sg2048 sb8192 ds512 mk512 rst512 junka1536 junkb1536 junkc768 junkd256 "
+        (BF, "ut512 vt512 kt512 gq512 qs512 one528 et528 sg2304 sb8192 ds512 mk512 rst512 junka1536 junkb1536 junkc768 junkd256 "
              "lb384 fl384 kc384 tt512 st512 hs384"),
-        (X4, "uq128 vq128 upq128 wq512 xq512 kq128 eq512 tq128 sq384 lq368"),
-        (U8, "us128 vs128 ups128 wsc512 xsc512 ks128 es512 ts128 ss384 ls368"),
+        (X4, "uq128 vq128 upq128 wq512 xq512 kq128 eq512 tq128 sq384 lq272"),
+        (U8, "us128 vs128 ups128 wsc512 xsc512 ks128 es512 ts128 ss384 ls272"),
         (F32, "pm512 sc512 cx512 rk512 rs32 rna32 vsrc512 o528 cq128 tsc128 ssc96 pg96 km64 kmt64 mkb64 mkc64 sm16 pa8 tab4096 cn320 cf320 cg16 "
-              "qq32 ea32 eb32 ca16 cb8 cr32 jj32 js32 kk8 dump8 kcol16 wa32 wb32 wf32 we32 el32 lab32 lac32 lj32 ha8 hb8 hc8 obs512 ys512 "
-              "ch96 hsc96"),
+              "qq32 ea32 eb8 ca16 cb8 cr32 jj32 js32 kk24 dump24 kcol16 wa32 wb32 wf32 we32 el32 lab32 lac32 lj32 ha24 hb24 hc24 obs512 ys512"),
         (U16, "rku32 posu8 tlu32 slu24 hlu24 elu128 vlu32 olu32 upu8 rfu32 tfu8"),
         (I32, "ti32 tj32")):
     for _s in _names.split():
@@ -62,7 +60,7 @@ for _t in range(R):
 for _b in range(8):
     SCRATCH["pb%d" % _b] = ("psum", [128, 512], F32)
 
-SEMAPHORES = (["pe", "dve", "act", "pool", "sent"] + ["d%d" % i for i in range(16)]
+SEMAPHORES = (["pe", "dve", "act", "pool", "sent"] + ["d%d" % i for i in range(24)]
               + ["ac%d" % t for t in range(R)] + ["aq%d" % t for t in range(R)])
 QUEUE_SEM = {"T": "pe", "V": "dve", "S": "act", "G": "pool"}
 
@@ -197,16 +195,16 @@ def rank_program(g, core, T, topo):
         for b, bank in enumerate(banks):
             mm(bank, 128, T.wq[:, 128 * b:128 * b + 128], T.wsc[:, 128 * b:128 * b + 128], q, s, ["wq", "wsc"] + r)
 
-    def unpack():
-        for b in range(4):
-            mm(4 + b, 512, T.eq[:, 128 * b:128 * b + 128], T.es[:, 128 * b:128 * b + 128], T.xq[:], T.xsc[:], ["eq%d" % b, "xq0", "xq1"])
+    def unpack(banks, q, s, r, which=range(4)):
+        for b in which:
+            mm(banks[b], 512, T.eq[:, 128 * b:128 * b + 128], T.es[:, 128 * b:128 * b + 128], q, s, ["eq%d" % b] + r)
 
     cf, cg, sm = T.cf, T.cg, T.sm
     ID = AF.Identity
     dma("Y", T.ut[:], T.u[:], [], ["ut"])
-    dma("S", T.x0[:, 1024:2048], T.x[:, 1024:2048], [], ["x0b"])
-    dma("Y", T.x0[:, 0:1024], T.x[:, 0:1024], [], ["x0a"])
-    dma("Y", T.wq[:].bitcast(dt.uint8), T.wc[:], ["x0a"], ["wq"])
+    for i, (lo, hi) in enumerate(PIECES):
+        dma("SSY"[i], T.x0[:, 4 * lo:4 * hi], T.x[:, 4 * lo:4 * hi], [], ["x0%d" % i])
+    dma("Y", T.wq[:].bitcast(dt.uint8), T.wc[:], ["x02"], ["wq"])
     dma("Y", T.wsc[:], T.ws[:], [], ["wsc"])
     dma("Y", T.vt[:], T.v[:], [], ["vt"])
 
@@ -218,74 +216,92 @@ def rank_program(g, core, T, topo):
     iota(T.qq[:], [[1, 32]], 0, ["qq"])
     ms(T.one[:], 1.0, ["one"])
     select(T.et[:], T.one[:], [[-1, 528]], A.is_equal, 3, 4, ["one"], ["et"])
-    iota(T.qs[:], [[0, 32], [1, 16]], 0, ["qs"])
-    select(T.gq[:], T.one[:, 0:512], [[-16, 8], [0, 64]], A.is_ge, 0, 1, ["one"], ["gq"])
     iota(T.cr[:, 0:M0], [[16, M0]], 8 * (32 - M0), ["cr_a"])
     iota(T.cr[:, M0:32], [[0, 32 - M0]], 248, ["cr_b"])
+    select(T.gq[:], T.one[:, 0:512], [[-16, 8], [0, 64]], A.is_ge, 0, 1, ["one"], ["gq"])
+    iota(T.qs[:], [[0, 32], [1, 16]], 0, ["qs"])
     select(T.kt[:], T.gq[:], [[16, 8], [0, 64]], A.is_ge, 15, -1, ["gq"], ["kt"])
-    for i in range(2, len(COLS)):
-        iota(T.cn[:, 32 * i:32 * i + 32], COLS[i][0], COLS[i][1], ["cn%d" % i])
-    iota(T.vsrc[:], [[640, 4], [1, 128]], 512 * LAB, ["vs0", "vs1"])
-    iota(T.mkc[:], [[0, 2], [1, 2], [0, 16]], 0, ["mk0"])
-    iota(T.jj[:], [[16, 32]], 0, ["jj0"])
-    iota(T.cb[:, 4:8], [[0, 4]], 0, ["cb_hi"])
-    iota(T.rs[:, 0:1], [[0, 1]], 0, ["rs0"])
-    iota(T.lab[:], [[8, 4], [0, 8]], 8 * LAB, ["lab"])
-    iota(T.o[:, 512:528], [[0, 16]], 1000000, ["o_hi"])
-    for t in range(R):
-        iota(T["x%d" % t][:, 4 * doff(t) + 2048:4 * doff(t) + 2064], [[0, 16]], 0, ["dz%d" % t])
-    iota(T.st[:, 384:512], [[0, 128]], 0, ["st_hi"])
-    iota(T.tab[:, 0:3072], [[1, 3072]], 512 * LAB, ["tab0"])
+
+    def constants_1():
+        for i in (1, 4, 5, 6, 7):
+            pad(i)
+        for i in range(2, len(COLS)):
+            iota(T.cn[:, 32 * i:32 * i + 32], COLS[i][0], COLS[i][1], ["cn%d" % i])
+        iota(T.mkc[:], [[0, 2], [1, 2], [0, 16]], 0, ["mk0"])
+        iota(T.jj[:], [[16, 32]], 0, ["jj0"])
+        iota(T.rs[:, 0:1], [[0, 1]], 0, ["rs0"])
+        iota(T.vsrc[:], [[640, 4], [1, 128]], 512 * LAB, ["vs0", "vs1"])
+        iota(T.kk[:], [[4, 24]], 127, ["kk0"])
+        iota(T.lab[:], [[8, 4], [0, 8]], 8 * LAB, ["lab"])
+        iota(T.o[:, 512:528], [[0, 16]], 1000000, ["o_hi"])
+        for t in range(R):
+            iota(T["x%d" % t][:, 4 * doff(t) + 2048:4 * doff(t) + 2064], [[0, 16]], 0, ["dz%d" % t])
+        iota(T.st[:, 384:512], [[0, 128]], 0, ["st_hi"])
+        iota(T.tab[:, 0:2048], [[1, 2048]], 512 * LAB, ["tab0"])
+
+    def rows(i):
+        return ["c%d" % m for m in range(29 - 4 * i, 33 - 4 * i)]
 
     def pad(i):
         lo = 16 * (29 - 4 * i)
-        ms(T.ct[:, 4 * (TBASE[i] + lo):4 * (TBASE[i] + TW[i])], 0.0, ["c%d" % m for m in range(29 - 4 * i, 33 - 4 * i)])
+        ap, keys = T.ct[:, 4 * (TBASE[i] + lo):4 * (TBASE[i] + TW[i])], rows(i)
+        if i in (0, 2, 3):
+            act(ap, T.one[:, 0:4 * (TW[i] - lo)], AF.Copy, ["one"], keys, scale=0.0)
+        else:
+            iota(ap, [[0, 4 * (TW[i] - lo)]], 0, keys)
 
+    for i in (3, 2):
+        pad(i)
+    ms(T.rst[:], 1e29, ["rst0"])
     tp(cf[:, 0:64], T.cn[:, 0:64], ["cn0", "cn1"], ["cols"])
-    pad(0)
+    ts(T.upu[:], T.qq[:, 0:8], 16.0, None, A.mult, None, ["qq"], ["upu"])
     ts(T.ea[:], T.qq[:], RF, None, A.is_equal, None, ["qq", "cols"], ["ea"])
     cp(T.rfu[:], cf[:, 0:32], ["cols"], ["rfu"])
     ts(T.ca[:], T.ea[:, 1:17], -2.0, None, A.mult, None, ["ea"], ["ca0"])
-    ts(T.upu[:], T.qq[:, 0:8], 16.0, None, A.mult, None, ["qq"], ["upu"])
+    ms(T.rst[:, 0:512:16], -1e29, ["rst"], ["rst0"])
     tt(T.ca[:], T.ca[:], T.ea[:, 0:16], A.add, ["ea", "ca0"], ["ca"])
     act(T.mk[:], T.ea[:].indirect(T.rfu[:]), AF.Copy, ["ea", "rfu"], ["mk"], scale=2e29, bias=-1e29)
-    for i in (2, 3, 1, 4):
-        pad(i)
+
+    def unit(b):
+        quant(T.eq[:, 128 * b:128 * b + 128], T.es[:, 128 * b:128 * b + 128], T.et[:, 3 - b:515 - b], ["et"], ["eq%d" % b])
+
     quant(T.uq[:], T.us[:], T.ut[:], ["ut"], ["uq"])
-    for i in (5, 6, 7):
-        pad(i)
     act(T.ups[:], T.us[:].indirect(T.upu[:]), AF.Copy, ["uq", "upu"], ["ups"])
-    act(T.rst[:], T.qs[:], AF.Copy, ["qs"], ["rst"], scale=2e29, bias=-1e29)
+    pad(0)
     cp(T.upq[:].bitcast(dt.uint32), T.uq[:].bitcast(dt.uint32).indirect(T.upu[:]), ["uq", "upu"], ["upq"])
     act(CC1, T.ea[:, 15:16], ID, ["ea", "cols"], ["cc1"], scale=HOLD, bias=CC0)
     act(T.cx[:], T.ca[:].indirect(T.rfu[:]), AF.Copy, ["ca", "rfu"], ["cxu", "cxm", "cxl"], scale=HOLD)
     act(T.cr[:], T.cr[:], ID, ["cr_a", "cr_b", "cc1"], ["cr"], bias=CC1)
 
-    def unit(b):
-        quant(T.eq[:, 128 * b:128 * b + 128], T.es[:, 128 * b:128 * b + 128], T.et[:, 3 - b:515 - b], ["et"], ["eq%d" % b])
-
     between = [
-        lambda: quant(T.lq[:, 240:368], T.ls[:, 240:368], T.x0[:, 0:512], ["x0a"], ["lz"]),
+        lambda: None,
+        lambda: None,
+        lambda: None,
+        lambda: None,
         lambda: tp(cf[:, 64:320], T.cn[:, 64:320], ["cn%d" % i for i in range(2, len(COLS))], ["col2"]),
-        lambda: ts(T.eb[:, 0:8], T.qq[:, 0:8], R4, None, A.is_equal, None, ["qq", "col2"], ["eb"]),
-        lambda: ts(T.cb[:, 0:4], T.eb[:, 1:5], -2.0, None, A.mult, None, ["eb"], ["cb0"]),
-        lambda: tt(T.cb[:, 0:4], T.cb[:, 0:4], T.eb[:, 0:4], A.add, ["eb", "cb0"], ["cb1"]),
-        lambda: cp(T.tfu[:], cf[:, 96:104], ["col2"], ["tfu"]),
-        lambda: ts(T.mkc[:], T.mkc[:], HF, 4 * BIG, A.not_equal, A.mult, ["mk0", "col2"], ["mk1"])]
+        lambda: cp(T.tfu[:], cf[:, 96:104], ["col2"], ["tfu"])]
 
-    def constants_3():
-        act(T.cb[:, 3:4], T.cb[:, 3:4], AF.Copy, ["cb1"], ["cb"], bias=-2.0)
-        act(T.ca[:, 15:16], T.ca[:, 15:16], AF.Copy, ["ca"], ["ca", "ca1"], bias=-2.0)
-        act(KB1, RW, ID, ["col2"], ["kb1"], scale=1.0 / 131072, bias=KB0)
-        act(T.jj[:], T.jj[:], ID, ["jj0", "cols"], ["jj"], bias=RF)
-        act(T.cq[:], T.cb[:].indirect(T.tfu[:]), AF.Copy, ["cb", "tfu", "cb_hi"], ["cq"], scale=B4)
+    def constants_4():
+        ts(T.mkc[:], T.mkc[:], HF, 4 * BIG, A.not_equal, A.mult, ["mk0", "col2"], ["mk1"])
         act(T.mkb[:, 0:32], T.mkc[:, 0:32], ID, ["mk1", "kb1"], ["mkb"], bias=KB1)
         act(T.mkb[:, 32:64], T.mkc[:, 32:64], ID, ["mk1", "col2"], ["mkc"], bias=KB0)
+
+    def constants_3():
+        act(T.eb[:], T.qq[:, 0:8], AF.Relu, ["qq", "col2"], ["eb"], scale=-1.0, bias=R4)
+        act(KB1, RW, ID, ["col2"], ["kb1"], scale=1.0 / 131072, bias=KB0)
+        act(T.jj[:], T.jj[:], ID, ["jj0", "cols"], ["jj"], bias=RF)
+        act(T.cb[:], T.eb[:], AF.Abs, ["eb"], ["cb1"], bias=-0.625)
+        unpacked(0)
+        act(T.cb[:, 3:4], T.cb[:, 3:4], AF.Copy, ["cb1"], ["cb"], bias=0.5)
         act(T.kcol[:, 8:14], T.jj[:, 0:6], AF.Copy, ["jj"], ["nk"], scale=-1.0, bias=-0.5)
-        act(T.ch[:], T.ca[:].indirect(T.rfu[:, 0:6]), AF.Copy, ["ca1", "rfu"], ["ch"], scale=B4)
-        act(T.kk[:], T.jj[:, 0:8], AF.Copy, ["jj"], ["kk"], scale=2.0, bias=256.0)
+        unpacked(1)
+        act(T.cq[:], T.cb[:].indirect(T.tfu[:]), AF.Copy, ["cb", "tfu"], ["cq"], scale=-4 * B4, bias=2.5 * B4)
+        unpacked(2)
+
+    def constants_6():
+        act(T.kk[:], T.kk[:], ID, ["kk0", "col2"], ["kk"], bias=R4)
         act(T.js[:], T.jj[:], AF.Copy, ["jj"], ["js"], scale=1.0 / 64, bias=-8.0 * LAB)
-        act(T.dump[:], T.jj[:, 0:8], AF.Copy, ["jj"], ["dump"], bias=512.0 - B4)
+        act(T.dump[:], T.kk[:], AF.Copy, ["kk"], ["dump"], bias=384.0 - B4)
 
     def constants_5():
         for t in range(R - 1):
@@ -303,7 +319,8 @@ def rank_program(g, core, T, topo):
 
     def tile(i):
         lo, w = TBASE[i], TW[i]
-        quant(T.cc[:, lo:lo + w], T.cs[:, lo:lo + w], T.ct[:, 4 * lo:4 * (lo + w)], ["c%d" % m for m in range(29 - 4 * i, 33 - 4 * i)], ["cc%d" % i])
+        wq = max(512 - 64 * i, 128) if t else w
+        quant(T.cc[:, lo:lo + wq], T.cs[:, lo:lo + wq], T.ct[:, 4 * lo:4 * (lo + wq)], rows(i), ["cc%d" % i])
         if w > 256:
             mm(2, w - 256, T.kq[:], T.ks[:], T.cc[:, lo + 256:lo + w], T.cs[:, lo + 256:lo + w], ["kq", "cc%d" % i], i == 0, i == 3)
         w = min(w, 256)
@@ -321,51 +338,71 @@ def rank_program(g, core, T, topo):
     def sort(a, b):
         cp(T.o[:, 0:512].indirect(T.rku[:, 4 * a:4 * b]), T.vsrc[:, 64 * a:64 * b], ["rku%d" % (a // 4), "vs%d" % (a // 4)], ["o"])
 
-    xkeys = ["x0a", "x0b"]
+    xkeys = ["x00", "x01", "x02"]
     for t in range(R):
         X, XN = T["x%d" % t], T["x%d" % (t + 1)]
         xk = "x%d" % t
         yo, do = 4 * yoff(t), 4 * doff(t)
         np_, na = NPASS[t], APASS[t]
         nv, ns = np_ - na, 16 * np_
+        cnt, lcnt = T["cnt%d" % t][:, 0:1], T["lcnt%d" % t][:, 0:1]
         la = 16 * sum(NPASS[t + 1:])
-        cnt, lcnt, lq, ls = T["cnt%d" % t][:, 0:1], T["lcnt%d" % t][:, 0:1], T.lq, T.ls
-        quant(T.xq[:, 256:512], T.xsc[:, 256:512], X[:, 1024:2048], xkeys[-1:] if t == 0 else xkeys, ["xq1"])
-        mm(2, 256, T.upq[:], T.ups[:], T.xq[:, 256:512], T.xsc[:, 256:512], ["upq", "ups", "xq1"])
-        quant(T.xq[:, 0:256], T.xsc[:, 0:256], X[:, 0:1024], xkeys, ["xq0"])
+
+        def qx(lo, hi):
+            return T.xq[:, lo:hi], T.xsc[:, lo:hi]
+
+        xqk = ["xq%d" % i for i in range(3)]
+        for i, (lo, hi) in enumerate(PIECES):
+            quant(*qx(lo, hi), X[:, 4 * lo:4 * hi], xkeys[i:i + 1] if t == 0 else xkeys, ["xq%d" % i])
+            mm(2 + i, hi - lo, T.upq[:], T.ups[:], *qx(lo, hi), ["upq", "ups", "xq%d" % i])
+            if t == 0 and i == 1:
+                unit(0)
         ws = 16 * (M0 - 1)
-        mm(0, 512, T.upq[:], T.ups[:], T.xq[:], T.xsc[:], ["upq", "ups", "xq0", "xq1"])
-        mm(1, ws, T.upq[:], T.ups[:], T.xq[:, 0:ws], T.xsc[:, 0:ws], ["upq", "ups", "xq0", "xq1"])
+        mm(1, ws, T.upq[:], T.ups[:], *qx(0, ws), ["upq", "ups"] + xqk)
+        mm(0, 512, T.upq[:], T.ups[:], *qx(0, 512), ["upq", "ups"] + xqk)
         if t == 0:
-            for b in range(3):
-                unit(b)
+            constants_1()
+        if t == 1:
+            iota(T.tab[:, 3072:4096], [[1, 1024]], 512 * (LAB + 6), ["tab2"])
+
+        def own(i, step):
+            (lo, hi), bank = PIECES[i], "pb%d" % (2 + i)
+            if step == 0:
+                tt(T.pm[:, lo:hi], T[bank][:, 0:hi - lo], T.mk[:, lo:hi], A.min, ["mk"], ["pm%d" % i, bank])
+            else:
+                scan(T.sc[:, lo:hi], T.rst[:, lo:hi], T.pm[:, lo:hi], 0.0, A.min, A.max, ["rst", "pm%d" % i], ["sc%d" % i])
+
+        if t == 0:
+            unit(1)
+            dma("Y", T.lq[:, 240:272].bitcast(dt.uint8), T.xq[:, 256:288].bitcast(dt.uint8), ["xq0"], ["lz"])
+            dma("Y", T.ls[:, 240:272], T.xsc[:, 256:288], ["xq0"], ["lz1"])
+        for i, step in ((0, 0), (1, 0), (0, 1), (2, 0), (1, 1)):
+            own(i, step)
+        if t == 0:
+            unit(2)
+            unit(3)
         if t == 2:
             quant(T.vq[:], T.vs[:], T.vt[:], ["vt"], ["vq"])
-        tt(T.pm[:, 256:512], T.pb2[:, 0:256], T.mk[:, 256:512], A.min, ["mk"], ["pm1", "pb2"])
-        if t == 0:
-            unit(3)
-        unpack()
-        scan(T.sc[:, 256:512], T.rst[:, 256:512], T.pm[:, 256:512], 0.0, A.min, A.max, ["rst", "pm1"], ["sc1"])
-        tt(T.pm[:, 0:256], T.pb0[:, 0:256], T.mk[:, 0:256], A.min, ["mk"], ["pm0", "pb0"])
+        own(2, 1)
+        unpack((4, 5, 6, 7), *qx(0, 512), xqk)
         ts(lane(31, 0, 496), T.pb0[:, 0:496], pivot(31), 0.5, A.is_lt, A.subtract, ["sc1"], ["c31", "pb0"])
-        scan(T.sc[:, 0:256], T.rst[:, 0:256], T.pm[:, 0:256], 0.0, A.min, A.max, ["rst", "pm0"], ["sc0"])
 
         arows = list(range(M0 - 1, 0, -1))
         for k in range(len(arows) + LAG):
             if k < len(arows):
                 m = arows[k]
-                act(T.sg[:, 512 * (k % 4):512 * (k % 4) + 16 * m], T.pb1[:, 0:16 * m], AF.Sign, ["sc%d" % (m // 16)],
-                    ["sg%d" % (k % 4), "pb1"], bias=pivot(m), scale=-1.0)
+                act(T.sg[:, 384 * (k % 6):384 * (k % 6) + 16 * m], T.pb1[:, 0:16 * m], AF.Sign, ["sc0" if m >= 16 else "sc2"],
+                    ["sg%d" % (k % 6), "pb1"], bias=pivot(m), scale=-1.0)
             j = k - LAG
             if j >= 0:
                 m = arows[j]
-                act(lane(m, 0, 16 * m), T.sg[:, 512 * (j % 4):512 * (j % 4) + 16 * m], AF.Relu, ["sg%d" % (j % 4)],
+                act(lane(m, 0, 16 * m), T.sg[:, 384 * (j % 6):384 * (j % 6) + 16 * m], AF.Relu, ["sg%d" % (j % 6)],
                     ["c%d" % m, "rs%d" % m], accum_out=T.rs[:, m:m + 1])
         ts(lane(30, 0, 480), T.pb0[:, 0:480], pivot(30), 0.5, A.is_lt, A.subtract, ["sc1"], ["c30", "pb0"])
-        tt(lane(32, 0, 512), T.pb0[:], T.sc[:], A.is_le, ["sc0", "sc1"], ["c32", "pb0"])
+        tt(lane(32, 0, 512), T.pb0[:], T.sc[:], A.is_le, ["sc0", "sc1", "sc2"], ["c32", "pb0"])
         for m in range(31, M0 - 1, -1):
             if m - 2 >= M0:
-                ts(lane(m - 2, 0, 16 * m - 32), T.pb0[:, 0:16 * m - 32], pivot(m - 2), 0.5, A.is_lt, A.subtract, ["sc1"], ["c%d" % (m - 2), "pb0"])
+                ts(lane(m - 2, 0, 16 * m - 32), T.pb0[:, 0:16 * m - 32], pivot(m - 2), 0.5, A.is_lt, A.subtract, ["sc0", "sc1"], ["c%d" % (m - 2), "pb0"])
             if m == 31:
                 scan(T.ds[:], T.qs[:], lane(32, 0, 512), 0.0, A.min, A.add, ["qs", "c32"], ["ds"])
             e = 256 * (m + 1)
@@ -384,11 +421,17 @@ def rank_program(g, core, T, topo):
            ["rna"] + ["sb%d" % m for m in range(M0, 32)], ["cxu"])
         while between:
             between.pop(0)()
+        tt(T.cx[:, 271:16 * M0:16], T.rna[:, 16:M0], T.rs[:, 16:M0], A.subtract, ["rna"] + ["rs%d" % m for m in range(16, M0)], ["cxm"])
+
+        def unpacked(b):
+            act(X[:, do + b:do + 2048:4], T["pb%d" % (4 + b)][:], AF.Copy, [], ["db%d" % b, "pb%d" % (4 + b)])
+
         if t == 0:
             constants_3()
-        tt(T.cx[:, 271:16 * M0:16], T.rna[:, 16:M0], T.rs[:, 16:M0], A.subtract, ["rna"] + ["rs%d" % m for m in range(16, M0)], ["cxm"])
-        for b in range(4):
-            act(X[:, do + b:do + 2048:4], T["pb%d" % (4 + b)][:], AF.Copy, [], ["db%d" % b, "pb%d" % (4 + b)])
+        else:
+            for b in range(4):
+                unpacked(b)
+        dbk = ["db%d" % b for b in range(4)]
         for step in TAIL.split():
             k = int(step[1:], 16)
             if step[0] == "q":
@@ -397,6 +440,8 @@ def rank_program(g, core, T, topo):
                 places(k)
             elif step[0] == "o":
                 offsets(k)
+                if k == 0 and t == 0:
+                    constants_4()
             elif step[0] == "s":
                 sort(k // 16, k % 16)
             else:
@@ -404,6 +449,8 @@ def rank_program(g, core, T, topo):
         act(T.junkd[:, 0:128], T.o[:, 0:128], AF.Sign, ["o", "col2"], ["jd0", "ca_"], scale=2.0, bias=NA, accum_out=CA)
         act(T.junkd[:, 128:256], T.o[:, 0:128], AF.Sign, ["o", "col2"], ["jd1", "cb_"], scale=2.0, bias=NB, accum_out=CB)
         act(T.lb[:], T.o[:, 128:512], AF.Copy, ["o"], ["lb"], scale=1.0 / 131072, bias=(1.0 / 1024 - 0.5) / 256)
+        if t == 0:
+            unpacked(3)
         ts(T.wa[:], T.rku[:], 128.0, 8.0 * (LAB + 4 + 2 * t), A.is_lt, A.mult, ["rku0", "rku1"], ["wa"])
         scan(T.tsc[:], T.o[:, 0:128], T.cq[:], -B4, A.max, A.add, ["o", "cq"], ["tsc"])
         tt(T.lac[:], T.lab[:], T.wa[:], A.max, ["lab", "wa"], ["lac"])
@@ -422,80 +469,91 @@ def rank_program(g, core, T, topo):
         ts(T.fl[:], T.lb[:], cnt, KEY, A.add, A.is_equal, ["lb"] + vk, ["fl"])
         ts(WL, KEY, cnt, 2048.0, A.subtract, A.mult, vk, ["wl"])
         scan(T.kc[:], T.fl[:], T.fl[:], 0.0, A.add, A.max, ["fl"], ["kc"])
-        ts(W, KEY, cnt, 131072.0, A.subtract, A.mult, vk, ["w"])
-        for m in range(nv, np_):
-            act(T.junka[:, 384 * (m - nv):384 * (m - nv + 1)], T.kc[:], AF.Sign, ["kc", "nk"], ["junk%d" % (m - nv), "pa%d" % m],
-                bias=T.kcol[:, 8 + m:9 + m], accum_out=T.pa[:, m:m + 1])
-        for m in range(nv):
-            ts(T.junkb[:, 384 * m:384 * m + 384], T.kc[:], T.jj[:, m:m + 1], 0.5, A.is_gt, A.subtract, ["kc", "jj"], ["j2%d" % m])
-        for m in range(nv):
-            if m == nv - 1:
-                quant(T.tq[:], T.ts[:], T.tt[:], ["tt"], ["tq"])
-                layer((0, 1, 2, 3), T.tq[:], T.ts[:], ["tq"])
-            scan(T.junkc[:, 192 * m:192 * m + 192], T.junkb[:, 384 * m:384 * m + 192], T.junkb[:, 384 * m + 192:384 * m + 384], 0.0, A.add, A.add,
-                 ["j2%d" % m], ["j3%d" % m])
         ts(T.wf[:], T.lac[:], WL, float(doff(t)), A.is_equal, A.mult, ["lac", "wl"], ["wf"])
-        ts(T.posu[:, 0:nv], T.junkc[:, 191:192 * nv:192], -1.0, 320.0, A.mult, A.add, ["j3%d" % m for m in range(nv)], ["posu_a"])
-        ts(T.posu[:, nv:np_], T.pa[:, nv:np_], -0.5, 320.0, A.mult, A.add, ["pa%d" % m for m in range(nv, np_)], ["posu_b"])
+        ts(W, KEY, cnt, 131072.0, A.subtract, A.mult, vk, ["w"])
+        a0, v0 = (0, na) if t == 0 else (nv, 0)
+        for i in range(na):
+            m = a0 + i
+            act(T.junka[:, 384 * i + 16 * a0:384 * i + 384], T.kc[:, 16 * a0:384], AF.Sign, ["kc", "nk"], ["junk%d" % i, "pa%d" % i],
+                bias=T.kcol[:, 8 + m:9 + m], accum_out=T.pa[:, i:i + 1])
+        if t == 0:
+            constants_6()
+
+        def source(k):
+            ts(T.elu[:, 32 * k:32 * k + 32], T.el[:], 4.0, float(k), A.mult, A.add, ["el"], ["elu%d" % k])
+
+        for i in range(nv):
+            m = v0 + i
+            ts(T.junkb[:, 384 * i + 16 * m:384 * i + 384], T.kc[:, 16 * m:384], T.jj[:, m:m + 1], 0.5, A.is_gt, A.subtract, ["kc", "jj"], ["j2%d" % i])
+        for i in range(nv):
+            m, e = v0 + i, 384 * i + 384
+            scan(T.junkc[:, 192 * i + 8 * m:192 * i + 192], T.junkb[:, e - 384 + 16 * m:e - 192 + 8 * m], T.junkb[:, e - 192 + 8 * m:e],
+                 -8.0 * m, A.add, A.add, ["j2%d" % i], ["j3%d" % i])
+        quant(T.tq[:], T.ts[:], T.tt[:], ["tt"], ["tq"])
+        layer((0, 1, 2, 3), T.tq[:], T.ts[:], ["tq"])
+        for q in ("SV" if nv > na else "VS"):
+            if q == "S":
+                ts(T.posu[:, a0:a0 + na], T.pa[:, 0:na], -0.5, 320.0 + 8 * a0, A.mult, A.add, ["pa%d" % i for i in range(na)], ["posu_b"])
+            else:
+                ts(T.posu[:, v0:v0 + nv], T.junkc[:, 191:192 * nv:192], -1.0, 320.0, A.mult, A.add, ["j3%d" % i for i in range(nv)], ["posu_a"])
         for b in range(4):
             act(X[:, yo + b:yo + 512:4], T["pb%d" % b][:, 0:128], AF.Copy, [], [xk + "y%d" % b, "pb%d" % b], scale=0.03125)
         tt(T.we[:], T.wf[:], T.jj[:], A.add, ["wf", "jj"], ["we"])
+        tt(T.lab[:], T.lac[:], T.wf[:], A.max, ["lac", "wf"], ["lab"])
         ts(T.pg[:, 0:ns], T.o[:].indirect(T.posu[:, 0:np_]), W, 512.0, A.subtract, A.min, ["posu_a", "posu_b", "o", "o_hi", "w"], ["pg"])
         tt(T.el[:], T.we[:], T.wb[:], A.max, ["we", "wb"], ["el"])
-        scan(T.ssc[:, 0:ns], T.pg[:, 0:ns], T.cq[:, 0:ns], -B4, A.max, A.add, ["pg", "cq"], ["ssc"])
-        ts(T.elu[:, 0:32], T.el[:], 4.0, 0.0, A.mult, A.add, ["el"], ["elu0"])
-        ts(T.slu[:, 0:ns // 4], T.ssc[:, 3:ns:4], 4.0, TB4, A.mult, A.add, ["ssc", "col2"], ["slu"])
-        dbk = ["db%d" % b for b in range(4)] + ["dz%d" % t]
-        dwin = X[:, do:do + 2064]
-        src = xkeys + dbk + [xk + "y%d" % b for b in range(4)]
-        xkeys = ["x%d_%d" % (t + 1, k) for k in range(4)]
-
-        def merge(k):
-            move(MERGE[k], XN[:, k:2048:4], X[:].indirect(T.elu[:, 32 * k:32 * k + 32]), src + ["elu%d" % k], [xkeys[k]])
-
-        cut = ns // 8 if SPLIT else ns // 4
-        if SPLIT:
-            act(T.st[:, 2 * ns:4 * ns], dwin.indirect(T.slu[:, cut:ns // 4]), AF.Copy, dbk + ["slu"], ["st1"])
-        merge(0)
-        ts(T.elu[:, 32:64], T.el[:], 4.0, 1.0, A.mult, A.add, ["el"], ["elu1"])
-        cp(T.st[:, 0:16 * cut], dwin.indirect(T.slu[:, 0:cut]), dbk + ["slu"], ["st0"])
-        ts(T.elu[:, 64:96], T.el[:], 4.0, 2.0, A.mult, A.add, ["el"], ["elu2"])
-        sq, ss = T.sq[:, 128 * t:128 * t + 128], T.ss[:, 128 * t:128 * t + 128]
-        quant(sq, ss, T.st[:], ["st0", "st_hi"] + (["st1"] if SPLIT else []), ["sq%d" % t])
-        send(lq[:, la:la + ns].bitcast(dt.uint8), T.sq[:, 128 * t:128 * t + ns].bitcast(dt.uint8), "aq%d" % t, ["sq%d" % t])
-        send(ls[:, la:la + ns], T.ss[:, 128 * t:128 * t + ns], "aq%d" % t, ["sq%d" % t])
-        arrival("aq%d" % t, 2, ["lq%d" % t])
-        if t == 0:
-            iota(T.tab[:, 3072:4096], [[1, 1024]], 512 * (LAB + 6), ["tab1"])
-        ts(T.elu[:, 96:128], T.el[:], 4.0, 3.0, A.mult, A.add, ["el"], ["elu3"])
-        ts(MN, cnt, lcnt, None, A.min, None, ["cnt%d" % t, "lcnt%d" % t], ["mn"])
-        tt(T.lab[:], T.lac[:], T.wf[:], A.max, ["lac", "wf"], ["lab"])
-        scan(T.hsc[:, 0:ns], T.pg[:, 0:ns], T.ch[:, 0:ns], -B4, A.max, A.add, ["pg", "ch"], ["hsc"])
-        ts(T.ha[:, 0:np_], T.kk[:, 0:np_], MN, -4096.0, A.is_lt, A.mult, ["kk", "mn"], ["ha"])
         if t < R - 1:
             tt(T.lj[:], T.lab[:], T.js[:], A.add, ["lab", "js"], ["lj"])
         else:
             ts(T.olu[:], T.lab[:], -8.0 * LAB, 0.125, A.add, A.mult, ["lab"], ["olu"])
-        for k in range(1, 4):
-            merge(k)
-        tt(T.hb[:, 0:np_], T.ha[:, 0:np_], T.dump[:, 0:np_], A.add, ["ha", "dump"], ["hb"])
+        scan(T.ssc[:, 0:ns], T.pg[:, 0:ns], T.cq[:, 0:ns], -B4, A.max, A.add, ["pg", "cq"], ["ssc"])
+        source(0)
+        source(1)
+        ts(T.slu[:, 0:ns // 4], T.ssc[:, 3:ns:4], 4.0, TB4, A.mult, A.add, ["ssc", "col2"], ["slu"])
+        src = xkeys + dbk + [xk + "y%d" % b for b in range(4)]
+        xkeys = []
+
+        def merge(q, k, lo, hi):
+            xkeys.append("x%d_%d_%d" % (t + 1, k, lo))
+            move(q, XN[:, 64 * lo + k:64 * hi:4], X[:, 0:do + 2048].indirect(T.elu[:, 32 * k + lo:32 * k + hi]), src + ["elu%d" % k], xkeys[-1:])
+
+        dwin, dk = X[:, do:do + 2064], dbk + ["dz%d" % t, "slu"]
+        act(T.st[:, 2 * ns:4 * ns], dwin.indirect(T.slu[:, ns // 8:ns // 4]), AF.Copy, dk, ["st1"])
+        source(2)
+        source(3)
+        cp(T.st[:, 0:2 * ns], dwin.indirect(T.slu[:, 0:ns // 8]), dk, ["st0"])
         if t < R - 1:
             ts(T.vlu[:], T.lj[:], 64.0, None, A.mult, None, ["lj"], ["vlu"])
-        tt(T.hc[:, 0:np_], T.hb[:, 0:np_], T.hsc[:, 15:ns:16], A.max, ["hb", "hsc"], ["hc"])
+        s0 = 128 * t
+        quant(T.sq[:, s0:s0 + 128], T.ss[:, s0:s0 + 128], T.st[:], ["st0", "st1", "st_hi"], ["sq%d" % t])
+        send(T.lq[:, la:la + ns].bitcast(dt.uint8), T.sq[:, s0:s0 + ns].bitcast(dt.uint8), "aq%d" % t, ["sq%d" % t])
+        send(T.ls[:, la:la + ns], T.ss[:, s0:s0 + ns], "aq%d" % t, ["sq%d" % t])
+        arrival("aq%d" % t, 2, ["lq%d" % t])
+        if t == 0:
+            iota(T.tab[:, 2048:3072], [[1, 1024]], 512 * (LAB + 4), ["tab1"])
+        merge("S", 0, 0, 32)
+        merge("S", 1, 0, 32)
+        ts(MN, cnt, lcnt, 0.5, A.min, A.mult, ["cnt%d" % t, "lcnt%d" % t], ["mn"])
+        merge("V", 2, 0, 16)
+        ts(T.ha[:, 0:ns // 4], T.kk[:, 0:ns // 4], MN, -4096.0, A.is_lt, A.mult, ["kk", "mn"], ["ha"])
+        merge("V", 2, 16, 32)
+        tt(T.hb[:, 0:ns // 4], T.ha[:, 0:ns // 4], T.dump[:, 0:ns // 4], A.add, ["ha", "dump"], ["hb"])
+        merge("V", 3, 0, 16)
+        tt(T.hc[:, 0:ns // 4], T.hb[:, 0:ns // 4], T.ssc[:, 3:ns:4], A.max, ["hb", "ssc"], ["hc"])
+        merge("V", 3, 16, 32)
+        ts(T.hlu[:, 0:ns // 4], T.hc[:, 0:ns // 4], 4.0, TB4, A.mult, A.add, ["hc", "col2"], ["hlu"])
+        layer((4, 5, 6, 7), T.lq[:, la:la + 128], T.ls[:, la:la + 128], ["lq%d" % t, "lz", "lz1"])
         for b in range(4):
-            ts(T.hlu[:, np_ * b:np_ * (b + 1)], T.hc[:, 0:np_], 4.0, 4 * B4 + b, A.mult, A.add, ["hc"], ["hlu%d" % b])
-        layer((4, 5, 6, 7), lq[:, la:la + 128], ls[:, la:la + 128], ["lq%d" % t, "lz"])
-        for b in range(4):
-            h = T.hs[:, ns * b:ns * (b + 1)]
+            h = T.hs[:, b:4 * ns:4]
             if b == 2:
                 act(h, T["pb%d" % (4 + b)][:, 0:ns], AF.Copy, [], ["h%d" % b, "pb%d" % (4 + b)], scale=0.03125)
             else:
                 ts(h, T["pb%d" % (4 + b)][:, 0:ns], 0.03125, None, A.mult, None, [], ["h%d" % b, "pb%d" % (4 + b)])
-        cp(XN[:, 0:2432].indirect(T.hlu[:, 0:4 * np_]), T.hs[:, 0:4 * ns], [c + str(b) for c in ("hlu", "h") for b in range(4)], xkeys)
+        cp(XN[:, 0:2432].indirect(T.hlu[:, 0:4 * np_]), T.hs[:, 0:4 * ns], ["hlu"] + ["h%d" % b for b in range(4)], xkeys)
         if t == 0:
             constants_5()
         if t < R - 1:
-            act(T.vsrc[:], T.tab[:, 0:3072 + 1024 * t].indirect(T.vlu[:]), AF.Copy, ["tab0", "vlu"] + ["tab1"] * t, ["vs0", "vs1"])
+            act(T.vsrc[:], T.tab[:, 0:3072 + 1024 * t].indirect(T.vlu[:]), AF.Copy, ["tab0", "tab1", "vlu"] + ["tab2"] * t, ["vs0", "vs1"])
             act(K2, RW, AF.Abs, ["col2", "w"], ["k2"], scale=-1.0, bias=W)
             act(K3, cnt, ID, ["ea", "cnt%d" % t, "c5%d" % t], ["k3"], scale=T.ea[:, 5 + 2 * t:6 + 2 * t], bias=cg[:, 4 + t:5 + t])
             act(K4, K2, AF.Relu, ["k2"], ["k4"], scale=-BIG, bias=BIG)
@@ -505,18 +563,19 @@ def rank_program(g, core, T, topo):
             act(T.obs[:], T.qq[:].indirect(T.olu[:]), AF.Copy, ["qq", "olu"], ["obs"])
             dma("Y", T.ob[:], T.obs[0:128:16, :], ["obs"], ["out6"])
 
-    for k in range(2):
-        lo = 256 * k
-        quant(T.xq[:, lo:lo + 256], T.xsc[:, lo:lo + 256], T.x3[:, 4 * lo:4 * lo + 1024], xkeys, ["xq%d" % k])
-        mm(k, 256, T.vq[:], T.vs[:], T.xq[:, lo:lo + 256], T.xsc[:, lo:lo + 256], ["vq", "xq%d" % k])
-    act(T.ys[:, 0:256], T.pb0[:, 0:256], AF.Copy, [], ["ys0", "pb0"])
-    dma("S", T.y[:, 0:256], T.ys[:, 0:256], ["ys0"], ["out1"])
-    cp(T.ys[:, 256:512], T.pb1[:, 0:256], [], ["ys1", "pb1"])
-    dma("Y", T.oc[:, 0:1024], T.xq[:, 0:256].bitcast(dt.uint8), ["xq0"], ["out0"])
-    dma("Y", T.oc[:, 1024:2048], T.xq[:, 256:512].bitcast(dt.uint8), ["xq1"], ["out8"])
     for k in range(4):
-        dma("Y", T.osc[4 * k:4 * k + 4, :], T.xsc[32 * k:32 * k + 4, :], ["xq0", "xq1"], ["out%d" % (2 + k)])
-    dma("S", T.y[:, 256:512], T.ys[:, 256:512], ["ys1"], ["out7"])
-    op("G", None, ["out%d" % k for k in range(9)], [], "sent", 0)
+        lo = 128 * k
+        quant(T.xq[:, lo:lo + 128], T.xsc[:, lo:lo + 128], T.x3[:, 4 * lo:4 * lo + 512], xkeys, ["yq%d" % k] + (xqk if k == 0 else []))
+        mm(k, 128, T.vq[:], T.vs[:], T.xq[:, lo:lo + 128], T.xsc[:, lo:lo + 128], ["vq", "yq%d" % k])
+    for k in range(4):
+        move("SSVV"[k], T.ys[:, 128 * k:128 * k + 128], T["pb%d" % k][:, 0:128], [], ["ys%d" % k, "pb%d" % k])
+    for k in range(2):
+        dma("Y", T.oc[:, 1024 * k:1024 * k + 1024], T.xq[:, 256 * k:256 * k + 256].bitcast(dt.uint8), ["yq%d" % (2 * k), "yq%d" % (2 * k + 1)],
+            ["out%d" % k])
+    for k in range(4):
+        dma("Y", T.osc[4 * k:4 * k + 4, :], T.xsc[32 * k:32 * k + 4, :], ["yq%d" % i for i in range(4)], ["out%d" % (2 + k)])
+    for k in range(4):
+        dma("SSSY"[k], T.y[:, 128 * k:128 * k + 128], T.ys[:, 128 * k:128 * k + 128], ["ys%d" % k], ["out%d" % (7 + k)])
+    op("G", None, ["out%d" % k for k in range(11)], [], "sent", 0)
     emit(g, T, ops)
     g.wait_ge(T.sem.sent, 3 * R * out_n)

from concourse.mybir import dt, AluOpType, AxisListType, ActivationFunctionType

A = AluOpType
AF = ActivationFunctionType
R = 3
NPASS = (6, 5, 4)
APASS = (2, 2, 2)
M0 = 22
PIECES = ((256, 384), (384, 512), (0, 256))
LAG = 2
TAIL = "q4 q5 p1 q6 o1 c0 q7 s47 p0 s78 o0 s04"
TW = (512, 448, 384, 384, 256, 192, 128, 128)
TBASE = [sum(TW[:i]) for i in range(8)]
CW = sum(TW)
BIG = 1024.0
HOLD, BP = 2048.0, 624.0
B4 = 131072.0
LAB = 138
F32, BF, I32, U16, X4, U8 = "float32", "bfloat16", "int32", "uint16", "float8_e4m3fn_x4", "uint8"
COLS = (([[0, 2], [1, 16]], 0),
        ([[0, 2], [-1, 16]], int(15 - HOLD - BP)),
        ([[0, 2], [1, 4], [0, 4]], 1),
        ([[0, 8], [1, 4]], 0),
        ([[1, 2], [0, 16]], 0),
        ([[0, 2], [-1024, 16]], 1 - 1024 * LAB),
        ([[0, 2], [-1024, 16]], 1 - 1024 * (LAB + 1)),
        ([[0, 2], [512, 16]], 512 * LAB),
        ([[0, 8], [1, 4]], int(4 * B4)),
        ([[0, 2], [int(BIG) - 256, 4], [0, 4]], 512))


def yoff(t):
    return 8 * (LAB + 4 + 2 * t) - int(BP)


def doff(t):
    return 8 * (LAB + 5 + 2 * t)


SCRATCH = {}
for _d, _names in (
        (BF, "ut512 vt512 kt512 gq512 qs512 one528 et528 sg2304 sb8192 ds512 mk512 rst512 junka1536 junkb1536 junkc768 junkd256 "
             "lb384 fl384 kc384 tt512 st512 hs384"),
        (X4, "uq128 vq128 upq128 wq512 xq512 kq128 eq512 tq128 sq384 lq272"),
        (U8, "us128 vs128 ups128 wsc512 xsc512 ks128 es512 ts128 ss384 ls272"),
        (F32, "pm512 sc512 cx512 rk512 rs32 rna32 vsrc512 o528 cq128 tsc128 ssc96 pg96 km64 kmt64 mkb64 mkc64 sm16 pa8 tab4096 cn320 cf320 cg16 "
              "qq32 ea32 eb8 ca16 cb8 cr32 jj32 js32 kk24 dump24 kcol16 wa32 wb32 wf32 we32 el32 lab32 lac32 lj32 ha24 hb24 hc24 obs512 ys512"),
        (U16, "rku32 posu8 tlu32 slu24 hlu24 elu128 vlu32 olu32 upu8 rfu32 tfu8"),
        (I32, "ti32 tj32")):
    for _s in _names.split():
        _n = _s.rstrip("0123456789")
        SCRATCH[_n] = ("sbuf", [128, int(_s[len(_n):])], _d)
SCRATCH["ct"] = ("sbuf", [128, 4 * CW], BF)
SCRATCH["cc"] = ("sbuf", [128, CW], X4)
SCRATCH["cs"] = ("sbuf", [128, CW], U8)
SCRATCH["x3"] = ("sbuf", [128, 2432], BF)
for _t in range(R):
    for _n, _w, _d in (("x", 4 * (doff(_t) + 516), BF), ("cnt", 8, F32), ("lcnt", 8, F32)):
        SCRATCH["%s%d" % (_n, _t)] = ("sbuf", [128, _w], _d)
for _b in range(8):
    SCRATCH["pb%d" % _b] = ("psum", [128, 512], F32)

SEMAPHORES = (["pe", "dve", "act", "pool", "sent"] + ["d%d" % i for i in range(24)]
              + ["ac%d" % t for t in range(R)] + ["aq%d" % t for t in range(R)])
QUEUE_SEM = {"T": "pe", "V": "dve", "S": "act", "G": "pool"}


def emit(g, T, ops):
    queue = {"T": g.tensor, "V": g.vector, "S": g.scalar, "G": g, "Y": g.sync}
    seen = {q: {} for q in queue}
    writer, readers, seq, marked, done = {}, {}, {}, {}, {}
    for o in ops:
        q = o["q"]
        need = []
        for k in o["r"]:
            need.append(writer[k])
            if k[:2] == "pb":
                need.extend(n for n in readers[k] if n[0] != QUEUE_SEM[q])
        for k in o["w"]:
            if k in writer:
                need.append(writer[k])
            need.extend(readers.get(k, []))
        if o["chain"]:
            need = [n for n in need if n[0] != QUEUE_SEM[q]]
        best = {}
        for s, n in need:
            best[s] = max(best.get(s, 0), n)
        waits = []
        for s, n in sorted(best.items(), key=lambda e: -done[e][1]):
            if seen[q].get(s, 0) < n:
                waits.append((s, n))
                marked.setdefault(s, set()).add(n)
                for s2, n2 in done[(s, n)][0].items():
                    seen[q][s2] = max(seen[q].get(s2, 0), n2)
        o["waits"] = waits
        s = o["sem"] if o["sem"] else QUEUE_SEM[q]
        seq[s] = seq.get(s, 0) + 1
        o["id"] = (s, seq[s])
        clock = dict(seen[q]) if o["fn"] else {}
        clock[s] = seq[s]
        done[o["id"]] = (clock, len(done))
        for k in o["w"]:
            writer[k] = o["id"]
            readers[k] = []
        for k in o["r"]:
            readers.setdefault(k, []).append(o["id"])
    count = {}
    for o in ops:
        if o["sem"]:
            count[o["id"]] = o["inc"]
    for s in QUEUE_SEM.values():
        for i, n in enumerate(sorted(marked.get(s, ()))):
            count[(s, n)] = i + 1
    for o in ops:
        for w in o["waits"]:
            queue[o["q"]].wait_ge(T.sem[w[0]], count[w])
        if o["fn"]:
            ins = o["fn"]()
            if o["sem"] and o["inc"]:
                ins.then_inc(T.sem[o["sem"]], o["inc"])
            elif not o["sem"] and o["id"] in count:
                ins.then_inc(T.sem[o["id"][0]], 1)


def rank_program(g, core, T, topo):
    rank = T.rank_of(core)
    if rank is None:
        return
    n = len(T.cores)
    nxt, prv = T.cores[(rank + 1) % n], T.cores[(rank - 1) % n]
    rid, pid = topo.addr(nxt)[0], topo.addr(nxt)[1]
    out_mask, out_n, in_n = topo.mask(core, nxt), len(topo.engines(core, nxt)), len(topo.engines(prv, core))
    V, S, PE = g.vector, g.scalar, g.tensor
    ops = []
    ndma = [0]

    def op(q, fn, r, w, sem=None, inc=0, chain=False):
        banks = [k for k in w if k[:2] == "pb" and q != "T"]
        ops.append({"q": q, "fn": fn, "r": list(r) + banks, "w": [k for k in w if k not in banks], "sem": sem, "inc": inc, "chain": chain})

    def dma(q, out, in_, r, w):
        e = g.sync if q == "Y" else g.scalar
        op(q, lambda: e.dma_start(out, in_), r, w, "d%d" % ndma[0], 16)
        ndma[0] += 1

    def ts(out, in0, s1, s2, o0, o1, r, w):
        if o1 is None:
            op("V", lambda: V.tensor_scalar(out, in0, s1, None, o0), r, w)
        else:
            op("V", lambda: V.tensor_scalar(out, in0, s1, s2, o0, o1), r, w)

    def tt(out, a, b, o, r, w):
        op("V", lambda: V.tensor_tensor(out, a, b, o), r, w)

    def cp(out, a, r, w):
        op("V", lambda: V.tensor_copy(out, a), r, w)

    def ms(ap, c, w, r=()):
        op("V", lambda: V.memset(ap, c), r, w)

    def tp(out, a, r, w):
        op("V", lambda: V.transpose(out, a), r, w)

    def scan(out, a, b, init, o0, o1, r, w):
        op("V", lambda: V.tensor_tensor_scan(out, a, b, init, o0, o1), r, w)

    def quant(q, s, a, r, w):
        op("V", lambda: V.quantize_mx(q, s, a), r, w)

    def act(out, a, f, r, w, **kw):
        op("S", lambda: S.activation(out, a, f, **kw), r, w)

    def move(q, out, a, r, w):
        if q == "V":
            cp(out, a, r, w)
        else:
            act(out, a, AF.Copy, r, w)

    def mm(bank, width, lq, lsc, rq, rsc, r, start=True, stop=True):
        op("T", lambda: PE.matmul_mx(T["pb%d" % bank][:, 0:width], lq, lsc, rq, rsc, start, stop), r, ["pb%d" % bank], chain=not start)

    def iota(out, pat, base, w):
        op("G", lambda: g.iota(out, pat, base, 0, allow_small_or_imprecise_dtypes=True), [], w)

    def select(out, in_, pat, cmp, base, cm, r, w):
        op("G", lambda: g.affine_select(out, in_, pat, cmp, 0.0, base, cm), r, w)

    def send(out, in_, sem, r):
        op("G", lambda: g.remote_dma(out, in_, T.sem[sem], T.sem.sent, pid, rid, out_mask), r, [], "sent", 0)

    def arrival(sem, k, w):
        op("G", None, [], w, sem, k * in_n)

    def layer(banks, q, s, r):
        for b, bank in enumerate(banks):
            mm(bank, 128, T.wq[:, 128 * b:128 * b + 128], T.wsc[:, 128 * b:128 * b + 128], q, s, ["wq", "wsc"] + r)

    def unpack(banks, q, s, r, which=range(4)):
        for b in which:
            mm(banks[b], 512, T.eq[:, 128 * b:128 * b + 128], T.es[:, 128 * b:128 * b + 128], q, s, ["eq%d" % b] + r)

    cf, cg, sm = T.cf, T.cg, T.sm
    ID = AF.Identity
    dma("Y", T.ut[:], T.u[:], [], ["ut"])
    for i, (lo, hi) in enumerate(PIECES):
        dma("SSY"[i], T.x0[:, 4 * lo:4 * hi], T.x[:, 4 * lo:4 * hi], [], ["x0%d" % i])
    dma("Y", T.wq[:].bitcast(dt.uint8), T.wc[:], ["x02"], ["wq"])
    dma("Y", T.wsc[:], T.ws[:], [], ["wsc"])
    dma("Y", T.vt[:], T.v[:], [], ["vt"])

    RF, CC0, R4, T4, HF, NA, NB, RW, TB4, KB0 = (cf[:, 32 * i:32 * i + 1] for i in range(10))
    CC1, KB1 = cg[:, 0:1], cg[:, 1:2]
    KEY, W, WL, MN, CA, CB, K2, K3, K4, K5 = (sm[:, i:i + 1] for i in range(10))
    for i in range(2):
        iota(T.cn[:, 32 * i:32 * i + 32], COLS[i][0], COLS[i][1], ["cn%d" % i])
    iota(T.qq[:], [[1, 32]], 0, ["qq"])
    ms(T.one[:], 1.0, ["one"])
    select(T.et[:], T.one[:], [[-1, 528]], A.is_equal, 3, 4, ["one"], ["et"])
    iota(T.cr[:, 0:M0], [[16, M0]], 8 * (32 - M0), ["cr_a"])
    iota(T.cr[:, M0:32], [[0, 32 - M0]], 248, ["cr_b"])
    select(T.gq[:], T.one[:, 0:512], [[-16, 8], [0, 64]], A.is_ge, 0, 1, ["one"], ["gq"])
    iota(T.qs[:], [[0, 32], [1, 16]], 0, ["qs"])
    select(T.kt[:], T.gq[:], [[16, 8], [0, 64]], A.is_ge, 15, -1, ["gq"], ["kt"])

    def constants_1():
        for i in (1, 4, 5, 6, 7):
            pad(i)
        for i in range(2, len(COLS)):
            iota(T.cn[:, 32 * i:32 * i + 32], COLS[i][0], COLS[i][1], ["cn%d" % i])
        iota(T.mkc[:], [[0, 2], [1, 2], [0, 16]], 0, ["mk0"])
        iota(T.jj[:], [[16, 32]], 0, ["jj0"])
        iota(T.rs[:, 0:1], [[0, 1]], 0, ["rs0"])
        iota(T.vsrc[:], [[640, 4], [1, 128]], 512 * LAB, ["vs0", "vs1"])
        iota(T.kk[:], [[4, 24]], 127, ["kk0"])
        iota(T.lab[:], [[8, 4], [0, 8]], 8 * LAB, ["lab"])
        iota(T.o[:, 512:528], [[0, 16]], 1000000, ["o_hi"])
        for t in range(R):
            iota(T["x%d" % t][:, 4 * doff(t) + 2048:4 * doff(t) + 2064], [[0, 16]], 0, ["dz%d" % t])
        iota(T.st[:, 384:512], [[0, 128]], 0, ["st_hi"])
        iota(T.tab[:, 0:2048], [[1, 2048]], 512 * LAB, ["tab0"])

    def rows(i):
        return ["c%d" % m for m in range(29 - 4 * i, 33 - 4 * i)]

    def pad(i):
        lo = 16 * (29 - 4 * i)
        ap, keys = T.ct[:, 4 * (TBASE[i] + lo):4 * (TBASE[i] + TW[i])], rows(i)
        if i in (0, 2, 3):
            act(ap, T.one[:, 0:4 * (TW[i] - lo)], AF.Copy, ["one"], keys, scale=0.0)
        else:
            iota(ap, [[0, 4 * (TW[i] - lo)]], 0, keys)

    for i in (3, 2):
        pad(i)
    ms(T.rst[:], 1e29, ["rst0"])
    tp(cf[:, 0:64], T.cn[:, 0:64], ["cn0", "cn1"], ["cols"])
    ts(T.upu[:], T.qq[:, 0:8], 16.0, None, A.mult, None, ["qq"], ["upu"])
    ts(T.ea[:], T.qq[:], RF, None, A.is_equal, None, ["qq", "cols"], ["ea"])
    cp(T.rfu[:], cf[:, 0:32], ["cols"], ["rfu"])
    ts(T.ca[:], T.ea[:, 1:17], -2.0, None, A.mult, None, ["ea"], ["ca0"])
    ms(T.rst[:, 0:512:16], -1e29, ["rst"], ["rst0"])
    tt(T.ca[:], T.ca[:], T.ea[:, 0:16], A.add, ["ea", "ca0"], ["ca"])
    act(T.mk[:], T.ea[:].indirect(T.rfu[:]), AF.Copy, ["ea", "rfu"], ["mk"], scale=2e29, bias=-1e29)

    def unit(b):
        quant(T.eq[:, 128 * b:128 * b + 128], T.es[:, 128 * b:128 * b + 128], T.et[:, 3 - b:515 - b], ["et"], ["eq%d" % b])

    quant(T.uq[:], T.us[:], T.ut[:], ["ut"], ["uq"])
    act(T.ups[:], T.us[:].indirect(T.upu[:]), AF.Copy, ["uq", "upu"], ["ups"])
    pad(0)
    cp(T.upq[:].bitcast(dt.uint32), T.uq[:].bitcast(dt.uint32).indirect(T.upu[:]), ["uq", "upu"], ["upq"])
    act(CC1, T.ea[:, 15:16], ID, ["ea", "cols"], ["cc1"], scale=HOLD, bias=CC0)
    act(T.cx[:], T.ca[:].indirect(T.rfu[:]), AF.Copy, ["ca", "rfu"], ["cxu", "cxm", "cxl"], scale=HOLD)
    act(T.cr[:], T.cr[:], ID, ["cr_a", "cr_b", "cc1"], ["cr"], bias=CC1)

    between = [
        lambda: None,
        lambda: None,
        lambda: None,
        lambda: None,
        lambda: tp(cf[:, 64:320], T.cn[:, 64:320], ["cn%d" % i for i in range(2, len(COLS))], ["col2"]),
        lambda: cp(T.tfu[:], cf[:, 96:104], ["col2"], ["tfu"])]

    def constants_4():
        ts(T.mkc[:], T.mkc[:], HF, 4 * BIG, A.not_equal, A.mult, ["mk0", "col2"], ["mk1"])
        act(T.mkb[:, 0:32], T.mkc[:, 0:32], ID, ["mk1", "kb1"], ["mkb"], bias=KB1)
        act(T.mkb[:, 32:64], T.mkc[:, 32:64], ID, ["mk1", "col2"], ["mkc"], bias=KB0)

    def constants_3():
        act(T.eb[:], T.qq[:, 0:8], AF.Relu, ["qq", "col2"], ["eb"], scale=-1.0, bias=R4)
        act(KB1, RW, ID, ["col2"], ["kb1"], scale=1.0 / 131072, bias=KB0)
        act(T.jj[:], T.jj[:], ID, ["jj0", "cols"], ["jj"], bias=RF)
        act(T.cb[:], T.eb[:], AF.Abs, ["eb"], ["cb1"], bias=-0.625)
        unpacked(0)
        act(T.cb[:, 3:4], T.cb[:, 3:4], AF.Copy, ["cb1"], ["cb"], bias=0.5)
        act(T.kcol[:, 8:14], T.jj[:, 0:6], AF.Copy, ["jj"], ["nk"], scale=-1.0, bias=-0.5)
        unpacked(1)
        act(T.cq[:], T.cb[:].indirect(T.tfu[:]), AF.Copy, ["cb", "tfu"], ["cq"], scale=-4 * B4, bias=2.5 * B4)
        unpacked(2)

    def constants_6():
        act(T.kk[:], T.kk[:], ID, ["kk0", "col2"], ["kk"], bias=R4)
        act(T.js[:], T.jj[:], AF.Copy, ["jj"], ["js"], scale=1.0 / 64, bias=-8.0 * LAB)
        act(T.dump[:], T.kk[:], AF.Copy, ["kk"], ["dump"], bias=384.0 - B4)

    def constants_5():
        for t in range(R - 1):
            act(cg[:, 2 + t:3 + t], T.ea[:, 4 + 2 * t:5 + 2 * t], AF.Copy, ["ea"], ["c4%d" % t], scale=256.0 - BIG)
        for t in range(R - 1):
            act(cg[:, 4 + t:5 + t], T.ea[:, 5 + 2 * t:6 + 2 * t], ID, ["ea", "c4%d" % t], ["c5%d" % t], scale=-256.0 - BIG,
                bias=cg[:, 2 + t:3 + t])

    def lane(m, lo, hi):
        i, k = (32 - m) // 4, (32 - m) % 4
        return T.ct[:, 4 * (TBASE[i] + lo) + k:4 * (TBASE[i] + hi):4]

    def pivot(m):
        return T.sc[:, 16 * m + 15:16 * m + 16]

    def tile(i):
        lo, w = TBASE[i], TW[i]
        wq = max(512 - 64 * i, 128) if t else w
        quant(T.cc[:, lo:lo + wq], T.cs[:, lo:lo + wq], T.ct[:, 4 * lo:4 * (lo + wq)], rows(i), ["cc%d" % i])
        if w > 256:
            mm(2, w - 256, T.kq[:], T.ks[:], T.cc[:, lo + 256:lo + w], T.cs[:, lo + 256:lo + w], ["kq", "cc%d" % i], i == 0, i == 3)
        w = min(w, 256)
        mm(3, w, T.kq[:], T.ks[:], T.cc[:, lo:lo + w], T.cs[:, lo:lo + w], ["kq", "cc%d" % i], i == 0, i == 7)

    def places(h):
        lo = 256 * h
        bank = "pb%d" % (3 - h)
        scan(T.rk[:, lo:lo + 256], T[bank][:, 0:256], T.cx[:, lo:lo + 256], -2 * HOLD, A.max, A.add,
             ["cxu", "cxm"] if h else ["cxl"], ["rk%d" % h, bank])

    def offsets(h):
        ts(T.rku[:, 16 * h:16 * h + 16], T.rk[:, 256 * h + 15:256 * h + 256:16], BP, None, A.add, None, ["rk%d" % h], ["rku%d" % h])

    def sort(a, b):
        cp(T.o[:, 0:512].indirect(T.rku[:, 4 * a:4 * b]), T.vsrc[:, 64 * a:64 * b], ["rku%d" % (a // 4), "vs%d" % (a // 4)], ["o"])

    xkeys = ["x00", "x01", "x02"]
    for t in range(R):
        X, XN = T["x%d" % t], T["x%d" % (t + 1)]
        xk = "x%d" % t
        yo, do = 4 * yoff(t), 4 * doff(t)
        np_, na = NPASS[t], APASS[t]
        nv, ns = np_ - na, 16 * np_
        cnt, lcnt = T["cnt%d" % t][:, 0:1], T["lcnt%d" % t][:, 0:1]
        la = 16 * sum(NPASS[t + 1:])

        def qx(lo, hi):
            return T.xq[:, lo:hi], T.xsc[:, lo:hi]

        xqk = ["xq%d" % i for i in range(3)]
        for i, (lo, hi) in enumerate(PIECES):
            quant(*qx(lo, hi), X[:, 4 * lo:4 * hi], xkeys[i:i + 1] if t == 0 else xkeys, ["xq%d" % i])
            mm(2 + i, hi - lo, T.upq[:], T.ups[:], *qx(lo, hi), ["upq", "ups", "xq%d" % i])
            if t == 0 and i == 1:
                unit(0)
        ws = 16 * (M0 - 1)
        mm(1, ws, T.upq[:], T.ups[:], *qx(0, ws), ["upq", "ups"] + xqk)
        mm(0, 512, T.upq[:], T.ups[:], *qx(0, 512), ["upq", "ups"] + xqk)
        if t == 0:
            constants_1()
        if t == 1:
            iota(T.tab[:, 3072:4096], [[1, 1024]], 512 * (LAB + 6), ["tab2"])

        def own(i, step):
            (lo, hi), bank = PIECES[i], "pb%d" % (2 + i)
            if step == 0:
                tt(T.pm[:, lo:hi], T[bank][:, 0:hi - lo], T.mk[:, lo:hi], A.min, ["mk"], ["pm%d" % i, bank])
            else:
                scan(T.sc[:, lo:hi], T.rst[:, lo:hi], T.pm[:, lo:hi], 0.0, A.min, A.max, ["rst", "pm%d" % i], ["sc%d" % i])

        if t == 0:
            unit(1)
            dma("Y", T.lq[:, 240:272].bitcast(dt.uint8), T.xq[:, 256:288].bitcast(dt.uint8), ["xq0"], ["lz"])
            dma("Y", T.ls[:, 240:272], T.xsc[:, 256:288], ["xq0"], ["lz1"])
        for i, step in ((0, 0), (1, 0), (0, 1), (2, 0), (1, 1)):
            own(i, step)
        if t == 0:
            unit(2)
            unit(3)
        if t == 2:
            quant(T.vq[:], T.vs[:], T.vt[:], ["vt"], ["vq"])
        own(2, 1)
        unpack((4, 5, 6, 7), *qx(0, 512), xqk)
        ts(lane(31, 0, 496), T.pb0[:, 0:496], pivot(31), 0.5, A.is_lt, A.subtract, ["sc1"], ["c31", "pb0"])

        arows = list(range(M0 - 1, 0, -1))
        for k in range(len(arows) + LAG):
            if k < len(arows):
                m = arows[k]
                act(T.sg[:, 384 * (k % 6):384 * (k % 6) + 16 * m], T.pb1[:, 0:16 * m], AF.Sign, ["sc0" if m >= 16 else "sc2"],
                    ["sg%d" % (k % 6), "pb1"], bias=pivot(m), scale=-1.0)
            j = k - LAG
            if j >= 0:
                m = arows[j]
                act(lane(m, 0, 16 * m), T.sg[:, 384 * (j % 6):384 * (j % 6) + 16 * m], AF.Relu, ["sg%d" % (j % 6)],
                    ["c%d" % m, "rs%d" % m], accum_out=T.rs[:, m:m + 1])
        ts(lane(30, 0, 480), T.pb0[:, 0:480], pivot(30), 0.5, A.is_lt, A.subtract, ["sc1"], ["c30", "pb0"])
        tt(lane(32, 0, 512), T.pb0[:], T.sc[:], A.is_le, ["sc0", "sc1", "sc2"], ["c32", "pb0"])
        for m in range(31, M0 - 1, -1):
            if m - 2 >= M0:
                ts(lane(m - 2, 0, 16 * m - 32), T.pb0[:, 0:16 * m - 32], pivot(m - 2), 0.5, A.is_lt, A.subtract, ["sc0", "sc1"], ["c%d" % (m - 2), "pb0"])
            if m == 31:
                scan(T.ds[:], T.qs[:], lane(32, 0, 512), 0.0, A.min, A.add, ["qs", "c32"], ["ds"])
            e = 256 * (m + 1)
            scan(T.sb[:, e - 8 * m:e], lane(m, 0, 8 * m), lane(m, 8 * m, 16 * m), 0.0, A.add, A.add, ["c%d" % m], ["sb%d" % m])
            if m == 30:
                tt(T.rna[:], T.cr[:], T.ds[:, 15:512:16], A.subtract, ["cr", "ds"], ["rna"])
            if m == 31 and t == 0:
                quant(T.kq[:], T.ks[:], T.kt[:], ["kt"], ["kq"])
            if m % 4 == 2 and m - 1 >= M0:
                tile((30 - m) // 4)
            if m < 30 and between:
                between.pop(0)()
        for i in range((33 - M0) // 4, 4):
            tile(i)
        tt(T.cx[:, 16 * M0 + 15:512:16], T.rna[:, M0:32], T.sb[:, 256 * M0 + 255:8192:256], A.subtract,
           ["rna"] + ["sb%d" % m for m in range(M0, 32)], ["cxu"])
        while between:
            between.pop(0)()
        tt(T.cx[:, 271:16 * M0:16], T.rna[:, 16:M0], T.rs[:, 16:M0], A.subtract, ["rna"] + ["rs%d" % m for m in range(16, M0)], ["cxm"])

        def unpacked(b):
            act(X[:, do + b:do + 2048:4], T["pb%d" % (4 + b)][:], AF.Copy, [], ["db%d" % b, "pb%d" % (4 + b)])

        if t == 0:
            constants_3()
        else:
            for b in range(4):
                unpacked(b)
        dbk = ["db%d" % b for b in range(4)]
        for step in TAIL.split():
            k = int(step[1:], 16)
            if step[0] == "q":
                tile(k)
            elif step[0] == "p":
                places(k)
            elif step[0] == "o":
                offsets(k)
                if k == 0 and t == 0:
                    constants_4()
            elif step[0] == "s":
                sort(k // 16, k % 16)
            else:
                tt(T.cx[:, 15:256:16], T.rna[:, 0:16], T.rs[:, 0:16], A.subtract, ["rna"] + ["rs%d" % m for m in range(16)], ["cxl"])
        act(T.junkd[:, 0:128], T.o[:, 0:128], AF.Sign, ["o", "col2"], ["jd0", "ca_"], scale=2.0, bias=NA, accum_out=CA)
        act(T.junkd[:, 128:256], T.o[:, 0:128], AF.Sign, ["o", "col2"], ["jd1", "cb_"], scale=2.0, bias=NB, accum_out=CB)
        act(T.lb[:], T.o[:, 128:512], AF.Copy, ["o"], ["lb"], scale=1.0 / 131072, bias=(1.0 / 1024 - 0.5) / 256)
        if t == 0:
            unpacked(3)
        ts(T.wa[:], T.rku[:], 128.0, 8.0 * (LAB + 4 + 2 * t), A.is_lt, A.mult, ["rku0", "rku1"], ["wa"])
        scan(T.tsc[:], T.o[:, 0:128], T.cq[:], -B4, A.max, A.add, ["o", "cq"], ["tsc"])
        tt(T.lac[:], T.lab[:], T.wa[:], A.max, ["lab", "wa"], ["lac"])
        ts(T.ti[:], T.tsc[:, 3:128:4], B4, None, A.add, None, ["tsc"], ["ti"])
        ts(T.km[:], T.mkb[:], CA, CB, A.subtract, A.add, ["mkb", "mkc", "ca_", "cb_"], ["km"])
        ts(T.tj[:], T.ti[:], 511, None, A.bitwise_and, None, ["ti"], ["tj"])
        tp(T.kmt[:], T.km[:], ["km"], ["kmt"])
        ts(T.tlu[:], T.tj[:], 4.0, T4, A.mult, A.add, ["tj", "col2"], ["tlu"])
        act(T.tt[:], X[:, 0:2048].indirect(T.tlu[:]), AF.Copy, xkeys + ["tlu"], ["tt"])
        op("V", lambda: V.tensor_reduce(KEY, T.kmt[:, 0:32], AxisListType.X, A.min), ["kmt"], ["key"])
        op("V", lambda cnt=cnt: V.tensor_reduce(cnt, T.kmt[:, 32:64], AxisListType.X, A.min), ["kmt"], ["cnt%d" % t])
        send(lcnt, cnt, "ac%d" % t, ["cnt%d" % t])
        arrival("ac%d" % t, 1, ["lcnt%d" % t])
        vk = ["key", "cnt%d" % t]
        tt(T.wb[:], T.wa[:], T.rk[:, 15:512:16], A.add, ["wa", "rk0", "rk1"], ["wb"])
        ts(T.fl[:], T.lb[:], cnt, KEY, A.add, A.is_equal, ["lb"] + vk, ["fl"])
        ts(WL, KEY, cnt, 2048.0, A.subtract, A.mult, vk, ["wl"])
        scan(T.kc[:], T.fl[:], T.fl[:], 0.0, A.add, A.max, ["fl"], ["kc"])
        ts(T.wf[:], T.lac[:], WL, float(doff(t)), A.is_equal, A.mult, ["lac", "wl"], ["wf"])
        ts(W, KEY, cnt, 131072.0, A.subtract, A.mult, vk, ["w"])
        a0, v0 = (0, na) if t == 0 else (nv, 0)
        for i in range(na):
            m = a0 + i
            act(T.junka[:, 384 * i + 16 * a0:384 * i + 384], T.kc[:, 16 * a0:384], AF.Sign, ["kc", "nk"], ["junk%d" % i, "pa%d" % i],
                bias=T.kcol[:, 8 + m:9 + m], accum_out=T.pa[:, i:i + 1])
        if t == 0:
            constants_6()

        def source(k):
            ts(T.elu[:, 32 * k:32 * k + 32], T.el[:], 4.0, float(k), A.mult, A.add, ["el"], ["elu%d" % k])

        for i in range(nv):
            m = v0 + i
            ts(T.junkb[:, 384 * i + 16 * m:384 * i + 384], T.kc[:, 16 * m:384], T.jj[:, m:m + 1], 0.5, A.is_gt, A.subtract, ["kc", "jj"], ["j2%d" % i])
        for i in range(nv):
            m, e = v0 + i, 384 * i + 384
            scan(T.junkc[:, 192 * i + 8 * m:192 * i + 192], T.junkb[:, e - 384 + 16 * m:e - 192 + 8 * m], T.junkb[:, e - 192 + 8 * m:e],
                 -8.0 * m, A.add, A.add, ["j2%d" % i], ["j3%d" % i])
        quant(T.tq[:], T.ts[:], T.tt[:], ["tt"], ["tq"])
        layer((0, 1, 2, 3), T.tq[:], T.ts[:], ["tq"])
        for q in ("SV" if nv > na else "VS"):
            if q == "S":
                ts(T.posu[:, a0:a0 + na], T.pa[:, 0:na], -0.5, 320.0 + 8 * a0, A.mult, A.add, ["pa%d" % i for i in range(na)], ["posu_b"])
            else:
                ts(T.posu[:, v0:v0 + nv], T.junkc[:, 191:192 * nv:192], -1.0, 320.0, A.mult, A.add, ["j3%d" % i for i in range(nv)], ["posu_a"])
        for b in range(4):
            act(X[:, yo + b:yo + 512:4], T["pb%d" % b][:, 0:128], AF.Copy, [], [xk + "y%d" % b, "pb%d" % b], scale=0.03125)
        tt(T.we[:], T.wf[:], T.jj[:], A.add, ["wf", "jj"], ["we"])
        tt(T.lab[:], T.lac[:], T.wf[:], A.max, ["lac", "wf"], ["lab"])
        ts(T.pg[:, 0:ns], T.o[:].indirect(T.posu[:, 0:np_]), W, 512.0, A.subtract, A.min, ["posu_a", "posu_b", "o", "o_hi", "w"], ["pg"])
        tt(T.el[:], T.we[:], T.wb[:], A.max, ["we", "wb"], ["el"])
        if t < R - 1:
            tt(T.lj[:], T.lab[:], T.js[:], A.add, ["lab", "js"], ["lj"])
        else:
            ts(T.olu[:], T.lab[:], -8.0 * LAB, 0.125, A.add, A.mult, ["lab"], ["olu"])
        scan(T.ssc[:, 0:ns], T.pg[:, 0:ns], T.cq[:, 0:ns], -B4, A.max, A.add, ["pg", "cq"], ["ssc"])
        source(0)
        source(1)
        ts(T.slu[:, 0:ns // 4], T.ssc[:, 3:ns:4], 4.0, TB4, A.mult, A.add, ["ssc", "col2"], ["slu"])
        src = xkeys + dbk + [xk + "y%d" % b for b in range(4)]
        xkeys = []

        def merge(q, k, lo, hi):
            xkeys.append("x%d_%d_%d" % (t + 1, k, lo))
            move(q, XN[:, 64 * lo + k:64 * hi:4], X[:, 0:do + 2048].indirect(T.elu[:, 32 * k + lo:32 * k + hi]), src + ["elu%d" % k], xkeys[-1:])

        dwin, dk = X[:, do:do + 2064], dbk + ["dz%d" % t, "slu"]
        act(T.st[:, 2 * ns:4 * ns], dwin.indirect(T.slu[:, ns // 8:ns // 4]), AF.Copy, dk, ["st1"])
        source(2)
        source(3)
        cp(T.st[:, 0:2 * ns], dwin.indirect(T.slu[:, 0:ns // 8]), dk, ["st0"])
        if t < R - 1:
            ts(T.vlu[:], T.lj[:], 64.0, None, A.mult, None, ["lj"], ["vlu"])
        s0 = 128 * t
        quant(T.sq[:, s0:s0 + 128], T.ss[:, s0:s0 + 128], T.st[:], ["st0", "st1", "st_hi"], ["sq%d" % t])
        send(T.lq[:, la:la + ns].bitcast(dt.uint8), T.sq[:, s0:s0 + ns].bitcast(dt.uint8), "aq%d" % t, ["sq%d" % t])
        send(T.ls[:, la:la + ns], T.ss[:, s0:s0 + ns], "aq%d" % t, ["sq%d" % t])
        arrival("aq%d" % t, 2, ["lq%d" % t])
        if t == 0:
            iota(T.tab[:, 2048:3072], [[1, 1024]], 512 * (LAB + 4), ["tab1"])
        merge("S", 0, 0, 32)
        merge("S", 1, 0, 32)
        ts(MN, cnt, lcnt, 0.5, A.min, A.mult, ["cnt%d" % t, "lcnt%d" % t], ["mn"])
        merge("V", 2, 0, 16)
        ts(T.ha[:, 0:ns // 4], T.kk[:, 0:ns // 4], MN, -4096.0, A.is_lt, A.mult, ["kk", "mn"], ["ha"])
        merge("V", 2, 16, 32)
        tt(T.hb[:, 0:ns // 4], T.ha[:, 0:ns // 4], T.dump[:, 0:ns // 4], A.add, ["ha", "dump"], ["hb"])
        merge("V", 3, 0, 16)
        tt(T.hc[:, 0:ns // 4], T.hb[:, 0:ns // 4], T.ssc[:, 3:ns:4], A.max, ["hb", "ssc"], ["hc"])
        merge("V", 3, 16, 32)
        ts(T.hlu[:, 0:ns // 4], T.hc[:, 0:ns // 4], 4.0, TB4, A.mult, A.add, ["hc", "col2"], ["hlu"])
        layer((4, 5, 6, 7), T.lq[:, la:la + 128], T.ls[:, la:la + 128], ["lq%d" % t, "lz", "lz1"])
        for b in range(4):
            h = T.hs[:, b:4 * ns:4]
            if b == 2:
                act(h, T["pb%d" % (4 + b)][:, 0:ns], AF.Copy, [], ["h%d" % b, "pb%d" % (4 + b)], scale=0.03125)
            else:
                ts(h, T["pb%d" % (4 + b)][:, 0:ns], 0.03125, None, A.mult, None, [], ["h%d" % b, "pb%d" % (4 + b)])
        cp(XN[:, 0:2432].indirect(T.hlu[:, 0:4 * np_]), T.hs[:, 0:4 * ns], ["hlu"] + ["h%d" % b for b in range(4)], xkeys)
        if t == 0:
            constants_5()
        if t < R - 1:
            act(T.vsrc[:], T.tab[:, 0:3072 + 1024 * t].indirect(T.vlu[:]), AF.Copy, ["tab0", "tab1", "vlu"] + ["tab2"] * t, ["vs0", "vs1"])
            act(K2, RW, AF.Abs, ["col2", "w"], ["k2"], scale=-1.0, bias=W)
            act(K3, cnt, ID, ["ea", "cnt%d" % t, "c5%d" % t], ["k3"], scale=T.ea[:, 5 + 2 * t:6 + 2 * t], bias=cg[:, 4 + t:5 + t])
            act(K4, K2, AF.Relu, ["k2"], ["k4"], scale=-BIG, bias=BIG)
            act(K5, K4, ID, ["k4", "k3"], ["k5"], bias=K3)
            act(T.mkb[:], T.km[:], ID, ["km", "k5"], ["mkb", "mkc"], bias=K5)
        else:
            act(T.obs[:], T.qq[:].indirect(T.olu[:]), AF.Copy, ["qq", "olu"], ["obs"])
            dma("Y", T.ob[:], T.obs[0:128:16, :], ["obs"], ["out6"])

    for k in range(4):
        lo = 128 * k
        quant(T.xq[:, lo:lo + 128], T.xsc[:, lo:lo + 128], T.x3[:, 4 * lo:4 * lo + 512], xkeys, ["yq%d" % k] + (xqk if k == 0 else []))
        mm(k, 128, T.vq[:], T.vs[:], T.xq[:, lo:lo + 128], T.xsc[:, lo:lo + 128], ["vq", "yq%d" % k])
    for k in range(4):
        move("SSVV"[k], T.ys[:, 128 * k:128 * k + 128], T["pb%d" % k][:, 0:128], [], ["ys%d" % k, "pb%d" % k])
    for k in range(2):
        dma("Y", T.oc[:, 1024 * k:1024 * k + 1024], T.xq[:, 256 * k:256 * k + 256].bitcast(dt.uint8), ["yq%d" % (2 * k), "yq%d" % (2 * k + 1)],
            ["out%d" % k])
    for k in range(4):
        dma("Y", T.osc[4 * k:4 * k + 4, :], T.xsc[32 * k:32 * k + 4, :], ["yq%d" % i for i in range(4)], ["out%d" % (2 + k)])
    for k in range(4):
        dma("SSSY"[k], T.y[:, 128 * k:128 * k + 128], T.ys[:, 128 * k:128 * k + 128], ["ys%d" % k], ["out%d" % (7 + k)])
    op("G", None, ["out%d" % k for k in range(11)], [], "sent", 0)
    emit(g, T, ops)
    g.wait_ge(T.sem.sent, 3 * R * out_n)
